import numpy as np, ml_dtypes
CORES = [16,18,20,22]
N = 4
BF = ml_dtypes.bfloat16
V, G, H, RO = 3584, 512, 1, 3
W = V + H * G
LIM = 2 ** 19 - 1
def pack(v, p):
    return {"x": np.ascontiguousarray(v.reshape(N, 128, V)).astype(np.int32), "pt": np.ascontiguousarray(p).astype(np.int32)}
def signs(rng, *shape):
    return rng.choice(np.array([-1, 1]), shape)
def points(rng):
    return np.ascontiguousarray(np.argsort(rng.random((N, 8, W)), axis=-1)[..., :V])
def crowd(rng, quiet):
    pool = np.broadcast_to(rng.integers(-2 ** 16, 2 ** 16 + 1, (8, 16, 24)), (N, 8, 16, 24))
    near = np.take_along_axis(pool, rng.integers(0, 24, (N, 8, 1, V)), 3) * rng.choice(np.array([-3, -2, -1, 1, 2, 3]), (N, 8, 1, V))
    noise = np.exp2(2 + 15 * rng.random((N, 8, 1, V))) * rng.standard_normal((N, 8, 16, V), dtype=np.float32)
    loud = near * (rng.random((N, 8, 1, V)) < 0.5) + noise.astype(np.int64)
    dense = rng.choice(np.array([0.15, 0.3, 1.0]), (N, 8, 1, 1))
    calm = rng.integers(-LIM, LIM + 1, (N, 8, 16, V)) * (rng.random((N, 8, 16, V)) < dense)
    v = np.where(rng.random((N, 8, 1, V)) < quiet, calm, loud)
    return np.minimum(np.maximum(v, -LIM), LIM)
def setup_inputs(rng):
    quiet = rng.permuted(np.tile(np.array([0.0, 0.1, 0.3, 0.5, 0.7, 0.9, 0.95, 1.0]), (N, 1)), axis=1).reshape(N, 8, 1, 1)
    rest = rng.permuted(np.tile(np.array([0.0, 0.0, 0.0, 0.0, 0.3, 0.6, 0.8, 0.92]), (N, 1)), axis=1).reshape(N, 8, 1)
    v = crowd(rng, quiet) * (rng.random((N, 8, 1, V)) > 0.03); p = points(rng)
    p = np.where(rng.random((N, 8, V)) < rest, np.arange(V), p)
    o = np.argsort(rng.random((N, 8, V)), axis=-1); t = V // 16; i = o[..., :t]; s = o[..., t:2 * t]
    np.put_along_axis(v, i[:, :, None, :], np.take_along_axis(v, s[:, :, None, :], 3) * signs(rng, N, 8, 1, t), 3)
    np.put_along_axis(p, i, s, 2)
    return pack(v, p)
def setup_inputs_room(rng):
    v = signs(rng, N, 8, 16, V) * rng.integers(4, 1001, (N, 8, 16, V)); p = np.zeros((N, 8, V), np.int64)
    for q in range(N):
        for g in range(8):
            o = rng.permutation(V); a, b, z, m = o[:32], o[32:64], o[64:320], o[320:]
            v[q, g][:, b] = signs(rng, 16, 32) * rng.integers(5000, LIM + 1, (16, 32))
            v[q, g][:, o[64:320]] = 0; v[q, g][:, a] = 0
            v[q, g][rng.integers(0, 16, 32), a] = signs(rng, 32) * rng.integers(1, 4, 32)
            u = rng.random(V)
            w = np.where(u < 0.5, z[rng.integers(0, 256, V)], np.where(u < 0.75, b[rng.integers(0, 32, V)], np.arange(V)))
            w[b] = np.where(rng.random(32) < 0.5, b, z[rng.integers(0, 256, 32)])
            w[z] = rng.integers(V, W, 256)
            w[z[:H]] = V + np.arange(H) * G + G - 1; w[z[H:2 * H]] = V + np.arange(H) * G; w[a[:2 * H]] = z[:2 * H]
            n = int(rng.choice(np.array([0, 1, G - 1, G, G + 1, V - 320])))
            if q == 0: n = (G, G + 1, V - 320, G - 1, 1, 0, G, G + 1)[g]
            w[rng.permutation(m)[:n]] = a[rng.integers(0, 32, n)]
            p[q, g] = w
    return pack(v, p)
def setup_inputs_ties(rng):
    v = np.zeros((N, 8, 16, V), np.int64); p = np.zeros((N, 8, V), np.int64); h = (V - 2) // 2
    alt = np.where(np.arange(16) % 2 == 0, 1, -1)[:, None]
    for q in range(N):
        for g in range(8):
            o = rng.permutation(V); s, i = o[2:2 + h], o[2 + h:2 + 2 * h]
            y = np.repeat(2 * np.exp2(17 * rng.random((8, h))).astype(np.int64), 2, axis=0) * signs(rng, 16, h)
            one = np.zeros((16, h), np.int64); one[rng.integers(0, 16, h), np.arange(h)] = signs(rng, h)
            big = signs(rng, 16, h) * rng.integers(1, LIM + 1, (16, h)); sg = signs(rng, h); k = rng.integers(0, 7, h)
            kinds = np.stack([y * sg, (y >> 1) * sg, y * sg + one, y * alt * sg, big, 0 * y, big])
            v[q, g, int(rng.integers(0, 16)), o[0]] = 1
            v[q, g][:, s] = y; v[q, g][:, i] = kinds[k, :, np.arange(h)].T
            p[q, g, o[:2]] = rng.integers(0, W, 2)
            p[q, g, s] = rng.integers(0, W, h) if g % 2 == 0 else rng.choice(np.array([0, V - 1, V, W - 1]), h)
            p[q, g, i] = np.where(k == 4, o[0], np.where(k == 6, o[1], s))
    return pack(v, p)
def setup_inputs_still(rng):
    v = crowd(rng, np.zeros((N, 8, 1, 1)))
    lone = np.where(np.arange(16)[:, None] == rng.integers(0, 16, (N, 8, 1, V)), rng.integers(1, LIM + 1, (1, 8, 1, 1)) * signs(rng, N, 8, 1, V), 0)
    mask = np.zeros((N, 8, 1, 1), bool); q = int(rng.integers(0, N)); mask[q] = True; mask[:, int(rng.integers(0, 8))] = True
    own = np.argsort(rng.random((N, 8, V)), axis=-1)
    p = np.where(rng.random((N, 8, V)) < 0.5, rng.integers(V, W, (N, 8, V)), own); p[q] = own[q]
    return pack(np.where(mask, lone, v), p)
def setup_inputs_spread(rng):
    v = (np.exp2(19 * rng.random((N, 8, 1, V))) * np.exp2(-4 * rng.random((N, 8, 16, 1))) * (2 * rng.random((N, 8, 16, V)) - 1)).astype(np.int64)
    v = np.where(rng.random((N, 8, 1, V)) < 0.05, LIM * signs(rng, N, 8, 16, V), v) * (rng.random((N, 8, 1, V)) > 0.0625)
    p = points(rng); odd = (np.arange(8) % 2 == 1)[None, :, None]
    few = np.minimum((W * rng.random((N, 8, V)) ** 4).astype(np.int64), W - 1); few = np.where(rng.random((N, 8, V)) < 0.5, few, W - 1 - few)
    return pack(v, np.where(odd, few, p))
def small(rng, n):
    return signs(rng, 16, n) * rng.integers(1, 1001, (16, n))
def long(rng, n):
    return signs(rng, 16, n) * rng.integers(5000, LIM - 999, (16, n))
def stops(rng, v, p, red):
    o = rng.permutation(np.setdiff1d(np.arange(V), red)); y, w, z = o[:24], o[24:48], o[48:120].reshape(3, 24)
    base = long(rng, 24); i = np.concatenate([rng.integers(0, 24, len(red)), np.arange(24)]); m = np.concatenate([red, w])
    v[:, y] = base; v[:, m] = base[:, i] * signs(rng, len(m)) + small(rng, len(m))
    p[y] = y; p[red] = y[i[:len(red)]]; p[w] = z[0]; p[z[0]] = z[1]; p[z[1]] = z[2]; p[z[2]] = y
def far(rng, v, p):
    base = long(rng, 24); kk = rng.integers(0, 24, (N, G)); at = rng.integers(V, W, (N, V))
    kind = kk[(np.arange(N)[:, None] - (at - V) // G - 1) % N, (at - V) % G]
    for q in range(N):
        v[q] = base[:, kind[q]] * signs(rng, V) + small(rng, V)
        v[q][:, :G] = base[:, kk[q]] * signs(rng, G)
        p[q] = at[q]
def one(rng, v, p):
    base = long(rng, 1); j = rng.integers(0, G, N); turn = int(rng.integers(0, 2))
    for q in range(N):
        d = int(rng.integers(1, H + 1))
        v[q] = base * signs(rng, V) + small(rng, V)
        v[q][:, j[q]] = base[:, 0] * int(signs(rng, 1)[0])
        p[q] = j[q] if (q + turn) % 2 == 0 else V + (d - 1) * G + j[(q - d) % N]
        p[q, j[q]] = j[q]
def grow(rng, v, p):
    o = rng.permutation(16); u = int(rng.integers(480000, LIM - 199)); form = np.zeros((16, 3), np.int64)
    form[o[0]] = (u, u, 3 * u // 4); form[o[1:4]] = (-u, u, -(u // 2)); form[o[4:]] = (u, -(u // 3), 0)
    for q in range(N):
        m = rng.permutation(V); y, s, x, w, z = m[:24], m[24:48], m[48:120], m[120:168], m[168:312].reshape(3, 48)
        for k, i in ((0, x), (0, w), (1, y), (2, s)):
            v[q][:, i] = (form[:, k:k + 1] + rng.integers(-200, 201, (16, len(i)))) * signs(rng, len(i))
        p[q, x] = y[rng.integers(0, 24, 72)]; p[q, y] = s[rng.integers(0, 24, 24)]; p[q, s] = s
        p[q, w] = z[0]; p[q, z[0]] = z[1]; p[q, z[1]] = z[2]; p[q, z[2]] = V + rng.integers(0, H, 48) * G + rng.integers(0, 96, 48)
def setup_inputs_full(rng):
    v = np.zeros((N, 8, 16, V), np.int64); p = points(rng); kind = rng.permutation(np.array([0, 1, 2, 3, 4, 0, 1, 4]))
    for g in range(8):
        if kind[g] == 2: far(rng, v[:, g], p[:, g])
        elif kind[g] == 3: one(rng, v[:, g], p[:, g])
        elif kind[g] == 4: grow(rng, v[:, g], p[:, g])
        else:
            for q in range(N):
                red = np.arange(int(rng.integers(0, 16)), V, 16) if kind[g] == 0 else 256 * int(rng.integers(1, V // 256)) + np.arange(256)
                stops(rng, v[q, g], p[q, g], red)
    return pack(v, p)
def check_inputs(d):
    bad = []
    for k, lo, hi in (("x", -LIM, LIM), ("pt", 0, W - 1)):
        if np.min(d[k]) < lo or np.max(d[k]) > hi: bad.append("range of " + k)
    return bad
def reference(x, pt):
    v = x.astype(np.int64).reshape(N, 8, 16, V); p = pt.astype(np.int64)
    num = np.broadcast_to(np.arange(G), (N, 8, G)); gv = v[..., :G]
    for rnd in range(RO):
        w = np.concatenate([v] + [np.roll(gv, d, axis=0) for d in range(1, H + 1)], axis=3)
        ptr = np.concatenate([p] + [np.roll(num, d, axis=0) for d in range(1, H + 1)], axis=2)
        y = np.take_along_axis(w, p[:, :, None, :], 3)
        old = np.sum(np.abs(v), axis=2); lp = np.sum(np.abs(v + y), axis=2); lm = np.sum(np.abs(v - y), axis=2)
        plus = (lp > 0) & (lp < old); minus = (lm > 0) & (lm < old)
        v = np.where(plus[:, :, None, :], v + y, np.where(minus[:, :, None, :], v - y, v))
        done = plus | minus
        p = np.where(done, p, np.take_along_axis(ptr, p, 2))
        num = np.argsort(np.where(done, 0, 1), axis=2, kind="stable")[..., :G]
        gv = np.take_along_axis(v, num[:, :, None, :], 3)
    return {"yx": v.reshape(N, 128, V).astype(np.float32), "yc": p.astype(np.float32)}

@@ -1,0 +1,552 @@
+from concourse.mybir import AluOpType as ALU, ActivationFunctionType as AF
+
+V, G, W = 3584, 512, 4096
+PS = [(0, 1024), (1024, 2048), (2048, 3072), (3072, 3584)]
+XC, XB, SD, XA = 0, 4096, 8192, 15360
+BIGN = XA + V
+HUGE = float(2 ** 25)
+LOADS = [(0, 512), (512, 1792), (1792, 2816), (2816, 3328), (3328, 3584)]
+
+F32, BF, I32, U16 = "float32", "bfloat16", "int32", "uint16"
+SCRATCH = {
+    "xin": ("sbuf", [128, W], I32), "big": ("sbuf", [128, BIGN], F32), "nx": ("sbuf", [128, W], F32),
+    "ab0": ("sbuf", [128, V], F32), "ab1": ("sbuf", [128, V], F32),
+    "tab0": ("sbuf", [128, W], BF), "tab1": ("sbuf", [128, W], BF), "tab2": ("sbuf", [128, W], BF), "tab3": ("sbuf", [128, V], BF),
+    "ptb": ("sbuf", [128, 224], I32), "pti": ("sbuf", [128, 448], I32), "ptd": ("sbuf", [128, 448], BF),
+    "yl": ("sbuf", [128, 224], U16), "xl": ("sbuf", [128, 224], U16), "pl": ("sbuf", [128, 224], U16),
+    "l1": ("sbuf", [128, 32], U16), "l2": ("sbuf", [128, 32], U16), "l3": ("sbuf", [128, 32], U16),
+    "jp": ("sbuf", [128, 224], F32), "tj": ("sbuf", [128, 224], F32), "po": ("sbuf", [128, 224], F32),
+    "jc": ("sbuf", [128, 224], F32), "c16": ("sbuf", [128, 224], F32), "ycs": ("sbuf", [128, 224], F32),
+    "old": ("sbuf", [128, 32, 8], F32), "zz": ("sbuf", [128, 48, 8], F32),
+    "fz0": ("sbuf", [128, 50, 8], BF), "fz1": ("sbuf", [128, 50, 8], BF), "fq0": ("sbuf", [128, 36, 4], BF), "fq1": ("sbuf", [128, 36, 4], BF),
+    "rr": ("sbuf", [128, 264], BF), "t2": ("sbuf", [128, 16], F32), "t3": ("sbuf", [128, 256], F32),
+    "cm1": ("sbuf", [128, G], BF), "cm2": ("sbuf", [128, G], BF), "cm3": ("sbuf", [128, G], BF),
+    "gs0": ("sbuf", [128, G], F32), "gs1": ("sbuf", [128, G], F32), "hs0": ("sbuf", [128, G], BF), "hs1": ("sbuf", [128, G], BF),
+    "kk": ("sbuf", [128, G], F32), "kb": ("sbuf", [128, G], BF), "pc": ("sbuf", [128, 8], I32), "col": ("sbuf", [128, 8], F32),
+    "ur": ("sbuf", [128, 144], F32), "uu": ("sbuf", [128, 144], F32), "b1": ("sbuf", [128, 128], BF), "b2": ("sbuf", [128, 128], BF),
+    "blk": ("sbuf", [128, 128], BF), "tri": ("sbuf", [128, 128], BF), "upp": ("sbuf", [128, 128], BF), "idn": ("sbuf", [128, 128], F32),
+    "z1": ("sbuf", [128, 144], BF), "z16": ("sbuf", [128, 144], BF), "zf": ("sbuf", [128, 144], BF), "zw": ("sbuf", [128, 144], BF),
+    "gind": ("sbuf", [128, 8], F32), "one": ("sbuf", [128, 256], BF), "neg": ("sbuf", [128, 224], BF),
+    "sel": ("sbuf", [128, 256], BF), "ssc": ("sbuf", [128, 17 * 128], BF),
+    "la": ("psum", [128, 64, 8], F32), "lb": ("psum", [128, 64, 8], F32),
+    "da": ("psum", [128, 512], F32), "db": ("psum", [128, 512], F32), "xw": ("psum", [128, 512], F32),
+    "tb": ("psum", [128, 512], F32), "tw": ("psum", [128, 512], F32), "ob": ("psum", [128, 512], F32),
+}
+PSUM = [k for k, v in SCRATCH.items() if v[0] == "psum"]
+WRITES = ["x0", "x1", "x2", "h1", "h2"]
+SEMAPHORES = ["cv", "ca", "ct", "cg"] + ["in" + w for w in WRITES] + ["out" + w for w in WRITES] + ["dm%d" % k for k in range(20)]
+
+
+def rank_program(g, core, T, topo):
+    rank = T.rank_of(core)
+    if rank is None:
+        return
+    nxt = T.cores[(rank + 1) % len(T.cores)]
+    rid, pid, _ = topo.addr(nxt)
+    mask = topo.mask(core, nxt)
+    neng = len(topo.engines(core, nxt))
+
+    Q = {"v": g.vector, "a": g.scalar, "t": g.tensor, "g": g, "s": g.sync}
+    cnt = {"v": 0, "a": 0, "t": 0, "g": 0}
+    known = {q: {} for q in Q}
+    clocks, hist, top, ndma = {}, {}, {}, [0]
+
+    def order(q, rd, wr):
+        need = {}
+        for acc, isw in [(r, False) for r in rd] + [(w, True) for w in wr]:
+            for (lo, hi, w0, q0, tok) in hist.get(acc[0], []):
+                if q0 == "t" and q == "t":
+                    continue
+                if (acc[0] in PSUM and q0 != q) or ((w0 or isw) and lo < acc[2] and acc[1] < hi):
+                    need[tok[0]] = max(need.get(tok[0], 0), tok[1])
+        for s, val in sorted(need.items(), key=lambda t: -len(clocks.get(t, {}))):
+            if known[q].get(s, 0) < val:
+                Q[q].wait_ge(T.sem[s], val)
+                known[q][s] = val
+                for s2, v2 in clocks.get((s, val), {}).items():
+                    known[q][s2] = max(known[q].get(s2, 0), v2)
+
+    def note(q, rd, wr, tok, by):
+        clocks[tok] = dict(known[q])
+        top[tok[0]] = max(top.get(tok[0], 0), tok[1])
+        for acc in wr:
+            h = hist.setdefault(acc[0], [])
+            if acc[0] not in PSUM:
+                h[:] = [e for e in h if not (acc[1] <= e[0] and e[1] <= acc[2])]
+            h.append((acc[1], acc[2], True, by, tok))
+        for acc in rd:
+            hist.setdefault(acc[0], []).append((acc[1], acc[2], False, by, tok))
+
+    def op(q, call, rd, wr):
+        order(q, rd, wr)
+        cnt[q] += 1
+        call().then_inc(T.sem["c" + q], 1)
+        note(q, rd, wr, ("c" + q, cnt[q]), q)
+
+    def dma(q, out, in_, rd, wr):
+        order(q, rd, wr)
+        s = "dm%d" % ndma[0]
+        ndma[0] += 1
+        Q[q].dma_start(out, in_).then_inc(T.sem[s], 16)
+        note(q, rd, wr, (s, 16), "dma")
+
+    def send(dst, src, name):
+        order("g", [src], [])
+        g.remote_dma(A(dst), A(src), T.sem["in" + name], T.sem["out" + name], pid, rid, mask)
+        note("g", [src], [], ("out" + name, neng), "dma")
+        note("g", [], [dst], ("in" + name, neng), "dma")
+        clocks[("in" + name, neng)] = {}
+
+    def A(r):
+        return T[r[0]][:, r[1]:r[2]]
+
+    def A3(r, step=8):
+        return T[r[0]][:, r[1] // 8:r[2] // 8, 0:step]
+
+    def gat(win, off):
+        return T[win[0]][:, win[1]:win[2]].indirect(T[off[0]][:, off[1]:off[2]])
+
+    def vcopy(o, i):
+        op("v", lambda: g.vector.tensor_copy(A(o), A(i)), [i], [o])
+
+    def vts(o, i, s1, s2, *ops):
+        cols = [s for s in (s1, s2) if isinstance(s, tuple)]
+        args = [A(s) if isinstance(s, tuple) else s for s in (s1, s2)]
+        op("v", lambda: g.vector.tensor_scalar(A(o), A(i), args[0], args[1], *ops), [i] + cols, [o])
+
+    def vtt(o, i0, i1, alu):
+        op("v", lambda: g.vector.tensor_tensor(A(o), A(i0), A(i1), alu), [i0, i1], [o])
+
+    def vset(o, c, lo=None, hi=None):
+        op("v", lambda: g.vector.memset(T[o][:] if lo is None else T[o][:, lo:hi], c), [], [(o, lo or 0, hi or 1 << 20)])
+
+    def act(o, i, fn, **kw):
+        cols = [s for s in kw.values() if isinstance(s, tuple)]
+        args = {k: A(s) if isinstance(s, tuple) else s for k, s in kw.items()}
+        op("a", lambda: g.scalar.activation(A(o), A(i), fn, **args), [i] + cols, [o])
+
+    def pick(q, o, win, off):
+        if q == "v":
+            op("v", lambda: g.vector.tensor_copy(A(o), gat(win, off)), [win, off], [o])
+        else:
+            op("a", lambda: g.scalar.activation(A(o), gat(win, off), AF.Copy), [win, off], [o])
+
+    def vgt(o, win, off, i1, alu):
+        op("v", lambda: g.vector.tensor_tensor(A(o), gat(win, off), A(i1), alu), [win, off, i1], [o])
+
+    def mm(o, oap, l, lap, r, rap, st, sp):
+        op("t", lambda: g.tensor.matmul(oap, lap, rap, st, sp), [l, r], [o])
+
+    def onto(z, i):
+        return T[z][:, 15 - i:143 - i]
+
+    def wrap(o, z, src, st=True, sp=True):
+        for i in range(16):
+            mm(o, A(o), (z, 0, 144), onto(z, i), src, T[src[0]][:, src[1] + i:src[2]:16], st and i == 0, sp and i == 15)
+
+    def stride(p):
+        return (PS[p][1] - PS[p][0]) // 128
+
+    def sums(ab, p, bank, b0):
+        lo, hi = PS[p]
+        for m in range(stride(p)):
+            mm((bank, 8 * b0, 8 * b0 + 64), T[bank][:, b0:b0 + 8, m], (ab, lo, hi), T[ab][:, lo + m:hi:stride(p)],
+               ("gind", 0, 8), T.gind[:, :], True, True)
+
+    def lists(tab, p0, p1, bank):
+        c0, c1 = PS[p0][0] // 16, PS[p1 - 1][1] // 16
+        o = (bank, c0, c1)
+        wrap(o, "zw", (tab, 16 * c0, 16 * c1))
+        return [lambda: vcopy(("yl", c0, c1), o), lambda: vtt(("jp", c0, c1), ("jc", c0, c1), o, ALU.subtract)]
+
+    def place(r, p, sg):
+        lo, hi = PS[p]
+        if r == 2 or p == 3:
+            return SD + (0 if r == 0 else 2 * lo) + sg * (hi - lo)
+        return SD + (1024 if r == 0 else 0) + sg * 3072 + lo
+
+    tiles = {}
+
+    def scaled(kind, a):
+        if (kind, a) not in tiles:
+            tiles[kind, a] = 128 * len(tiles)
+            act(("ssc", tiles[kind, a], tiles[kind, a] + 128), ("sel", 128 * kind, 128 * kind + 128), AF.Copy, scale=float(a))
+        return tiles[kind, a]
+
+    def jump(r, p, sg):
+        return scaled(p // 3, place(r, p, sg) - (XA, XB, XC)[r] - PS[p][0])
+
+    dma("a", T.xin[:, 0:G], T.x[:, 0:G], [], [("xin", 0, G)])
+    dma("s", T.ptb[:, :], T.pt[:, :], [], [("ptb", 0, 224)])
+    for lo, hi in LOADS[1:3]:
+        dma("s", T.xin[:, lo:hi], T.x[:, lo:hi], [], [("xin", lo, hi)])
+    op("g", lambda: g.iota(T.pc[:, 0:1], [[0, 1]], 0, 1), [], [("pc", 0, 1)])
+    op("g", lambda: g.iota(T.ur[:, :], [[1, 144]], -15, -1, allow_small_or_imprecise_dtypes=True), [], [("ur", 0, 144)])
+    vset("one", 1.0)
+    op("g", lambda: g.affine_select(T.sel[:, 0:128], T.one[:, 0:128], [[-1, 2], [-2, 64]], ALU.is_equal, 0.0, 0, 1), [("one", 0, 128)], [("sel", 0, 128)])
+    op("g", lambda: g.affine_select(T.sel[:, 128:256], T.one[:, 0:128], [[-1, 4], [-4, 32]], ALU.is_equal, 0.0, 0, 1), [("one", 0, 128)], [("sel", 128, 256)])
+    op("g", lambda: g.iota(T.c16[:, :], [[16, 224]], 0, 0, allow_small_or_imprecise_dtypes=True), [], [("c16", 0, 224)])
+    send(("xin", V, W), ("xin", 0, G), "x0")
+    op("g", lambda: g.iota(T.kk[:, :], [[1, G]], 0, 0, allow_small_or_imprecise_dtypes=True), [], [("kk", 0, G)])
+    vset("tab0", 0.0, 0, V)
+    vts(("pc", 4, 5), ("pc", 0, 1), 15, None, ALU.bitwise_and)
+    vset("neg", -1.0, 0, 192)
+    vcopy(("col", 0, 1), ("pc", 4, 5))
+    vset("neg", 0.0, 192, 224)
+    vts(("uu", 0, 144), ("ur", 0, 144), ("col", 0, 1), None, ALU.add)
+    vts(("col", 1, 2), ("col", 0, 1), 1.0, None, ALU.is_le)
+    op("v", lambda: g.vector.tensor_scalar(T.gind[:, :], T.uu[:, 15:143:16], 0.0, None, ALU.is_equal), [("uu", 0, 144)], [("gind", 0, 8)])
+    vts(("zw", 0, 144), ("uu", 0, 144), 0.0, ("col", 1, 2), ALU.is_equal, ALU.mult)
+    minus = scaled(0, -1)
+    for r, p in ((0, 0), (0, 3), (1, 0), (1, 3), (2, 0)):
+        jump(r, p, 0)
+        jump(r, p, 1)
+
+    def arrive(lo, hi, rest=True):
+        vts(("nx", lo, hi), ("xin", lo, hi), -1.0, None, ALU.mult)
+        if rest:
+            act(("ab0", lo, hi), ("nx", lo, hi), AF.Abs)
+            act(("big", XA + lo, XA + hi), ("nx", lo, hi), AF.Copy, scale=-1.0)
+
+    vts(("pti", 0, 224), ("ptb", 0, 224), 0xF00, None, ALU.bitwise_and)
+    vts(("pti", 224, 448), ("ptb", 0, 224), 0xFF, None, ALU.bitwise_and)
+    vset("rr", 0.0, 0, 8)
+    vcopy(("ptd", 0, 448), ("pti", 0, 448))
+    for k in range(2):
+        dma("s", T.tab0[k:128:16, 0:V], T.ptd[:, 224 * k:224 * k + 224], [("ptd", 224 * k, 224 * k + 224), ("tab0", 0, V)], [("row%d" % k, 0, V)])
+    hist["tab0"] += hist["row0"] + hist["row1"]
+    for lo, hi in LOADS[3:]:
+        dma("s", T.xin[:, lo:hi], T.x[:, lo:hi], [], [("xin", lo, hi)])
+    arrive(*LOADS[0])
+    vts(("b1", 0, 128), ("uu", 15, 143), 0.0, None, ALU.is_ge)
+    vts(("b2", 0, 128), ("uu", 15, 143), 15.0, None, ALU.is_le)
+    vts(("jc", 0, 224), ("c16", 0, 224), ("col", 0, 1), None, ALU.add)
+    vtt(("blk", 0, 128), ("b1", 0, 128), ("b2", 0, 128), ALU.mult)
+    op("g", lambda: g.affine_select(T.tri[:, :], T.blk[:, :], [[1, 128]], ALU.is_ge, 0.0, 0, -1), [("blk", 0, 128)], [("tri", 0, 128)])
+    op("g", lambda: g.affine_select(T.upp[:, :], T.blk[:, :], [[-1, 128]], ALU.is_gt, 0.0, 0, 1), [("blk", 0, 128)], [("upp", 0, 128)])
+    vts(("col", 2, 3), ("col", 0, 1), 13.0, -3584.0, ALU.is_equal, ALU.mult)
+    vts(("col", 3, 4), ("col", 0, 1), 0.0, 256.0, ALU.is_equal, ALU.mult)
+    vts(("col", 4, 5), ("col", 0, 1), 1.0, None, ALU.is_equal)
+    vts(("idn", 0, 128), ("ur", 15, 143), 0.0, None, ALU.is_equal)
+    vts(("col", 5, 6), ("col", 2, 3), 256.0, None, ALU.add)
+    vts(("z1", 0, 144), ("uu", 0, 144), 0.0, None, ALU.is_equal)
+    act(("kb", 0, G), ("kk", 0, G), AF.Identity, bias=-256.0)
+    act(("tab0", V, V + 256), ("kk", 0, 256), AF.Identity, scale=("col", 4, 5))
+    act(("tab0", V + 256, W), ("kk", 0, 256), AF.Identity, scale=("col", 4, 5), bias=("col", 3, 4))
+    arrive(*LOADS[1])
+    vts(("z16", 0, 144), ("uu", 0, 144), 0.0, 16.0, ALU.is_equal, ALU.mult)
+    vts(("zf", 0, 144), ("uu", 0, 144), 0.0, ("col", 5, 6), ALU.is_equal, ALU.mult)
+    for f in ("fz0", "fz1", "fq0", "fq1"):
+        vset(f, 0.0)
+    arrive(*LOADS[2])
+    first = lists("tab0", 0, 1, "da")
+    rest = lists("tab0", 1, 4, "db")
+    arrive(*LOADS[3])
+    arrive(V, W, False)
+    arrive(*LOADS[4])
+    first[0]()
+    for p in range(4):
+        sums("ab0", p, "lb", 8 * p)
+
+    def lengths():
+        op("v", lambda: g.vector.tensor_copy(A3(("old", 0, 192)), A3(("lb", 0, 192))), [("lb", 0, 192)], [("old", 0, 192)])
+        op("v", lambda: g.vector.tensor_copy(A3(("old", 192, 256), 4), A3(("lb", 192, 256), 4)), [("lb", 192, 256)], [("old", 192, 256)])
+    later = [rest[:1], [first[1], rest[1], lengths]]
+
+    for r in range(3):
+        last = r == 2
+        X0, X1 = (XA, XB, XC)[r], (XB, XC, XA)[r]
+        xs, x0 = ("xin", 0) if r == 0 else ("big", X0)
+        tab, ntab = "tab%d" % r, "tab%d" % (r + 1)
+        groups = [[0], [1], [2], [3]] if last else [[0, 1], [2], [3]]
+        grp = {p: (n, gp) for n, gp in enumerate(groups) for p in gp}
+
+        def lens(n):
+            return ("la", "lb")[n % 2], 256 * (n // 2), 64 * len(groups[n])
+
+        def start(n):
+            return (SD + (0 if 3 in groups[n] else 1024), XB, XC)[r]
+
+        def span(p, lo, hi):
+            return PS[p][0] + lo, (PS[p][1] if hi is None else PS[p][0] + hi)
+
+        def cols(n):
+            return PS[groups[n][0]][0] // 16, PS[groups[n][-1]][1] // 16
+
+        def form(p, sg, lo=0, hi=None):
+            a, b = span(p, lo, hi)
+            o, off = ("big", place(r, p, sg) + lo, place(r, p, sg) + lo + b - a), ("yl", a // 16, b // 16)
+            if sg:
+                vgt(o, ("nx", 0, W), off, (xs, x0 + a, x0 + b), ALU.add)
+            else:
+                vgt(o, (xs, x0, x0 + W), off, ("nx", a, b), ALU.subtract)
+
+        def size(p, sg, lo=0, hi=None):
+            a, b = span(p, lo, hi)
+            act(("ab%d" % sg, a, b), ("big", place(r, p, sg) + lo, place(r, p, sg) + lo + b - a), AF.Abs)
+            if hi is None:
+                n, gp = grp[p]
+                sums("ab%d" % sg, p, lens(n)[0], lens(n)[1] // 8 + 8 * (sg * len(gp) + gp.index(p)))
+
+        def both(p, sg, lo=0, hi=None):
+            form(p, sg, lo, hi)
+            size(p, sg, lo, hi)
+
+        def decide(n, steps=(0, 1, 2)):
+            gp = groups[n]
+            (bank, l0, w), st = lens(n), stride(gp[0])
+            L, z, o = (bank, l0, l0 + 2 * w), ("zz", 0, 2 * w), ("old", 64 * gp[0], 64 * gp[0] + w)
+            if 0 in steps:
+                op("v", lambda: g.vector.tensor_scalar(A3(z, st), A3(L, st), 0.0, HUGE, ALU.is_equal, ALU.mult), [L], [z])
+            if 1 in steps:
+                op("v", lambda: g.vector.tensor_tensor(A3(L, st), A3(L, st), A3(z, st), ALU.max), [L, z], [L])
+            if 2 in steps:
+                for sg in range(2):
+                    Ls, fz = (bank, l0 + sg * w, l0 + sg * w + w), ("fq%d" if st == 4 else "fz%d") % sg
+                    out = T[fz][:, 3:35:4, :] if st == 4 else T[fz][:, 1 + 16 * gp[0]:1 + 16 * (gp[-1] + 1):2, :]
+                    op("v", lambda: g.vector.tensor_tensor(out, A3(Ls, st), A3(o, st), ALU.is_lt), [Ls, o], [(fz, 128 * gp[0], 128 * gp[-1] + 128)])
+
+        def turn(n, what, const):
+            gp = groups[n]
+            bank, (c0, c1) = (("da" if n % 2 == 0 else "db"), "xw")[what], cols(n)
+            if const and what:
+                mm((bank, c0, c1), A((bank, c0, c1)), ("idn", 0, 128), T.idn[:, :], ("jc", c0, c1), A(("jc", c0, c1)), True, False)
+            elif const and (last or n < 2):
+                mm((bank, c0, c1), A((bank, c0, c1)), ("one", 0, 128), T.one[0:1, 0:128], ("neg", 0, c1 - c0), T.neg[0:1, 0:c1 - c0], True, False)
+            elif const:
+                mm((bank, 192, 256), A((bank, 192, 256)), ("one", 0, 128), T.one[0:1, 0:128], ("neg", 160, 224), T.neg[0:1, 160:224], True, False)
+            else:
+                for p in gp:
+                    flags(p, (bank, PS[p][0] // 16, PS[p][1] // 16), lambda sg: ("ssc", jump(r, p, sg)) if what else ("sel", 128 * (p // 3)), p == gp[-1])
+
+        def flags(p, out, rhs, stop):
+            H = 16 // stride(p)
+            for sg in range(2):
+                for h in range(H):
+                    fz, (rb, c) = ("fq%d" if H == 4 else "fz%d") % sg, rhs(sg)
+                    rs = (rb, c + 128 // H * h, c + 128 // H * h + out[2] - out[1])
+                    lap = T[fz][:, 3 - h:35 - h, :] if H == 4 else T[fz][:, 1 - h + 16 * p:17 - h + 16 * p, :]
+                    mm(out, A(out), (fz, 128 * p, 128 * p + 128), lap, rs, A(rs), False, stop and sg == 1 and h == H - 1)
+
+        def shorten(n):
+            gp = groups[n]
+            (bank, l0, w), st = lens(n), stride(gp[0])
+            o = ("old", 64 * gp[0], 64 * gp[0] + w)
+            for sg in range(2):
+                Ls = (bank, l0 + sg * w, l0 + sg * w + w)
+                op("v", lambda: g.vector.tensor_tensor(A3(o, st), A3(Ls, st), A3(o, st), ALU.min), [Ls, o], [o])
+
+        def xlist(n):
+            vts(("xl",) + cols(n), ("xw",) + cols(n), float(X0 - start(n)), None, ALU.add)
+
+        def tmul(n):
+            vtt(("tj",) + cols(n), ("da" if n % 2 == 0 else "db",) + cols(n), ("jp",) + cols(n), ALU.mult)
+
+        def plist(c0, c1):
+            vtt(("po", c0, c1), ("tj", c0, c1), ("jc", c0, c1), ALU.add)
+            vcopy(("pl", c0, c1), ("po", c0, c1))
+
+        def select(q, p, lo=0, hi=None):
+            a, b = span(p, lo, hi)
+            win = ("big", start(grp[p][0]), XA + V if r == 0 else place(r, p if last or p == 3 else 2, 1) + PS[p][1] - PS[p][0])
+            pick(q, ("big", X1 + a, X1 + b), win, ("xl", a // 16, b // 16))
+            if last:
+                dma("s", T.yx[:, a:b], T.big[:, X1 + a:X1 + b], [("big", X1 + a, X1 + b)], [])
+
+        def follow(q, a, b):
+            pick(q, (ntab, a, b), (tab, 0, W), ("pl", a // 16, b // 16))
+
+        def negate(q, lo, hi, X1=X1):
+            if q == "v":
+                vts(("nx", lo, hi), ("big", X1 + lo, X1 + hi), -1.0, None, ALU.mult)
+            else:
+                act(("nx", lo, hi), ("big", X1 + lo, X1 + hi), AF.Copy, scale=-1.0)
+
+        def scan(c0, c1, bank):
+            rd = [(bank, c0, c1), ("one", 0, c1 - c0), ("rr", c0, c0 + 1)]
+            op("v", lambda: g.vector.tensor_tensor_scan(A(("rr", c0 + 1, c1 + 1)), A(rd[1]), A(rd[0]), A(rd[2]), ALU.add, ALU.add), rd, [("rr", c0 + 1, c1 + 1)])
+
+        def ends(i0, i1):
+            for i in range(i0, i1):
+                c = ("rr", 16 * i + 16, 16 * i + 17)
+                mm(("tb", 0, 1), T.tb[:, 0:1], ("z1", 0, 144), onto("z1", i), c, A(c), i == 0, i == 15)
+
+        def pending():
+            for f in later.pop(0):
+                f()
+
+        form(0, 0)
+        pending()
+        form(1, 0)
+        size(0, 0)
+        size(1, 0)
+        both(0, 1)
+        pending()
+        both(1, 1)
+        if r == 1:
+            for p in range(1, 4):
+                jump(2, p, 0)
+                jump(2, p, 1)
+        turn(0, 0, True)
+        turn(0, 1, True)
+        if not last:
+            both(2, 0)
+            both(2, 1, 0, 512)
+            decide(0, (0, 1))
+            form(2, 1, 512)
+            decide(0, (2,))
+            turn(0, 1, False)
+            size(2, 1, 512)
+            turn(0, 0, False)
+            both(3, 0)
+            both(3, 1, 0, 320)
+            xlist(0)
+            both(3, 1, 320)
+            select("a", 0)
+            select("a", 1)
+            turn(1, 0, True)
+            decide(1, (0,))
+            scan(0, 128, "da")
+            decide(1, (1,))
+            tmul(0)
+            turn(2, 0, True)
+            flags(0, ("da", 224, 256), lambda sg: ("ssc", minus), False)
+            decide(1, (2,))
+            turn(1, 0, False)
+            ends(0, 8)
+            turn(1, 1, True)
+            turn(1, 1, False)
+            shorten(1)
+            decide(2, (0, 1))
+            scan(128, 192, "db")
+            decide(2, (2,))
+            turn(2, 0, False)
+            ends(8, 12)
+            xlist(1)
+            select("a", 2)
+            scan(192, 256, "da")
+            ends(12, 16)
+            wrap(("tw", 0, 16), "z1", ("rr", 1, 257))
+            vtt(("po", 0, 128), ("tj", 0, 128), ("jc", 0, 128), ALU.add)
+            vts(("cm1", 0, G), ("kb", 0, G), 256.0, ("tb", 0, 1), ALU.add, ALU.is_ge)
+            wrap(("tb", 32, 64), "z1", ("cm1", 0, G))
+            turn(2, 1, True)
+            turn(2, 1, False)
+            wrap(("ob", 0, 32), "z16", ("cm1", 0, G), True, False)
+            vcopy(("pl", 0, 128), ("po", 0, 128))
+            vcopy(("t2", 0, 16), ("tw", 0, 16))
+            tmul(1)
+            tmul(2)
+            vcopy(("l1", 0, 32), ("tb", 32, 64))
+            vgt(("cm2", 0, G), ("t2", 0, 16), ("l1", 0, 32), ("kk", 0, G), ALU.is_le)
+            R = ("rr", 0, 257)
+            mm(("tw", 256, 512), T.tw[:, 256:512], ("tri", 0, 128), T.tri[:, :], R, T.rr[:, 1:257], True, False)
+            mm(("tw", 256, 512), T.tw[:, 256:512], ("upp", 0, 128), T.upp[:, :], R, T.rr[:, 0:256], False, True)
+            wrap(("ob", 0, 32), "z1", ("cm2", 0, G), False, True)
+            wrap(("tb", 64, 96), "zf", ("cm1", 0, G), True, False)
+            wrap(("tb", 64, 96), "z16", ("cm2", 0, G), False, False)
+            xlist(2)
+            select("a", 3)
+            follow("a", 0, 768)
+            vcopy(("t3", 0, 256), ("tw", 256, 512))
+            vcopy(("l2", 0, 32), ("ob", 0, 32))
+            vgt(("cm3", 0, G), ("t3", 0, 256), ("l2", 0, 32), ("kk", 0, G), ALU.is_le)
+            wrap(("tb", 64, 96), "z1", ("cm3", 0, G), False, True)
+            for n, (z, i) in enumerate((("zf", 0), ("z16", 1), ("z1", 1))):
+                cm = ("cm%d" % (n + 1), 0, G)
+                mm(("xw", 0, G), T.xw[:, :], (z, 0, 144), onto(z, i), cm, A(cm), n == 0, n == 2)
+            shorten(0)
+            vcopy(("l3", 0, 32), ("tb", 64, 96))
+            gs, hs = ("gs%d" % r, 0, G), ("hs%d" % r, 0, G)
+            for h, q in enumerate("va"):
+                pick(q, (gs[0], 256 * h, 256 * h + 256), ("big", X1, X1 + V), ("l3", 16 * h, 16 * h + 16))
+            send(("big", X1 + V, X1 + W), gs, "x%d" % (r + 1))
+            plist(128, 224)
+            follow("a", 768, 1024)
+            f0 = lists(ntab, 0, 1, "da")
+            follow("a", *PS[1])
+            f1 = lists(ntab, 1, 2, "db")
+            act(hs, ("xw", 0, G), AF.Copy)
+            send((ntab, V, W), hs, "h%d" % (r + 1))
+            follow("a", 2048, V)
+            f2 = lists(ntab, 2, 4, "ob")
+            negate("v", 0, 1024)
+            f0[0]()
+            negate("v", 1024, 2048)
+            f1[0]()
+            f0[1]()
+            f1[1]()
+            shorten(2)
+            negate("a", 2048, V)
+            later = [[lambda negate=negate: negate("a", V, W)], f2]
+        else:
+            for h in range(2):
+                decide(0, (h,))
+                form(2, 0, 512 * h, 512 * (h + 1))
+            decide(0, (2,))
+            turn(0, 1, False)
+            turn(0, 0, False)
+            size(2, 0)
+            form(2, 1, 0, 512)
+            xlist(0)
+            select("a", 0, 0, 512)
+            size(2, 1, 0, 512)
+            turn(1, 0, True)
+            turn(1, 1, True)
+            decide(1, (0,))
+            both(2, 1, 512)
+            decide(1, (1,))
+            form(3, 0)
+            decide(1, (2,))
+            turn(1, 1, False)
+            turn(1, 0, False)
+            size(3, 0)
+            both(3, 1, 0, 320)
+            both(3, 1, 320)
+            select("v", 0, 512)
+            xlist(1)
+            select("a", 1)
+            turn(2, 1, True)
+            decide(2, (0,))
+            tmul(0)
+            decide(2, (1,))
+            tmul(1)
+            decide(2, (2,))
+            turn(2, 1, False)
+            turn(2, 0, True)
+            turn(2, 0, False)
+            turn(3, 0, True)
+            decide(3, (0,))
+            vtt(("po", 0, 128), ("tj", 0, 128), ("jc", 0, 128), ALU.add)
+            decide(3, (1,))
+            vcopy(("pl", 0, 128), ("po", 0, 128))
+            xlist(2)
+            turn(3, 1, True)
+            decide(3, (2,))
+            turn(3, 1, False)
+            turn(3, 0, False)
+
+            def finish(q, i0, i1):
+                follow(q, 224 * i0, 224 * i1)
+                for i in range(i0, i1):
+                    src = (ntab, 224 * i, 224 * i + 224)
+                    mm(("ob", 0, 224), T.ob[:, 0:224], ("zw", 0, 144), onto("zw", i), src, A(src), i == 0, i == 15)
+            finish("a", 0, 4)
+            select("v", 2, 0, 512)
+            xlist(3)
+            select("a", 3)
+            select("v", 2, 512)
+            finish("a", 4, 8)
+            tmul(2)
+            tmul(3)
+            plist(128, 224)
+            finish("v", 8, 11)
+            finish("a", 11, 13)
+            finish("v", 13, 14)
+            finish("a", 14, 15)
+            finish("v", 15, 16)
+            vcopy(("ycs", 0, 224), ("ob", 0, 224))
+            dma("a", T.yc[:, :], T.ycs[:, :], [("ycs", 0, 224)], [])
+
+    for s, val in top.items():
+        g.sync.wait_ge(T.sem[s], val)

@@ -2,39 +2,103 @@ from concourse.mybir import AluOpType as ALU, ActivationFunctionType as AF
 
 V, G, W = 3584, 512, 4096
 PS = [(0, 1024), (1024, 2048), (2048, 3072), (3072, 3584)]
+GROUPS = [[(0,), (1, 2), (3,)]] * 2 + [[(0,), (1,), (2,), (3,)]]
+LENS = [{(3, 0): ("la", 0), (0, 0): ("la", 32), (0, 1): ("la", 96),
+         (1, 0): ("lb", 0), (2, 0): ("lb", 64), (1, 1): ("lb", 128), (2, 1): ("lb", 192), (3, 1): ("tw", 32)}] * 2 + [
+        {(p, sg): (("la", "lb")[p % 2], 128 * (p // 2) + 64 * sg) for p in range(4) for sg in range(2)}]
+OLD = [32, 96, 160, 0]
 XC, XB, SD, XA = 0, 4096, 8192, 15360
-BIGN = XA + V
+BIGN = XA + W
+TA, TI, TB, TC = 0, W, 2 * W, 3 * W
 HUGE = float(2 ** 25)
-LOADS = [(0, 512), (512, 1792), (1792, 2816), (2816, 3328), (3328, 3584)]
+NT = 32
+
+SEARCH = {"v": "D1 D30 D31 C1 X1 C3 cm1 P16-48 t2 l1 cm2 t3 X3 Z l2 cm3 M l3 gs0 P48-56 n0-22 y0-16 m n22-50 y16-32 f0-32",
+          "a": "s0-16 g0-4 s16-48 s48-56 g4-16 gs1 g16-34 hs n50-56 g34-50",
+          "t": "sB2 sA3 sB3 R1 R30 T1 R31 E1 E3 t2 l1 t3 b3 T3 l2a l2 l3a l3 hs Y0-16 Y16-32"}
+PLAN = [
+    {"v": "A0-16 B0-16 old' A16-24 B16-24 A24-32 B24-32 A32-40 B32-40 D0 A40-48 X0 B40-44 C0 B44-48 P0-16 A48-56 B48-53 B53-56 " + SEARCH["v"],
+     "a": "n56-64' H16-24 H24-32 a0-16 b0-16 H32-40 a16-32 b16-32 a32-40 b32-40 a40-48 b40-44 b44-48 a48-56 b48-53 b53-56 " + SEARCH["a"],
+     "t": "o0' o1' x16-24 o2' x24-32 o3' x32-40 sA0 sB0 b0 sA1 T0 sB1 oth b1 E0 sA2 " + SEARCH["t"]},
+    {"v": "A0-16 B0-16 A16-24 B16-24 y32-48' A24-32 B24-32 A32-48 D0 y48-56' B32-40 X0 B40-44 C0 B44-48 P0-16 A48-56 B48-53 B53-56 " + SEARCH["v"],
+     "a": "n56-64' H16-24 H24-32 a0-16 g50-56' b0-16 a16-32 b16-32 a32-48 b32-40 f32-56' b40-44 b44-48 a48-56 b48-53 b53-56 " + SEARCH["a"],
+     "t": "x16-24 x24-32 Y32-48' sA0 sB0 b0 Y48-56' sA1 T0 sB1 oth sA2 b1 E0 " + SEARCH["t"]},
+    {"v": "A0-16 y32-48' B0-16 A16-24 B16-24 A24-32 B24-32 A32-48 y48-56' D0 B32-40 f32-56' P0-16 X0 B40-48 D1 A48-56 P16-32 X1 B48-56 "
+          "D2 s21-32 X2 P32-48 D3 s39-48 X3 P48-56 g14-28 g42-50 s51-56 yc",
+     "a": "n56-64' H16-24 H24-32 a0-16 b0-16 g50-56' a16-32 b16-32 a32-48 b32-40 s0-8 b40-48 s8-16 a48-56 s16-21 b48-56 "
+          "g0-14 s32-39 s48-51 g28-42 g50-56 yc",
+     "t": "x16-24 x24-32 Y32-48' sA0 sB0 b0 Y48-56' sA1 T0 sB1 b1 sA2 b2 T1 sB2 b3 T2 sA3 sB3 T3 yc"}]
 
 F32, BF, I32, U16 = "float32", "bfloat16", "int32", "uint16"
 SCRATCH = {
     "xin": ("sbuf", [128, W], I32), "big": ("sbuf", [128, BIGN], F32), "nx": ("sbuf", [128, W], F32),
-    "ab0": ("sbuf", [128, V], F32), "ab1": ("sbuf", [128, V], F32),
-    "tab0": ("sbuf", [128, W], BF), "tab1": ("sbuf", [128, W], BF), "tab2": ("sbuf", [128, W], BF), "tab3": ("sbuf", [128, V], BF),
-    "ptb": ("sbuf", [128, 224], I32), "pti": ("sbuf", [128, 448], I32), "ptd": ("sbuf", [128, 448], BF),
-    "yl": ("sbuf", [128, 224], U16), "xl": ("sbuf", [128, 224], U16), "pl": ("sbuf", [128, 224], U16),
+    "ab0": ("sbuf", [128, V], F32), "ab1": ("sbuf", [128, V], F32), "tab": ("sbuf", [128, 4 * W], BF),
+    "yy": ("sbuf", [128, 3 * G], F32), "ptb": ("sbuf", [128, 224], I32), "pti": ("sbuf", [128, 448], I32), "ptd": ("sbuf", [128, 448], BF),
+    "yl": ("sbuf", [128, 224], U16), "xl": ("sbuf", [128, 224], U16), "pl": ("sbuf", [128, 224], U16), "yf": ("sbuf", [128, 224], F32),
     "l1": ("sbuf", [128, 32], U16), "l2": ("sbuf", [128, 32], U16), "l3": ("sbuf", [128, 32], U16),
-    "jp": ("sbuf", [128, 224], F32), "tj": ("sbuf", [128, 224], F32), "po": ("sbuf", [128, 224], F32),
-    "jc": ("sbuf", [128, 224], F32), "c16": ("sbuf", [128, 224], F32), "ycs": ("sbuf", [128, 224], F32),
-    "old": ("sbuf", [128, 32, 8], F32), "zz": ("sbuf", [128, 48, 8], F32),
+    "c16": ("sbuf", [128, 224], F32), "c16b": ("sbuf", [128, 224], BF), "ycs": ("sbuf", [128, 224], F32),
+    "old": ("sbuf", [128, 224], F32), "cc": ("sbuf", [128, 448], F32), "zz": ("sbuf", [128, 448], F32),
     "fz0": ("sbuf", [128, 50, 8], BF), "fz1": ("sbuf", [128, 50, 8], BF), "fq0": ("sbuf", [128, 36, 4], BF), "fq1": ("sbuf", [128, 36, 4], BF),
     "rr": ("sbuf", [128, 264], BF), "t2": ("sbuf", [128, 16], F32), "t3": ("sbuf", [128, 256], F32),
     "cm1": ("sbuf", [128, G], BF), "cm2": ("sbuf", [128, G], BF), "cm3": ("sbuf", [128, G], BF),
     "gs0": ("sbuf", [128, G], F32), "gs1": ("sbuf", [128, G], F32), "hs0": ("sbuf", [128, G], BF), "hs1": ("sbuf", [128, G], BF),
-    "kk": ("sbuf", [128, G], F32), "kb": ("sbuf", [128, G], BF), "pc": ("sbuf", [128, 8], I32), "col": ("sbuf", [128, 8], F32),
+    "kk": ("sbuf", [128, G], F32), "kb": ("sbuf", [128, G], BF), "pc": ("sbuf", [128, 8], I32), "col": ("sbuf", [128, 8], F32), "hb": ("sbuf", [128, 16], F32),
     "ur": ("sbuf", [128, 144], F32), "uu": ("sbuf", [128, 144], F32), "b1": ("sbuf", [128, 128], BF), "b2": ("sbuf", [128, 128], BF),
     "blk": ("sbuf", [128, 128], BF), "tri": ("sbuf", [128, 128], BF), "upp": ("sbuf", [128, 128], BF), "idn": ("sbuf", [128, 128], F32),
     "z1": ("sbuf", [128, 144], BF), "z16": ("sbuf", [128, 144], BF), "zf": ("sbuf", [128, 144], BF), "zw": ("sbuf", [128, 144], BF),
-    "gind": ("sbuf", [128, 8], F32), "one": ("sbuf", [128, 256], BF), "neg": ("sbuf", [128, 224], BF),
-    "sel": ("sbuf", [128, 256], BF), "ssc": ("sbuf", [128, 17 * 128], BF),
-    "la": ("psum", [128, 64, 8], F32), "lb": ("psum", [128, 64, 8], F32),
-    "da": ("psum", [128, 512], F32), "db": ("psum", [128, 512], F32), "xw": ("psum", [128, 512], F32),
+    "gind": ("sbuf", [128, 8], F32), "one": ("sbuf", [128, 192], BF), "zer": ("sbuf", [128, 128], BF),
+    "ssc": ("sbuf", [128, NT * 128], BF),
+    "la": ("psum", [128, 512], F32), "lb": ("psum", [128, 512], F32),
+    "xa": ("psum", [128, 512], F32), "xb": ("psum", [128, 512], F32), "pw": ("psum", [128, 512], F32),
     "tb": ("psum", [128, 512], F32), "tw": ("psum", [128, 512], F32), "ob": ("psum", [128, 512], F32),
 }
 PSUM = [k for k, v in SCRATCH.items() if v[0] == "psum"]
 WRITES = ["x0", "x1", "x2", "h1", "h2"]
-SEMAPHORES = ["cv", "ca", "ct", "cg"] + ["in" + w for w in WRITES] + ["out" + w for w in WRITES] + ["dm%d" % k for k in range(20)]
+SEMAPHORES = ["cv", "ca", "ct", "cg"] + ["in" + w for w in WRITES] + ["out" + w for w in WRITES] + ["dm%d" % k for k in range(40)]
+
+
+def steps(q):
+    return [(r - s.endswith("'"), s.rstrip("'")) for r in range(3) for s in PLAN[r][q].split()]
+
+
+def spans(r, letter, lo, hi):
+    found = []
+    for q in "vat":
+        for r0, s in steps(q):
+            if r0 == r and s[0] == letter and "-" in s:
+                a, b = (64 * int(k) for k in s[1:].split("-"))
+                if lo <= a and b <= hi:
+                    found.append((q, s, a, b))
+    found.sort(key=lambda e: e[2])
+    assert [lo] + [e[3] for e in found] == [e[2] for e in found] + [hi], (r, letter, lo, hi, found)
+    return found
+
+
+def clash(acc, isw, seen):
+    return (seen[2] or isw) and seen[0] < acc[2] and acc[1] < seen[1]
+
+
+def arrange(jobs):
+    seen, pre = {}, []
+    for n, j in enumerate(jobs):
+        both = [(r, False) for r in j["rd"]] + [(w, True) for w in j["wr"]]
+        pre.append({e[3] for acc, isw in both for e in seen.get(acc[0], [])
+                    if clash(acc, isw, e) or (acc[0] in PSUM and (jobs[e[3]]["q"] != j["q"] or (j["q"] == "t" and acc[0] not in ("la", "lb"))))})
+        for acc in j["wr"]:
+            seen[acc[0]] = [e for e in seen.get(acc[0], []) if acc[0] in PSUM or not (acc[1] <= e[0] and e[1] <= acc[2])]
+        for acc, isw in both:
+            seen.setdefault(acc[0], []).append((acc[1], acc[2], isw, n))
+    lines = []
+    for q in "vatgs":
+        at = {s: k for k, s in enumerate(steps(q))} if q in "vat" else {}
+        lines.append(sorted((n for n, j in enumerate(jobs) if j["q"] == q), key=lambda n: (at[jobs[n]["step"]] if at and jobs[n]["step"] else -1, n)))
+    done, out = set(), []
+    while len(out) < len(jobs):
+        ready = [line for line in lines if line and pre[line[0]] <= done]
+        assert ready, [(jobs[line[0]]["step"], [jobs[m]["step"] for m in pre[line[0]] - done]) for line in lines if line]
+        out.append(min(ready).pop(0))
+        done.add(out[-1])
+    return out
 
 
 def rank_program(g, core, T, topo):
@@ -45,19 +109,426 @@ def rank_program(g, core, T, topo):
     rid, pid, _ = topo.addr(nxt)
     mask = topo.mask(core, nxt)
     neng = len(topo.engines(core, nxt))
-
     Q = {"v": g.vector, "a": g.scalar, "t": g.tensor, "g": g, "s": g.sync}
+
+    jobs, now = [], [None]
+
+    def job(q, calls, rd, wr, kind="op"):
+        jobs.append({"q": q, "calls": calls, "rd": rd, "wr": wr, "kind": kind, "step": now[0]})
+
+    def op(q, call, rd, wr):
+        job(q, [call], rd, wr)
+
+    def dma(q, out, in_, rd, wr, **kw):
+        job(q, [lambda: Q[q].dma_start(out, in_, **kw)], rd, wr, "dma")
+
+    def send(dst, src, name):
+        job("g", name, [src], [dst], "send")
+
+    def mms(calls):
+        job("t", [lambda c=c: g.tensor.matmul(c[1], c[3], c[5], c[6], c[7]) for c in calls],
+            sorted({c[2] for c in calls} | {c[4] for c in calls}), sorted({c[0] for c in calls}))
+
+    def A(r):
+        return T[r[0]][:, r[1]:r[2]]
+
+    def gat(win, off):
+        return T[win[0]][:, win[1]:win[2]].indirect(T[off[0]][:, off[1]:off[2]])
+
+    def vcopy(o, i):
+        op("v", lambda: g.vector.tensor_copy(A(o), A(i)), [i], [o])
+
+    def vts(o, i, s1, s2, *ops):
+        cols = [s for s in (s1, s2) if isinstance(s, tuple)]
+        args = [A(s) if isinstance(s, tuple) else s for s in (s1, s2)]
+        op("v", lambda: g.vector.tensor_scalar(A(o), A(i), args[0], args[1], *ops), [i] + cols, [o])
+
+    def vtt(o, i0, i1, alu, oap=None):
+        op("v", lambda: g.vector.tensor_tensor(A(o) if oap is None else oap, A(i0), A(i1), alu), [i0, i1], [o])
+
+    def vset(o, c, lo=None, hi=None):
+        op("v", lambda: g.vector.memset(T[o][:] if lo is None else T[o][:, lo:hi], c), [], [(o, lo or 0, hi or 1 << 20)])
+
+    def act(o, i, fn, **kw):
+        cols = [s for s in kw.values() if isinstance(s, tuple)]
+        args = {k: A(s) if isinstance(s, tuple) else s for k, s in kw.items()}
+        op("a", lambda: g.scalar.activation(A(o), A(i), fn, **args), [i] + cols, [o])
+
+    def copy(q, o, i, scale=1.0):
+        if q == "v":
+            vts(o, i, scale, None, ALU.mult)
+        else:
+            act(o, i, AF.Copy, scale=scale)
+
+    def pick(q, o, win, off, more=()):
+        if q == "v":
+            op("v", lambda: g.vector.tensor_copy(A(o), gat(win, off)), [win, off, *more], [o])
+        else:
+            op("a", lambda: g.scalar.activation(A(o), gat(win, off), AF.Copy), [win, off, *more], [o])
+
+    def vgt(o, win, off, i1, alu):
+        op("v", lambda: g.vector.tensor_tensor(A(o), gat(win, off), A(i1), alu), [win, off, i1], [o])
+
+    def plainly(o, l, r, st, sp):
+        return (o, A(o), l, A(l), r, A(r), st, sp)
+
+    def row(o, r, st):
+        return (o, A(o), ("one", 0, 128), T.one[0:1, 0:128], r, T[r[0]][0:1, r[1]:r[2]], st, False)
+
+    def iota(o, pattern, base, mult):
+        op("g", lambda: g.iota(A(o), pattern, base, mult, allow_small_or_imprecise_dtypes=True), [], [o])
+
+    def onto(o, z, i, src, st, sp, step=1):
+        return (o, A(o), (z, 0, 144), T[z][:, 15 - i:143 - i], src, T[src[0]][:, src[1] + (i if step > 1 else 0):src[2]:step], st, sp)
+
+    def wrap(o, z, src, st=True, sp=True):
+        mms([onto(o, z, i, src, st and i == 0, sp and i == 15, 16) for i in range(16)])
+
+    def stride(p):
+        return (PS[p][1] - PS[p][0]) // 128
+
+    def sums(ab, p, bank, c):
+        (lo, hi), st = PS[p], stride(p)
+        mms([((bank, c, c + 8 * st), T[bank][:, c + m:c + 8 * st:st], (ab, lo, hi), T[ab][:, lo + m:hi:st], ("gind", 0, 8), T.gind[:, :], True, True)
+             for m in range(st)])
+
+    def reach(r, p):
+        gp = [k for k in GROUPS[r] if p in k][0]
+        return PS[gp[0]][0], PS[gp[-1]][1]
+
+    def place(r, p, sg):
+        lo, hi = reach(r, p)
+        return (XA - 2 * hi if r == 0 else SD + 2 * lo) + sg * (hi - lo) - lo
+
+    tiles = {}
+    SHAPES = [[[-1, 2], [-2, 64]], [[-1, 4], [-4, 32]]]
+
+    def scaled(kind, a):
+        if (kind, a) not in tiles:
+            o = tiles[kind, a] = ("ssc", 128 * len(tiles), 128 * len(tiles) + 128)
+            op("g", lambda: g.affine_select(A(o), T.zer[:, :], SHAPES[kind], ALU.not_equal, float(a), 0, 1), [("zer", 0, 128)], [o])
+        return tiles[kind, a]
+
+    def weight(r, p, sg, what):
+        return scaled(p // 3, (place(r, p, sg) - (XA, XB, XC)[r], 1, (W, -W, -2 * W)[r])[what])
+
+    def weights(r):
+        for p in range(4):
+            for what in range(3):
+                for sg in range(2):
+                    weight(r, p, sg, what)
+
+    dma("a", T.xin[:, 0:G], T.x[:, 0:G], [], [("xin", 0, G)])
+    dma("s", T.ptb[:, :], T.pt[:, :], [], [("ptb", 0, 224)])
+    dma("s", T.xin[:, G:2048], T.x[:, G:2048], [], [("xin", G, 2048)])
+    op("g", lambda: g.iota(T.pc[:, 0:1], [[0, 1]], 0, 1), [], [("pc", 0, 1)])
+    iota(("ur", 0, 144), [[1, 144]], -15, -1)
+    iota(("c16", 0, 224), [[16, 224]], 0, 0)
+    iota(("kk", 0, G), [[1, G]], 0, 0)
+    vset("tab", 0.0, TA, TA + V)
+    vts(("pc", 4, 5), ("pc", 0, 1), 15, None, ALU.bitwise_and)
+    vset("zer", 0.0)
+    vcopy(("col", 0, 1), ("pc", 4, 5))
+    vset("one", 1.0)
+    vts(("col", 3, 4), ("col", 0, 1), 0.0, 16.0, ALU.is_equal, ALU.mult)
+    vts(("col", 4, 5), ("col", 0, 1), 1.0, None, ALU.is_equal)
+    vts(("uu", 0, 144), ("ur", 0, 144), ("col", 0, 1), None, ALU.add)
+    vts(("hb", 0, 16), ("c16", 0, 16), ("col", 3, 4), None, ALU.mult)
+    vts(("pti", 0, 224), ("ptb", 0, 224), 0xF00, None, ALU.bitwise_and)
+    vts(("pti", 224, 448), ("ptb", 0, 224), 0xFF, None, ALU.bitwise_and)
+    vts(("col", 1, 2), ("col", 0, 1), 1.0, None, ALU.is_le)
+    vcopy(("ptd", 0, 448), ("pti", 0, 448))
+    for k in range(2):
+        dma("s", T.tab[k:128:16, TA:TA + V], T.ptd[:, 224 * k:224 * k + 224], [("ptd", 224 * k, 224 * k + 224), ("tab", TA, TA + V)], [("row", k, k + 1)])
+    for lo, hi in PS[2:]:
+        dma("s", T.xin[:, lo:hi], T.x[:, lo:hi], [], [("xin", lo, hi)])
+    send(("xin", V, W), ("xin", 0, G), "x0")
+
+    def own(b0, b1):
+        for b in range(b0, b1):
+            at = TI + 256 * b if b < 16 else TA + V + 256 * (b - 16)
+            act(("tab", at, at + 256), ("kk", 0, 256), AF.Identity, scale=("col", 4, 5), bias=("hb", b % 16, b % 16 + 1))
+
+    def arrive(lo, hi, q="v"):
+        act(("ab0", lo, hi), ("xin", lo, hi), AF.Abs)
+        copy(q, ("big", XA + lo, XA + hi), ("xin", lo, hi), -1.0)
+
+    def first_lists(c0, c1, bank):
+        wrap((bank, c0, c1), "zw", ("tab", TA + 16 * c0, TA + 16 * c1))
+        jobs[-1]["rd"].append(("row", 0, 2))
+        vcopy(("yl", c0, c1), (bank, c0, c1))
+        vcopy(("yf", c0, c1), (bank, c0, c1))
+
+    own(0, 4)
+    op("v", lambda: g.vector.tensor_scalar(T.gind[:, :], T.uu[:, 15:143:16], 0.0, None, ALU.is_equal), [("uu", 0, 144)], [("gind", 0, 8)])
+    vts(("zw", 0, 144), ("uu", 0, 144), 0.0, ("col", 1, 2), ALU.is_equal, ALU.mult)
+    arrive(0, G)
+    own(4, 12)
+    vts(("b1", 0, 128), ("uu", 15, 143), 0.0, None, ALU.is_ge)
+    vts(("b2", 0, 128), ("uu", 15, 143), 15.0, None, ALU.is_le)
+    vts(("col", 2, 3), ("col", 0, 1), 13.0, -float(V), ALU.is_equal, ALU.mult)
+    vtt(("blk", 0, 128), ("b1", 0, 128), ("b2", 0, 128), ALU.mult)
+    vts(("col", 5, 6), ("col", 2, 3), 256.0, None, ALU.add)
+    vts(("idn", 0, 128), ("ur", 15, 143), 0.0, None, ALU.is_equal)
+    vcopy(("c16b", 0, 224), ("c16", 0, 224))
+    vts(("z1", 0, 144), ("uu", 0, 144), 0.0, None, ALU.is_equal)
+    vts(("z16", 0, 144), ("uu", 0, 144), 0.0, 16.0, ALU.is_equal, ALU.mult)
+    vts(("zf", 0, 144), ("uu", 0, 144), 0.0, ("col", 5, 6), ALU.is_equal, ALU.mult)
+    vset("rr", 0.0, 0, 8)
+    for f in ("fz0", "fz1", "fq0", "fq1"):
+        vset(f, 0.0)
+    weights(0)
+    scaled(0, -1)
+    op("g", lambda: g.affine_select(T.tri[:, :], T.blk[:, :], [[1, 128]], ALU.is_ge, 0.0, 0, -1), [("blk", 0, 128)], [("tri", 0, 128)])
+    op("g", lambda: g.affine_select(T.upp[:, :], T.blk[:, :], [[-1, 128]], ALU.is_gt, 0.0, 0, 1), [("blk", 0, 128)], [("upp", 0, 128)])
+    iota(("kb", 0, G), [[1, G]], -256, 0)
+    weights(1)
+    weights(2)
+    arrive(G, 2048)
+    own(12, 18)
+    first_lists(0, 128, "pw")
+    first_lists(128, 224, "tw")
+    for p in range(4):
+        if p >= 2:
+            arrive(*PS[p], "va"[p - 2])
+        now[0] = (-1, "o%d" % p)
+        sums("ab0", p, "lb", 256 + OLD[p])
+        now[0] = None
+    now[0] = (-1, "n56-64")
+    copy("a", ("big", XA + V, XA + W), ("xin", V, W), -1.0)
+    now[0] = (-1, "old")
+    vcopy(("old", 0, 224), ("lb", 256, 480))
+
+    def one_round(r):
+        last = r == 2
+        X0 = (XA, XB, XC)[r]
+        came, made = (("xin", 0), ("nx", 0), ("big", XC))[r], (("big", XA), ("big", XB), ("nx", 0))[r]
+        new, nneg = (("nx", 0), ("big", XC), ("big", XA))[r], (("big", XB), ("nx", 0), None)[r]
+        tw0, tw1 = (TA, TI, TI)[r], (TB, TC, TC + W)[r]
+        t0, t1 = (TA, TB, TC)[r], (TB, TC, TA)[r]
+
+        shared = [64 * int(s[1:].split("-")[0]) for r0, s in steps("a") if r0 == r and s[0] == "H"]
+
+        def step(name):
+            now[0] = (r, name)
+
+        def who(name):
+            step(name)
+            return "v" if (r, name) in steps("v") else "a"
+
+        def each(letter, lo, hi):
+            for q, s, a, b in spans(r, letter, lo, hi):
+                step(s)
+                yield q, a, b
+
+        def rg(buf, a, b):
+            return (buf[0], buf[1] + a, buf[1] + b)
+
+        def cols(*gp):
+            return PS[gp[0]][0] // 16, PS[gp[-1]][1] // 16
+
+        def lens(gp, sg):
+            (bank, c), (c0, c1) = LENS[r][gp[0], sg], cols(*gp)
+            return (bank, c, c + c1 - c0)
+
+        def region(what, c0, c1):
+            n = [k for k, gp in enumerate(GROUPS[r]) if cols(*gp)[0] <= c0][-1]
+            if what == 1 and n:
+                return (("ob", "pw")[n - 1], c0, c1)
+            at = 128 * what - cols(*GROUPS[r][n])[0]
+            return (("xa", "xb")[n % 2], at + c0, at + c1)
+
+        def form(gp, sg):
+            at, (lo, hi) = place(r, gp[0], sg), reach(r, gp[0])
+            win, mine = (made, came) if sg else (came, made)
+            for q, a, b in each("AB"[sg], lo, hi):
+                o, off = ("big", at + a, at + b), ("yl", a // 16, b // 16)
+                if a in shared:
+                    k, name = shared.index(a), now[0]
+                    y, x = ("yy", G * k, G * k + G), (("tw", "xb", "ob")[k], 0, G)
+                    if not sg:
+                        step("H%d-%d" % (a // 64, b // 64))
+                        pick("a", y, rg(came, 0, W), off)
+                        step("x%d-%d" % (a // 64, b // 64))
+                        mms([plainly(x, ("idn", 0, 128), ("big", X0 + a, X0 + b), True, True)])
+                        now[0] = name
+                    vtt(o, x, y, ALU.subtract if sg else ALU.add)
+                elif q == "v":
+                    vgt(o, rg(win, 0, W), off, rg(mine, a, b), ALU.subtract if (sg == 1) != last else ALU.add)
+                else:
+                    pick(q, o, rg(win, 0, W), off)
+                    dma("g", A(o), T.big[:, X0 + a:X0 + b], [("big", X0 + a, X0 + b), o], [o], accum_op=ALU.add)
+            for _, a, b in each("ab"[sg], lo, hi):
+                act(("ab%d" % sg, a, b), ("big", at + a, at + b), AF.Abs)
+            for p in gp:
+                step("s%s%d" % ("AB"[sg], p))
+                sums("ab%d" % sg, p, *LENS[r][p, sg])
+
+        def decide(gp, sgs=(0, 1)):
+            step("D%d" % gp[0] if len(sgs) == 2 else "D%d%d" % (gp[0], sgs[0]))
+            c0, c1 = cols(*gp)
+            for sg in sgs:
+                vtt(("cc", 224 * sg + c0, 224 * sg + c1), lens(gp, sg), ("old", OLD[gp[0]], OLD[gp[0]] + c1 - c0), ALU.is_lt)
+            for sg in sgs:
+                fz = ("fq%d" if gp == (3,) else "fz%d") % sg
+                out = T[fz][:, 3:35:4, :] if gp == (3,) else T[fz][:, 1 + 16 * gp[0]:17 + 16 * gp[-1]:2, :]
+                vtt((fz, c0, c1), lens(gp, sg), ("cc", 224 * sg + c0, 224 * sg + c1), ALU.min, out)
+
+        def shorten():
+            for L, z in ((("la", 0, 160), ("zz", 0, 160)), (("lb", 0, 256), ("zz", 160, 416)), (("tw", 32, 64), ("zz", 416, 448))):
+                step("Z")
+                vts(z, L, 0.0, HUGE, ALU.is_equal, ALU.mult)
+                step("M")
+                vtt(L, L, z, ALU.max)
+            step("m")
+            for p, sg, n in ((3, 0, 96), (1, 0, 128), (0, 1, 64), (1, 1, 128), (3, 1, 32)):
+                (bank, c), o = LENS[r][p, sg], ("old", OLD[p], OLD[p] + n)
+                vtt(o, (bank, c, c + n), o, ALU.min)
+
+        def begin(gp):
+            step("b%d" % gp[0])
+            mms([row(region(0, *cols(*gp)), ("c16b",) + cols(*gp), True), plainly(region(2, *cols(*gp)), ("idn", 0, 128), ("yf",) + cols(*gp), False, False)])
+
+        def flags(p, sg, out, tile, stop):
+            H, fz = 16 // stride(p), ("fq%d" if p == 3 else "fz%d") % sg
+            calls = []
+            for h in range(H):
+                rs = (tile[0], tile[1] + 128 // H * h, tile[1] + 128 // H * h + out[2] - out[1])
+                lap = T[fz][:, 3 - h:35 - h, :] if H == 4 else T[fz][:, 1 - h + 16 * p:17 - h + 16 * p, :]
+                calls.append((out, A(out), (fz,) + cols(p), lap, rs, A(rs), (out[:2], sg, h) == (("ob", 64), 0, 0), stop and h == H - 1))
+            mms(calls)
+
+        def turn(name, gp, whats, sgs=(0, 1), stop=True):
+            step(name)
+            for what in whats:
+                for p in gp:
+                    for sg in sgs:
+                        flags(p, sg, region(what, *cols(p)), weight(r, p, sg, what), stop and (what, p, sg) == (whats[-1], gp[-1], sgs[-1]))
+
+        def select(gp):
+            lo, hi = reach(r, gp[0])
+            win = ("big", place(r, gp[0], 0) + lo, XA + V) if r == 0 else ("big", X0, place(r, gp[0], 1) + hi)
+            step("X%d" % gp[0])
+            vts(("xl",) + cols(*gp), region(0, *cols(*gp)), float(X0 - win[1]), ("col", 0, 1), ALU.add, ALU.add)
+            for q, a, b in each("s", lo, hi):
+                pick(q, rg(new, a, b), win, ("xl", a // 16, b // 16))
+                if last:
+                    dma("s", T.yx[:, a:b], A(rg(new, a, b)), [rg(new, a, b)], [])
+
+        def places(lo, hi):
+            for _, a, b in each("P", lo, hi):
+                vts(("pl", a // 16, b // 16), region(2, a // 16, b // 16), float(t0 - tw0), None, ALU.add)
+
+        def follow():
+            for q, a, b in each("g", 0, V):
+                pick(q, ("tab", t1 + a, t1 + b), ("tab", tw0, tw1), ("pl", a // 16, b // 16), [("row", 0, 2)] * (r == 0))
+
+        def scan(c0, c1):
+            step("C%d" % (c0 // 64))
+            rd = [region(1, c0, c1), ("one", 0, c1 - c0), ("rr", c0, c0 + 1)]
+            op("v", lambda: g.vector.tensor_tensor_scan(A(("rr", c0 + 1, c1 + 1)), A(rd[1]), A(rd[0]), A(rd[2]), ALU.mult, ALU.add), rd, [("rr", c0 + 1, c1 + 1)])
+            step("E%d" % (c0 // 64))
+            mms([onto(("tb", 0, 1), "z1", i, ("rr", 16 * i + 16, 16 * i + 17), i == 0, i == 15) for i in range(c0 // 16, c1 // 16)])
+
+        def settle(gp):
+            form(gp, 0)
+            form(gp, 1)
+            begin(gp)
+            decide(gp)
+            turn("T%d" % gp[0], gp, (0, 2) if last else (1, 0, 2))
+            select(gp)
+
+        if last:
+            for gp in GROUPS[r]:
+                settle(gp)
+                places(*PS[gp[0]])
+            follow()
+            step("yc")
+            for i in range(16):
+                mms([onto(("ob", 0, 224), "zw", i, ("tab", t1 + 224 * i, t1 + 224 * i + 224), i == 0, i == 15)])
+            vcopy(("ycs", 0, 224), ("ob", 0, 224))
+            dma("a", T.yc[:, :], T.ycs[:, :], [("ycs", 0, 224)], [])
+            return
+        settle((0,))
+        scan(0, 64)
+        places(*PS[0])
+        step("oth")
+        mms([row(("pw", 224, 256), ("one", 0, 32), True)])
+        for sg in range(2):
+            flags(0, sg, ("pw", 224, 256), scaled(0, -1), False)
+        form((1, 2), 0)
+        form((1, 2), 1)
+        decide((1, 2))
+        turn("R1", (1, 2), (1,))
+        scan(64, 192)
+        for sg in range(2):
+            form((3,), sg)
+            decide((3,), (sg,))
+            turn("R3%d" % sg, (3,), (1,), (sg,), sg == 1)
+        scan(192, 256)
+        for gp in GROUPS[r][1:]:
+            begin(gp)
+            turn("T%d" % gp[0], gp, (0, 2))
+            select(gp)
+            places(*reach(r, gp[0]))
+        follow()
+        step("cm1")
+        vts(("cm1", 0, G), ("kb", 0, G), 256.0, ("tb", 0, 1), ALU.add, ALU.is_ge)
+        step("t2")
+        wrap(("tw", 0, 16), "z1", ("rr", 1, 257))
+        vcopy(("t2", 0, 16), ("tw", 0, 16))
+        step("l1")
+        wrap(("tb", 32, 64), "z1", ("cm1", 0, G))
+        vcopy(("l1", 0, 32), ("tb", 32, 64))
+        step("cm2")
+        vgt(("cm2", 0, G), ("t2", 0, 16), ("l1", 0, 32), ("kk", 0, G), ALU.is_le)
+        q, o = who("t3"), ("tw", 256, 512)
+        mms([plainly(o, ("tri", 0, 128), ("rr", 1, 257), True, False), plainly(o, ("upp", 0, 128), ("rr", 0, 256), False, True)])
+        copy(q, ("t3", 0, 256), o)
+        step("l2a")
+        wrap(("ob", 0, 32), "z16", ("cm1", 0, G), True, False)
+        step("l2")
+        wrap(("ob", 0, 32), "z1", ("cm2", 0, G), False, True)
+        vcopy(("l2", 0, 32), ("ob", 0, 32))
+        step("l3a")
+        wrap(("tb", 64, 96), "zf", ("cm1", 0, G), True, False)
+        wrap(("tb", 64, 96), "z16", ("cm2", 0, G), False, False)
+        step("cm3")
+        vgt(("cm3", 0, G), ("t3", 0, 256), ("l2", 0, 32), ("kk", 0, G), ALU.is_le)
+        step("l3")
+        wrap(("tb", 64, 96), "z1", ("cm3", 0, G), False, True)
+        vcopy(("l3", 0, 32), ("tb", 64, 96))
+        gs, hs = ("gs%d" % r, 0, G), ("hs%d" % r, 0, G)
+        for h in range(2):
+            pick(who("gs%d" % h), (gs[0], 256 * h, 256 * h + 256), rg(new, 0, V), ("l3", 16 * h, 16 * h + 16))
+        send(rg(new, V, W), gs, "x%d" % (r + 1))
+        q = who("hs")
+        mms([onto(("xa", 0, G), z, i, ("cm%d" % (n + 1), 0, G), n == 0, n == 2) for n, (z, i) in enumerate((("zf", 0), ("z16", 1), ("z1", 1)))])
+        copy(q, hs, ("xa", 0, G))
+        send(("tab", t1 + V, t1 + W), hs, "h%d" % (r + 1))
+        for q, a, b in each("n", 0, W):
+            copy(q, rg(nneg, a, b), rg(new, a, b), -1.0)
+        shorten()
+        for bank, lo, hi in (("pw", 0, 2048), ("ob", 2048, V)):
+            for _, a, b in each("Y", lo, hi):
+                wrap((bank, a // 16, b // 16), "zw", ("tab", t1 + a, t1 + b))
+                step("y%d-%d" % (a // 64, b // 64))
+                vcopy(("yl", a // 16, b // 16), (bank, a // 16, b // 16))
+            for q, a, b in each("f", lo, hi):
+                copy(q, ("yf", a // 16, b // 16), (bank, a // 16, b // 16))
+
+    for r in range(3):
+        one_round(r)
+
     cnt = {"v": 0, "a": 0, "t": 0, "g": 0}
     known = {q: {} for q in Q}
-    clocks, hist, top, ndma = {}, {}, {}, [0]
+    clocks, hist, top, ndma = {}, {}, {}, 0
 
     def order(q, rd, wr):
         need = {}
         for acc, isw in [(r, False) for r in rd] + [(w, True) for w in wr]:
             for (lo, hi, w0, q0, tok) in hist.get(acc[0], []):
-                if q0 == "t" and q == "t":
-                    continue
-                if (acc[0] in PSUM and q0 != q) or ((w0 or isw) and lo < acc[2] and acc[1] < hi):
+                if (q0, q) != ("t", "t") and ((acc[0] in PSUM and q0 != q) or clash(acc, isw, (lo, hi, w0))):
                     need[tok[0]] = max(need.get(tok[0], 0), tok[1])
         for s, val in sorted(need.items(), key=lambda t: -len(clocks.get(t, {}))):
             if known[q].get(s, 0) < val:
@@ -77,476 +548,27 @@ def rank_program(g, core, T, topo):
         for acc in rd:
             hist.setdefault(acc[0], []).append((acc[1], acc[2], False, by, tok))
 
-    def op(q, call, rd, wr):
+    for n in arrange(jobs):
+        j = jobs[n]
+        q, rd, wr = j["q"], j["rd"], j["wr"]
+        if j["kind"] == "send":
+            name = j["calls"]
+            order(q, rd, [])
+            g.remote_dma(A(wr[0]), A(rd[0]), T.sem["in" + name], T.sem["out" + name], pid, rid, mask)
+            note(q, rd, [], ("out" + name, neng), "dma")
+            note(q, [], wr, ("in" + name, neng), "dma")
+            clocks[("in" + name, neng)] = {}
+            continue
         order(q, rd, wr)
-        cnt[q] += 1
-        call().then_inc(T.sem["c" + q], 1)
-        note(q, rd, wr, ("c" + q, cnt[q]), q)
-
-    def dma(q, out, in_, rd, wr):
-        order(q, rd, wr)
-        s = "dm%d" % ndma[0]
-        ndma[0] += 1
-        Q[q].dma_start(out, in_).then_inc(T.sem[s], 16)
-        note(q, rd, wr, (s, 16), "dma")
-
-    def send(dst, src, name):
-        order("g", [src], [])
-        g.remote_dma(A(dst), A(src), T.sem["in" + name], T.sem["out" + name], pid, rid, mask)
-        note("g", [src], [], ("out" + name, neng), "dma")
-        note("g", [], [dst], ("in" + name, neng), "dma")
-        clocks[("in" + name, neng)] = {}
-
-    def A(r):
-        return T[r[0]][:, r[1]:r[2]]
-
-    def A3(r, step=8):
-        return T[r[0]][:, r[1] // 8:r[2] // 8, 0:step]
-
-    def gat(win, off):
-        return T[win[0]][:, win[1]:win[2]].indirect(T[off[0]][:, off[1]:off[2]])
-
-    def vcopy(o, i):
-        op("v", lambda: g.vector.tensor_copy(A(o), A(i)), [i], [o])
-
-    def vts(o, i, s1, s2, *ops):
-        cols = [s for s in (s1, s2) if isinstance(s, tuple)]
-        args = [A(s) if isinstance(s, tuple) else s for s in (s1, s2)]
-        op("v", lambda: g.vector.tensor_scalar(A(o), A(i), args[0], args[1], *ops), [i] + cols, [o])
-
-    def vtt(o, i0, i1, alu):
-        op("v", lambda: g.vector.tensor_tensor(A(o), A(i0), A(i1), alu), [i0, i1], [o])
-
-    def vset(o, c, lo=None, hi=None):
-        op("v", lambda: g.vector.memset(T[o][:] if lo is None else T[o][:, lo:hi], c), [], [(o, lo or 0, hi or 1 << 20)])
-
-    def act(o, i, fn, **kw):
-        cols = [s for s in kw.values() if isinstance(s, tuple)]
-        args = {k: A(s) if isinstance(s, tuple) else s for k, s in kw.items()}
-        op("a", lambda: g.scalar.activation(A(o), A(i), fn, **args), [i] + cols, [o])
-
-    def pick(q, o, win, off):
-        if q == "v":
-            op("v", lambda: g.vector.tensor_copy(A(o), gat(win, off)), [win, off], [o])
+        if j["kind"] == "dma":
+            j["calls"][0]().then_inc(T.sem["dm%d" % ndma], 16)
+            note(q, rd, wr, ("dm%d" % ndma, 16), "dma")
+            ndma += 1
         else:
-            op("a", lambda: g.scalar.activation(A(o), gat(win, off), AF.Copy), [win, off], [o])
-
-    def vgt(o, win, off, i1, alu):
-        op("v", lambda: g.vector.tensor_tensor(A(o), gat(win, off), A(i1), alu), [win, off, i1], [o])
-
-    def mm(o, oap, l, lap, r, rap, st, sp):
-        op("t", lambda: g.tensor.matmul(oap, lap, rap, st, sp), [l, r], [o])
-
-    def onto(z, i):
-        return T[z][:, 15 - i:143 - i]
-
-    def wrap(o, z, src, st=True, sp=True):
-        for i in range(16):
-            mm(o, A(o), (z, 0, 144), onto(z, i), src, T[src[0]][:, src[1] + i:src[2]:16], st and i == 0, sp and i == 15)
-
-    def stride(p):
-        return (PS[p][1] - PS[p][0]) // 128
-
-    def sums(ab, p, bank, b0):
-        lo, hi = PS[p]
-        for m in range(stride(p)):
-            mm((bank, 8 * b0, 8 * b0 + 64), T[bank][:, b0:b0 + 8, m], (ab, lo, hi), T[ab][:, lo + m:hi:stride(p)],
-               ("gind", 0, 8), T.gind[:, :], True, True)
-
-    def lists(tab, p0, p1, bank):
-        c0, c1 = PS[p0][0] // 16, PS[p1 - 1][1] // 16
-        o = (bank, c0, c1)
-        wrap(o, "zw", (tab, 16 * c0, 16 * c1))
-        return [lambda: vcopy(("yl", c0, c1), o), lambda: vtt(("jp", c0, c1), ("jc", c0, c1), o, ALU.subtract)]
-
-    def place(r, p, sg):
-        lo, hi = PS[p]
-        if r == 2 or p == 3:
-            return SD + (0 if r == 0 else 2 * lo) + sg * (hi - lo)
-        return SD + (1024 if r == 0 else 0) + sg * 3072 + lo
-
-    tiles = {}
-
-    def scaled(kind, a):
-        if (kind, a) not in tiles:
-            tiles[kind, a] = 128 * len(tiles)
-            act(("ssc", tiles[kind, a], tiles[kind, a] + 128), ("sel", 128 * kind, 128 * kind + 128), AF.Copy, scale=float(a))
-        return tiles[kind, a]
-
-    def jump(r, p, sg):
-        return scaled(p // 3, place(r, p, sg) - (XA, XB, XC)[r] - PS[p][0])
-
-    dma("a", T.xin[:, 0:G], T.x[:, 0:G], [], [("xin", 0, G)])
-    dma("s", T.ptb[:, :], T.pt[:, :], [], [("ptb", 0, 224)])
-    for lo, hi in LOADS[1:3]:
-        dma("s", T.xin[:, lo:hi], T.x[:, lo:hi], [], [("xin", lo, hi)])
-    op("g", lambda: g.iota(T.pc[:, 0:1], [[0, 1]], 0, 1), [], [("pc", 0, 1)])
-    op("g", lambda: g.iota(T.ur[:, :], [[1, 144]], -15, -1, allow_small_or_imprecise_dtypes=True), [], [("ur", 0, 144)])
-    vset("one", 1.0)
-    op("g", lambda: g.affine_select(T.sel[:, 0:128], T.one[:, 0:128], [[-1, 2], [-2, 64]], ALU.is_equal, 0.0, 0, 1), [("one", 0, 128)], [("sel", 0, 128)])
-    op("g", lambda: g.affine_select(T.sel[:, 128:256], T.one[:, 0:128], [[-1, 4], [-4, 32]], ALU.is_equal, 0.0, 0, 1), [("one", 0, 128)], [("sel", 128, 256)])
-    op("g", lambda: g.iota(T.c16[:, :], [[16, 224]], 0, 0, allow_small_or_imprecise_dtypes=True), [], [("c16", 0, 224)])
-    send(("xin", V, W), ("xin", 0, G), "x0")
-    op("g", lambda: g.iota(T.kk[:, :], [[1, G]], 0, 0, allow_small_or_imprecise_dtypes=True), [], [("kk", 0, G)])
-    vset("tab0", 0.0, 0, V)
-    vts(("pc", 4, 5), ("pc", 0, 1), 15, None, ALU.bitwise_and)
-    vset("neg", -1.0, 0, 192)
-    vcopy(("col", 0, 1), ("pc", 4, 5))
-    vset("neg", 0.0, 192, 224)
-    vts(("uu", 0, 144), ("ur", 0, 144), ("col", 0, 1), None, ALU.add)
-    vts(("col", 1, 2), ("col", 0, 1), 1.0, None, ALU.is_le)
-    op("v", lambda: g.vector.tensor_scalar(T.gind[:, :], T.uu[:, 15:143:16], 0.0, None, ALU.is_equal), [("uu", 0, 144)], [("gind", 0, 8)])
-    vts(("zw", 0, 144), ("uu", 0, 144), 0.0, ("col", 1, 2), ALU.is_equal, ALU.mult)
-    minus = scaled(0, -1)
-    for r, p in ((0, 0), (0, 3), (1, 0), (1, 3), (2, 0)):
-        jump(r, p, 0)
-        jump(r, p, 1)
-
-    def arrive(lo, hi, rest=True):
-        vts(("nx", lo, hi), ("xin", lo, hi), -1.0, None, ALU.mult)
-        if rest:
-            act(("ab0", lo, hi), ("nx", lo, hi), AF.Abs)
-            act(("big", XA + lo, XA + hi), ("nx", lo, hi), AF.Copy, scale=-1.0)
-
-    vts(("pti", 0, 224), ("ptb", 0, 224), 0xF00, None, ALU.bitwise_and)
-    vts(("pti", 224, 448), ("ptb", 0, 224), 0xFF, None, ALU.bitwise_and)
-    vset("rr", 0.0, 0, 8)
-    vcopy(("ptd", 0, 448), ("pti", 0, 448))
-    for k in range(2):
-        dma("s", T.tab0[k:128:16, 0:V], T.ptd[:, 224 * k:224 * k + 224], [("ptd", 224 * k, 224 * k + 224), ("tab0", 0, V)], [("row%d" % k, 0, V)])
-    hist["tab0"] += hist["row0"] + hist["row1"]
-    for lo, hi in LOADS[3:]:
-        dma("s", T.xin[:, lo:hi], T.x[:, lo:hi], [], [("xin", lo, hi)])
-    arrive(*LOADS[0])
-    vts(("b1", 0, 128), ("uu", 15, 143), 0.0, None, ALU.is_ge)
-    vts(("b2", 0, 128), ("uu", 15, 143), 15.0, None, ALU.is_le)
-    vts(("jc", 0, 224), ("c16", 0, 224), ("col", 0, 1), None, ALU.add)
-    vtt(("blk", 0, 128), ("b1", 0, 128), ("b2", 0, 128), ALU.mult)
-    op("g", lambda: g.affine_select(T.tri[:, :], T.blk[:, :], [[1, 128]], ALU.is_ge, 0.0, 0, -1), [("blk", 0, 128)], [("tri", 0, 128)])
-    op("g", lambda: g.affine_select(T.upp[:, :], T.blk[:, :], [[-1, 128]], ALU.is_gt, 0.0, 0, 1), [("blk", 0, 128)], [("upp", 0, 128)])
-    vts(("col", 2, 3), ("col", 0, 1), 13.0, -3584.0, ALU.is_equal, ALU.mult)
-    vts(("col", 3, 4), ("col", 0, 1), 0.0, 256.0, ALU.is_equal, ALU.mult)
-    vts(("col", 4, 5), ("col", 0, 1), 1.0, None, ALU.is_equal)
-    vts(("idn", 0, 128), ("ur", 15, 143), 0.0, None, ALU.is_equal)
-    vts(("col", 5, 6), ("col", 2, 3), 256.0, None, ALU.add)
-    vts(("z1", 0, 144), ("uu", 0, 144), 0.0, None, ALU.is_equal)
-    act(("kb", 0, G), ("kk", 0, G), AF.Identity, bias=-256.0)
-    act(("tab0", V, V + 256), ("kk", 0, 256), AF.Identity, scale=("col", 4, 5))
-    act(("tab0", V + 256, W), ("kk", 0, 256), AF.Identity, scale=("col", 4, 5), bias=("col", 3, 4))
-    arrive(*LOADS[1])
-    vts(("z16", 0, 144), ("uu", 0, 144), 0.0, 16.0, ALU.is_equal, ALU.mult)
-    vts(("zf", 0, 144), ("uu", 0, 144), 0.0, ("col", 5, 6), ALU.is_equal, ALU.mult)
-    for f in ("fz0", "fz1", "fq0", "fq1"):
-        vset(f, 0.0)
-    arrive(*LOADS[2])
-    first = lists("tab0", 0, 1, "da")
-    rest = lists("tab0", 1, 4, "db")
-    arrive(*LOADS[3])
-    arrive(V, W, False)
-    arrive(*LOADS[4])
-    first[0]()
-    for p in range(4):
-        sums("ab0", p, "lb", 8 * p)
-
-    def lengths():
-        op("v", lambda: g.vector.tensor_copy(A3(("old", 0, 192)), A3(("lb", 0, 192))), [("lb", 0, 192)], [("old", 0, 192)])
-        op("v", lambda: g.vector.tensor_copy(A3(("old", 192, 256), 4), A3(("lb", 192, 256), 4)), [("lb", 192, 256)], [("old", 192, 256)])
-    later = [rest[:1], [first[1], rest[1], lengths]]
-
-    for r in range(3):
-        last = r == 2
-        X0, X1 = (XA, XB, XC)[r], (XB, XC, XA)[r]
-        xs, x0 = ("xin", 0) if r == 0 else ("big", X0)
-        tab, ntab = "tab%d" % r, "tab%d" % (r + 1)
-        groups = [[0], [1], [2], [3]] if last else [[0, 1], [2], [3]]
-        grp = {p: (n, gp) for n, gp in enumerate(groups) for p in gp}
-
-        def lens(n):
-            return ("la", "lb")[n % 2], 256 * (n // 2), 64 * len(groups[n])
-
-        def start(n):
-            return (SD + (0 if 3 in groups[n] else 1024), XB, XC)[r]
-
-        def span(p, lo, hi):
-            return PS[p][0] + lo, (PS[p][1] if hi is None else PS[p][0] + hi)
-
-        def cols(n):
-            return PS[groups[n][0]][0] // 16, PS[groups[n][-1]][1] // 16
-
-        def form(p, sg, lo=0, hi=None):
-            a, b = span(p, lo, hi)
-            o, off = ("big", place(r, p, sg) + lo, place(r, p, sg) + lo + b - a), ("yl", a // 16, b // 16)
-            if sg:
-                vgt(o, ("nx", 0, W), off, (xs, x0 + a, x0 + b), ALU.add)
-            else:
-                vgt(o, (xs, x0, x0 + W), off, ("nx", a, b), ALU.subtract)
-
-        def size(p, sg, lo=0, hi=None):
-            a, b = span(p, lo, hi)
-            act(("ab%d" % sg, a, b), ("big", place(r, p, sg) + lo, place(r, p, sg) + lo + b - a), AF.Abs)
-            if hi is None:
-                n, gp = grp[p]
-                sums("ab%d" % sg, p, lens(n)[0], lens(n)[1] // 8 + 8 * (sg * len(gp) + gp.index(p)))
-
-        def both(p, sg, lo=0, hi=None):
-            form(p, sg, lo, hi)
-            size(p, sg, lo, hi)
-
-        def decide(n, steps=(0, 1, 2)):
-            gp = groups[n]
-            (bank, l0, w), st = lens(n), stride(gp[0])
-            L, z, o = (bank, l0, l0 + 2 * w), ("zz", 0, 2 * w), ("old", 64 * gp[0], 64 * gp[0] + w)
-            if 0 in steps:
-                op("v", lambda: g.vector.tensor_scalar(A3(z, st), A3(L, st), 0.0, HUGE, ALU.is_equal, ALU.mult), [L], [z])
-            if 1 in steps:
-                op("v", lambda: g.vector.tensor_tensor(A3(L, st), A3(L, st), A3(z, st), ALU.max), [L, z], [L])
-            if 2 in steps:
-                for sg in range(2):
-                    Ls, fz = (bank, l0 + sg * w, l0 + sg * w + w), ("fq%d" if st == 4 else "fz%d") % sg
-                    out = T[fz][:, 3:35:4, :] if st == 4 else T[fz][:, 1 + 16 * gp[0]:1 + 16 * (gp[-1] + 1):2, :]
-                    op("v", lambda: g.vector.tensor_tensor(out, A3(Ls, st), A3(o, st), ALU.is_lt), [Ls, o], [(fz, 128 * gp[0], 128 * gp[-1] + 128)])
-
-        def turn(n, what, const):
-            gp = groups[n]
-            bank, (c0, c1) = (("da" if n % 2 == 0 else "db"), "xw")[what], cols(n)
-            if const and what:
-                mm((bank, c0, c1), A((bank, c0, c1)), ("idn", 0, 128), T.idn[:, :], ("jc", c0, c1), A(("jc", c0, c1)), True, False)
-            elif const and (last or n < 2):
-                mm((bank, c0, c1), A((bank, c0, c1)), ("one", 0, 128), T.one[0:1, 0:128], ("neg", 0, c1 - c0), T.neg[0:1, 0:c1 - c0], True, False)
-            elif const:
-                mm((bank, 192, 256), A((bank, 192, 256)), ("one", 0, 128), T.one[0:1, 0:128], ("neg", 160, 224), T.neg[0:1, 160:224], True, False)
-            else:
-                for p in gp:
-                    flags(p, (bank, PS[p][0] // 16, PS[p][1] // 16), lambda sg: ("ssc", jump(r, p, sg)) if what else ("sel", 128 * (p // 3)), p == gp[-1])
-
-        def flags(p, out, rhs, stop):
-            H = 16 // stride(p)
-            for sg in range(2):
-                for h in range(H):
-                    fz, (rb, c) = ("fq%d" if H == 4 else "fz%d") % sg, rhs(sg)
-                    rs = (rb, c + 128 // H * h, c + 128 // H * h + out[2] - out[1])
-                    lap = T[fz][:, 3 - h:35 - h, :] if H == 4 else T[fz][:, 1 - h + 16 * p:17 - h + 16 * p, :]
-                    mm(out, A(out), (fz, 128 * p, 128 * p + 128), lap, rs, A(rs), False, stop and sg == 1 and h == H - 1)
-
-        def shorten(n):
-            gp = groups[n]
-            (bank, l0, w), st = lens(n), stride(gp[0])
-            o = ("old", 64 * gp[0], 64 * gp[0] + w)
-            for sg in range(2):
-                Ls = (bank, l0 + sg * w, l0 + sg * w + w)
-                op("v", lambda: g.vector.tensor_tensor(A3(o, st), A3(Ls, st), A3(o, st), ALU.min), [Ls, o], [o])
-
-        def xlist(n):
-            vts(("xl",) + cols(n), ("xw",) + cols(n), float(X0 - start(n)), None, ALU.add)
-
-        def tmul(n):
-            vtt(("tj",) + cols(n), ("da" if n % 2 == 0 else "db",) + cols(n), ("jp",) + cols(n), ALU.mult)
-
-        def plist(c0, c1):
-            vtt(("po", c0, c1), ("tj", c0, c1), ("jc", c0, c1), ALU.add)
-            vcopy(("pl", c0, c1), ("po", c0, c1))
-
-        def select(q, p, lo=0, hi=None):
-            a, b = span(p, lo, hi)
-            win = ("big", start(grp[p][0]), XA + V if r == 0 else place(r, p if last or p == 3 else 2, 1) + PS[p][1] - PS[p][0])
-            pick(q, ("big", X1 + a, X1 + b), win, ("xl", a // 16, b // 16))
-            if last:
-                dma("s", T.yx[:, a:b], T.big[:, X1 + a:X1 + b], [("big", X1 + a, X1 + b)], [])
-
-        def follow(q, a, b):
-            pick(q, (ntab, a, b), (tab, 0, W), ("pl", a // 16, b // 16))
-
-        def negate(q, lo, hi, X1=X1):
-            if q == "v":
-                vts(("nx", lo, hi), ("big", X1 + lo, X1 + hi), -1.0, None, ALU.mult)
-            else:
-                act(("nx", lo, hi), ("big", X1 + lo, X1 + hi), AF.Copy, scale=-1.0)
-
-        def scan(c0, c1, bank):
-            rd = [(bank, c0, c1), ("one", 0, c1 - c0), ("rr", c0, c0 + 1)]
-            op("v", lambda: g.vector.tensor_tensor_scan(A(("rr", c0 + 1, c1 + 1)), A(rd[1]), A(rd[0]), A(rd[2]), ALU.add, ALU.add), rd, [("rr", c0 + 1, c1 + 1)])
-
-        def ends(i0, i1):
-            for i in range(i0, i1):
-                c = ("rr", 16 * i + 16, 16 * i + 17)
-                mm(("tb", 0, 1), T.tb[:, 0:1], ("z1", 0, 144), onto("z1", i), c, A(c), i == 0, i == 15)
-
-        def pending():
-            for f in later.pop(0):
-                f()
-
-        form(0, 0)
-        pending()
-        form(1, 0)
-        size(0, 0)
-        size(1, 0)
-        both(0, 1)
-        pending()
-        both(1, 1)
-        if r == 1:
-            for p in range(1, 4):
-                jump(2, p, 0)
-                jump(2, p, 1)
-        turn(0, 0, True)
-        turn(0, 1, True)
-        if not last:
-            both(2, 0)
-            both(2, 1, 0, 512)
-            decide(0, (0, 1))
-            form(2, 1, 512)
-            decide(0, (2,))
-            turn(0, 1, False)
-            size(2, 1, 512)
-            turn(0, 0, False)
-            both(3, 0)
-            both(3, 1, 0, 320)
-            xlist(0)
-            both(3, 1, 320)
-            select("a", 0)
-            select("a", 1)
-            turn(1, 0, True)
-            decide(1, (0,))
-            scan(0, 128, "da")
-            decide(1, (1,))
-            tmul(0)
-            turn(2, 0, True)
-            flags(0, ("da", 224, 256), lambda sg: ("ssc", minus), False)
-            decide(1, (2,))
-            turn(1, 0, False)
-            ends(0, 8)
-            turn(1, 1, True)
-            turn(1, 1, False)
-            shorten(1)
-            decide(2, (0, 1))
-            scan(128, 192, "db")
-            decide(2, (2,))
-            turn(2, 0, False)
-            ends(8, 12)
-            xlist(1)
-            select("a", 2)
-            scan(192, 256, "da")
-            ends(12, 16)
-            wrap(("tw", 0, 16), "z1", ("rr", 1, 257))
-            vtt(("po", 0, 128), ("tj", 0, 128), ("jc", 0, 128), ALU.add)
-            vts(("cm1", 0, G), ("kb", 0, G), 256.0, ("tb", 0, 1), ALU.add, ALU.is_ge)
-            wrap(("tb", 32, 64), "z1", ("cm1", 0, G))
-            turn(2, 1, True)
-            turn(2, 1, False)
-            wrap(("ob", 0, 32), "z16", ("cm1", 0, G), True, False)
-            vcopy(("pl", 0, 128), ("po", 0, 128))
-            vcopy(("t2", 0, 16), ("tw", 0, 16))
-            tmul(1)
-            tmul(2)
-            vcopy(("l1", 0, 32), ("tb", 32, 64))
-            vgt(("cm2", 0, G), ("t2", 0, 16), ("l1", 0, 32), ("kk", 0, G), ALU.is_le)
-            R = ("rr", 0, 257)
-            mm(("tw", 256, 512), T.tw[:, 256:512], ("tri", 0, 128), T.tri[:, :], R, T.rr[:, 1:257], True, False)
-            mm(("tw", 256, 512), T.tw[:, 256:512], ("upp", 0, 128), T.upp[:, :], R, T.rr[:, 0:256], False, True)
-            wrap(("ob", 0, 32), "z1", ("cm2", 0, G), False, True)
-            wrap(("tb", 64, 96), "zf", ("cm1", 0, G), True, False)
-            wrap(("tb", 64, 96), "z16", ("cm2", 0, G), False, False)
-            xlist(2)
-            select("a", 3)
-            follow("a", 0, 768)
-            vcopy(("t3", 0, 256), ("tw", 256, 512))
-            vcopy(("l2", 0, 32), ("ob", 0, 32))
-            vgt(("cm3", 0, G), ("t3", 0, 256), ("l2", 0, 32), ("kk", 0, G), ALU.is_le)
-            wrap(("tb", 64, 96), "z1", ("cm3", 0, G), False, True)
-            for n, (z, i) in enumerate((("zf", 0), ("z16", 1), ("z1", 1))):
-                cm = ("cm%d" % (n + 1), 0, G)
-                mm(("xw", 0, G), T.xw[:, :], (z, 0, 144), onto(z, i), cm, A(cm), n == 0, n == 2)
-            shorten(0)
-            vcopy(("l3", 0, 32), ("tb", 64, 96))
-            gs, hs = ("gs%d" % r, 0, G), ("hs%d" % r, 0, G)
-            for h, q in enumerate("va"):
-                pick(q, (gs[0], 256 * h, 256 * h + 256), ("big", X1, X1 + V), ("l3", 16 * h, 16 * h + 16))
-            send(("big", X1 + V, X1 + W), gs, "x%d" % (r + 1))
-            plist(128, 224)
-            follow("a", 768, 1024)
-            f0 = lists(ntab, 0, 1, "da")
-            follow("a", *PS[1])
-            f1 = lists(ntab, 1, 2, "db")
-            act(hs, ("xw", 0, G), AF.Copy)
-            send((ntab, V, W), hs, "h%d" % (r + 1))
-            follow("a", 2048, V)
-            f2 = lists(ntab, 2, 4, "ob")
-            negate("v", 0, 1024)
-            f0[0]()
-            negate("v", 1024, 2048)
-            f1[0]()
-            f0[1]()
-            f1[1]()
-            shorten(2)
-            negate("a", 2048, V)
-            later = [[lambda negate=negate: negate("a", V, W)], f2]
-        else:
-            for h in range(2):
-                decide(0, (h,))
-                form(2, 0, 512 * h, 512 * (h + 1))
-            decide(0, (2,))
-            turn(0, 1, False)
-            turn(0, 0, False)
-            size(2, 0)
-            form(2, 1, 0, 512)
-            xlist(0)
-            select("a", 0, 0, 512)
-            size(2, 1, 0, 512)
-            turn(1, 0, True)
-            turn(1, 1, True)
-            decide(1, (0,))
-            both(2, 1, 512)
-            decide(1, (1,))
-            form(3, 0)
-            decide(1, (2,))
-            turn(1, 1, False)
-            turn(1, 0, False)
-            size(3, 0)
-            both(3, 1, 0, 320)
-            both(3, 1, 320)
-            select("v", 0, 512)
-            xlist(1)
-            select("a", 1)
-            turn(2, 1, True)
-            decide(2, (0,))
-            tmul(0)
-            decide(2, (1,))
-            tmul(1)
-            decide(2, (2,))
-            turn(2, 1, False)
-            turn(2, 0, True)
-            turn(2, 0, False)
-            turn(3, 0, True)
-            decide(3, (0,))
-            vtt(("po", 0, 128), ("tj", 0, 128), ("jc", 0, 128), ALU.add)
-            decide(3, (1,))
-            vcopy(("pl", 0, 128), ("po", 0, 128))
-            xlist(2)
-            turn(3, 1, True)
-            decide(3, (2,))
-            turn(3, 1, False)
-            turn(3, 0, False)
-
-            def finish(q, i0, i1):
-                follow(q, 224 * i0, 224 * i1)
-                for i in range(i0, i1):
-                    src = (ntab, 224 * i, 224 * i + 224)
-                    mm(("ob", 0, 224), T.ob[:, 0:224], ("zw", 0, 144), onto("zw", i), src, A(src), i == 0, i == 15)
-            finish("a", 0, 4)
-            select("v", 2, 0, 512)
-            xlist(3)
-            select("a", 3)
-            select("v", 2, 512)
-            finish("a", 4, 8)
-            tmul(2)
-            tmul(3)
-            plist(128, 224)
-            finish("v", 8, 11)
-            finish("a", 11, 13)
-            finish("v", 13, 14)
-            finish("a", 14, 15)
-            finish("v", 15, 16)
-            vcopy(("ycs", 0, 224), ("ob", 0, 224))
-            dma("a", T.yc[:, :], T.ycs[:, :], [("ycs", 0, 224)], [])
+            for call in j["calls"]:
+                call().then_inc(T.sem["c" + q], 1)
+                cnt[q] += 1
+            note(q, rd, wr, ("c" + q, cnt[q]), q)
 
     for s, val in top.items():
         g.sync.wait_ge(T.sem[s], val)

@@ -3,8 +3,8 @@ from concourse.mybir import AluOpType as ALU, ActivationFunctionType as AF
 V, G, W = 3584, 512, 4096
 PS = [(0, 1024), (1024, 2048), (2048, 3072), (3072, 3584)]
 GROUPS = [[(0,), (1, 2), (3,)]] * 2 + [[(0,), (1,), (2,), (3,)]]
-LENS = [{(3, 0): ("la", 0), (0, 0): ("la", 32), (0, 1): ("la", 96),
-         (1, 0): ("lb", 0), (2, 0): ("lb", 64), (1, 1): ("lb", 128), (2, 1): ("lb", 192), (3, 1): ("tw", 32)}] * 2 + [
+LENS = [{(3, 0): ("la", 0), (0, 0): ("la", 32), (3, 1): ("la", 96), (0, 1): ("la", 128),
+         (1, 0): ("lb", 0), (2, 0): ("lb", 64), (1, 1): ("lb", 128), (2, 1): ("lb", 192)}] * 2 + [
         {(p, sg): (("la", "lb")[p % 2], 128 * (p // 2) + 64 * sg) for p in range(4) for sg in range(2)}]
 OLD = [32, 96, 160, 0]
 XC, XB, SD, XA = 0, 4096, 8192, 15360
@@ -13,36 +13,37 @@ TA, TI, TB, TC = 0, W, 2 * W, 3 * W
 HUGE = float(2 ** 25)
 NT = 32
 
-SEARCH = {"v": "D1 D30 D31 C1 X1 C3 cm1 P16-48 t2 l1 cm2 t3 X3 Z l2 cm3 M l3 gs0 P48-56 n0-22 y0-16 m n22-50 y16-32 f0-32",
-          "a": "s0-16 g0-4 s16-48 s48-56 g4-16 gs1 g16-34 hs n50-56 g34-50",
-          "t": "sB2 sA3 sB3 R1 R30 T1 R31 E1 E3 t2 l1 t3 b3 T3 l2a l2 l3a l3 hs Y0-16 Y16-32"}
+SEARCH = {"v": "P0-16 D1 D3 C1 X1 cm1 t2 g0-3 l1 P16-48 cm2 X3 P48-56 Z l2 cm3 M l3 gs0 g16-35 y0-16 m y16-32 ",
+          "a": "s0-16 s16-48 t3 s48-56 g3-16 gs1 g35-56 hs ",
+          "t": "sB2 sA3 sB3 R1 T1 R3 E1 t2 l1 t3 b3 T3 l2a l2 l3a l3 Y0-16 hs U Y16-32 Y32-56"}
+KEPT = (1024, 2560)
+PHASE = {"v": "A0-16 y32-56' B0-16 A16-24 B16-24 A24-32 B24-32 A32-40 B32-40 D0 A40-48 X0 B40-44 B44-48 C0 A48-56 B48-53 B53-56 ",
+         "a": "H16-24 H24-32 a0-16 H32-40 f0-56' b0-16 old' a16-32 b16-32 a32-40 b32-40 a40-48 b40-44 b44-48 a48-56 b48-53 b53-56 ",
+         "t": "x16-24 x24-32 x32-40 sA0 sB0 b0 sA1 T0 oth sB1 b1 sA2 E0 "}
 PLAN = [
-    {"v": "A0-16 B0-16 old' A16-24 B16-24 A24-32 B24-32 A32-40 B32-40 D0 A40-48 X0 B40-44 C0 B44-48 P0-16 A48-56 B48-53 B53-56 " + SEARCH["v"],
-     "a": "n56-64' H16-24 H24-32 a0-16 b0-16 H32-40 a16-32 b16-32 a32-40 b32-40 a40-48 b40-44 b44-48 a48-56 b48-53 b53-56 " + SEARCH["a"],
-     "t": "o0' o1' x16-24 o2' x24-32 o3' x32-40 sA0 sB0 b0 sA1 T0 sB1 oth b1 E0 sA2 " + SEARCH["t"]},
-    {"v": "A0-16 B0-16 A16-24 B16-24 y32-48' A24-32 B24-32 A32-48 D0 y48-56' B32-40 X0 B40-44 C0 B44-48 P0-16 A48-56 B48-53 B53-56 " + SEARCH["v"],
-     "a": "n56-64' H16-24 H24-32 a0-16 g50-56' b0-16 a16-32 b16-32 a32-48 b32-40 f32-56' b40-44 b44-48 a48-56 b48-53 b53-56 " + SEARCH["a"],
-     "t": "x16-24 x24-32 Y32-48' sA0 sB0 b0 Y48-56' sA1 T0 sB1 oth sA2 b1 E0 " + SEARCH["t"]},
-    {"v": "A0-16 y32-48' B0-16 A16-24 B16-24 A24-32 B24-32 A32-48 y48-56' D0 B32-40 f32-56' P0-16 X0 B40-48 D1 A48-56 P16-32 X1 B48-56 "
-          "D2 s21-32 X2 P32-48 D3 s39-48 X3 P48-56 g14-28 g42-50 s51-56 yc",
-     "a": "n56-64' H16-24 H24-32 a0-16 b0-16 g50-56' a16-32 b16-32 a32-48 b32-40 s0-8 b40-48 s8-16 a48-56 s16-21 b48-56 "
-          "g0-14 s32-39 s48-51 g28-42 g50-56 yc",
-     "t": "x16-24 x24-32 Y32-48' sA0 sB0 b0 Y48-56' sA1 T0 sB1 b1 sA2 b2 T1 sB2 b3 T2 sA3 sB3 T3 yc"}]
+    {"v": PHASE["v"] + SEARCH["v"], "a": PHASE["a"] + SEARCH["a"] + "U", "t": "o0' o1' o2' o3' " + PHASE["t"] + SEARCH["t"]},
+    {"v": PHASE["v"] + SEARCH["v"] + "U", "a": PHASE["a"] + SEARCH["a"], "t": PHASE["t"] + SEARCH["t"]},
+    {"v": "A0-16 y32-56' B0-16 A16-24 B16-24 A24-32 B24-32 A32-40 B32-40 D0 A40-48 X0 S0 P0-16 D1 B40-48 A48-56 X1 P16-32 B48-56 "
+          "F0-8 D2 F8-16 X2 S2 P32-48 D3 g0-7 X3 S3 P48-56 s48-56 F40-48 F48-56 g21-28 g42-52 yc",
+     "a": "H16-24 H24-32 a0-16 H32-40 b0-16 f0-56' a16-32 b16-32 a32-40 b32-40 a40-48 s0-16 b40-48 a48-56 b48-56 "
+          "s16-32 s40-48 s32-40 g7-21 g28-42 g52-56 yc",
+     "t": "x16-24 x24-32 x32-40 sA0 sB0 b0 sA1 T0 sB1 b1 T1 sA2 W0-8 b2 sB2 sA3 W8-16 T2 b3 sB3 T3 W40-48 W48-56 yc"}]
 
 F32, BF, I32, U16 = "float32", "bfloat16", "int32", "uint16"
 SCRATCH = {
-    "xin": ("sbuf", [128, W], I32), "big": ("sbuf", [128, BIGN], F32), "nx": ("sbuf", [128, W], F32),
+    "xin": ("sbuf", [128, W], I32), "big": ("sbuf", [128, BIGN], F32), "cp": ("sbuf", [128, V], F32),
     "ab0": ("sbuf", [128, V], F32), "ab1": ("sbuf", [128, V], F32), "tab": ("sbuf", [128, 4 * W], BF),
-    "yy": ("sbuf", [128, 3 * G], F32), "ptb": ("sbuf", [128, 224], I32), "pti": ("sbuf", [128, 448], I32), "ptd": ("sbuf", [128, 448], BF),
+    "yy": ("sbuf", [128, 4 * G], F32), "fan": ("sbuf", [128, 16 * 128], BF), "hib": ("sbuf", [128, 256], BF),
+    "turned": ("sbuf", [128, 224], BF), "ptb": ("sbuf", [128, 224], I32), "pti": ("sbuf", [128, 448], I32), "ptd": ("sbuf", [128, 448], BF),
     "yl": ("sbuf", [128, 224], U16), "xl": ("sbuf", [128, 224], U16), "pl": ("sbuf", [128, 224], U16), "yf": ("sbuf", [128, 224], F32),
     "l1": ("sbuf", [128, 32], U16), "l2": ("sbuf", [128, 32], U16), "l3": ("sbuf", [128, 32], U16),
-    "c16": ("sbuf", [128, 224], F32), "c16b": ("sbuf", [128, 224], BF), "ycs": ("sbuf", [128, 224], F32),
+    "c16b": ("sbuf", [128, 224], BF), "ycs": ("sbuf", [128, 224], F32),
     "old": ("sbuf", [128, 224], F32), "cc": ("sbuf", [128, 448], F32), "zz": ("sbuf", [128, 448], F32),
     "fz0": ("sbuf", [128, 50, 8], BF), "fz1": ("sbuf", [128, 50, 8], BF), "fq0": ("sbuf", [128, 36, 4], BF), "fq1": ("sbuf", [128, 36, 4], BF),
     "rr": ("sbuf", [128, 264], BF), "t2": ("sbuf", [128, 16], F32), "t3": ("sbuf", [128, 256], F32),
     "cm1": ("sbuf", [128, G], BF), "cm2": ("sbuf", [128, G], BF), "cm3": ("sbuf", [128, G], BF),
     "gs0": ("sbuf", [128, G], F32), "gs1": ("sbuf", [128, G], F32), "hs0": ("sbuf", [128, G], BF), "hs1": ("sbuf", [128, G], BF),
-    "kk": ("sbuf", [128, G], F32), "kb": ("sbuf", [128, G], BF), "pc": ("sbuf", [128, 8], I32), "col": ("sbuf", [128, 8], F32), "hb": ("sbuf", [128, 16], F32),
+    "kk": ("sbuf", [128, G], F32), "kb": ("sbuf", [128, G], BF), "pc": ("sbuf", [128, 8], I32), "col": ("sbuf", [128, 8], F32),
     "ur": ("sbuf", [128, 144], F32), "uu": ("sbuf", [128, 144], F32), "b1": ("sbuf", [128, 128], BF), "b2": ("sbuf", [128, 128], BF),
     "blk": ("sbuf", [128, 128], BF), "tri": ("sbuf", [128, 128], BF), "upp": ("sbuf", [128, 128], BF), "idn": ("sbuf", [128, 128], F32),
     "z1": ("sbuf", [128, 144], BF), "z16": ("sbuf", [128, 144], BF), "zf": ("sbuf", [128, 144], BF), "zw": ("sbuf", [128, 144], BF),
@@ -223,69 +224,67 @@ def rank_program(g, core, T, topo):
     dma("s", T.xin[:, G:2048], T.x[:, G:2048], [], [("xin", G, 2048)])
     op("g", lambda: g.iota(T.pc[:, 0:1], [[0, 1]], 0, 1), [], [("pc", 0, 1)])
     iota(("ur", 0, 144), [[1, 144]], -15, -1)
-    iota(("c16", 0, 224), [[16, 224]], 0, 0)
-    iota(("kk", 0, G), [[1, G]], 0, 0)
+    iota(("c16b", 0, 224), [[16, 224]], 0, 0)
     vset("tab", 0.0, TA, TA + V)
     vts(("pc", 4, 5), ("pc", 0, 1), 15, None, ALU.bitwise_and)
     vset("zer", 0.0)
     vcopy(("col", 0, 1), ("pc", 4, 5))
     vset("one", 1.0)
-    vts(("col", 3, 4), ("col", 0, 1), 0.0, 16.0, ALU.is_equal, ALU.mult)
-    vts(("col", 4, 5), ("col", 0, 1), 1.0, None, ALU.is_equal)
     vts(("uu", 0, 144), ("ur", 0, 144), ("col", 0, 1), None, ALU.add)
-    vts(("hb", 0, 16), ("c16", 0, 16), ("col", 3, 4), None, ALU.mult)
+    vts(("col", 1, 2), ("col", 0, 1), 1.0, None, ALU.is_le)
     vts(("pti", 0, 224), ("ptb", 0, 224), 0xF00, None, ALU.bitwise_and)
     vts(("pti", 224, 448), ("ptb", 0, 224), 0xFF, None, ALU.bitwise_and)
-    vts(("col", 1, 2), ("col", 0, 1), 1.0, None, ALU.is_le)
+    vts(("zw", 0, 144), ("uu", 0, 144), 0.0, ("col", 1, 2), ALU.is_equal, ALU.mult)
     vcopy(("ptd", 0, 448), ("pti", 0, 448))
+
+    def rows(at, n, k, src, rd):
+        dma("s", T.tab[k:128:16, at:at + n], src, [rd, ("tab", at, at + n)], [("row", at + k, at + k + 1)])
     for k in range(2):
-        dma("s", T.tab[k:128:16, TA:TA + V], T.ptd[:, 224 * k:224 * k + 224], [("ptd", 224 * k, 224 * k + 224), ("tab", TA, TA + V)], [("row", k, k + 1)])
+        rows(TA, V, k, T.ptd[:, 224 * k:224 * k + 224], ("ptd", 224 * k, 224 * k + 224))
     for lo, hi in PS[2:]:
         dma("s", T.xin[:, lo:hi], T.x[:, lo:hi], [], [("xin", lo, hi)])
     send(("xin", V, W), ("xin", 0, G), "x0")
+    iota(("kb", 0, G), [[1, G]], -256, 0)
 
-    def own(b0, b1):
-        for b in range(b0, b1):
-            at = TI + 256 * b if b < 16 else TA + V + 256 * (b - 16)
-            act(("tab", at, at + 256), ("kk", 0, 256), AF.Identity, scale=("col", 4, 5), bias=("hb", b % 16, b % 16 + 1))
-
-    def arrive(lo, hi, q="v"):
+    def arrive(lo, hi, q):
         act(("ab0", lo, hi), ("xin", lo, hi), AF.Abs)
-        copy(q, ("big", XA + lo, XA + hi), ("xin", lo, hi), -1.0)
+        copy(q, ("big", XA + lo, XA + hi), ("xin", lo, hi))
 
     def first_lists(c0, c1, bank):
         wrap((bank, c0, c1), "zw", ("tab", TA + 16 * c0, TA + 16 * c1))
-        jobs[-1]["rd"].append(("row", 0, 2))
+        jobs[-1]["rd"].append(("row", TA, TA + 2))
         vcopy(("yl", c0, c1), (bank, c0, c1))
         vcopy(("yf", c0, c1), (bank, c0, c1))
 
-    own(0, 4)
     op("v", lambda: g.vector.tensor_scalar(T.gind[:, :], T.uu[:, 15:143:16], 0.0, None, ALU.is_equal), [("uu", 0, 144)], [("gind", 0, 8)])
-    vts(("zw", 0, 144), ("uu", 0, 144), 0.0, ("col", 1, 2), ALU.is_equal, ALU.mult)
-    arrive(0, G)
-    own(4, 12)
+    arrive(0, G, "a")
+    vts(("idn", 0, 128), ("ur", 15, 143), 0.0, None, ALU.is_equal)
     vts(("b1", 0, 128), ("uu", 15, 143), 0.0, None, ALU.is_ge)
     vts(("b2", 0, 128), ("uu", 15, 143), 15.0, None, ALU.is_le)
     vts(("col", 2, 3), ("col", 0, 1), 13.0, -float(V), ALU.is_equal, ALU.mult)
     vtt(("blk", 0, 128), ("b1", 0, 128), ("b2", 0, 128), ALU.mult)
     vts(("col", 5, 6), ("col", 2, 3), 256.0, None, ALU.add)
-    vts(("idn", 0, 128), ("ur", 15, 143), 0.0, None, ALU.is_equal)
-    vcopy(("c16b", 0, 224), ("c16", 0, 224))
     vts(("z1", 0, 144), ("uu", 0, 144), 0.0, None, ALU.is_equal)
     vts(("z16", 0, 144), ("uu", 0, 144), 0.0, 16.0, ALU.is_equal, ALU.mult)
     vts(("zf", 0, 144), ("uu", 0, 144), 0.0, ("col", 5, 6), ALU.is_equal, ALU.mult)
+    vset("hib", 256.0)
     vset("rr", 0.0, 0, 8)
+    vts(("hib", 0, 256), ("hib", 0, 256), ("col", 0, 1), None, ALU.mult)
     for f in ("fz0", "fz1", "fq0", "fq1"):
         vset(f, 0.0)
     weights(0)
     scaled(0, -1)
+    iota(("kk", 0, G), [[1, G]], 0, 0)
     op("g", lambda: g.affine_select(T.tri[:, :], T.blk[:, :], [[1, 128]], ALU.is_ge, 0.0, 0, -1), [("blk", 0, 128)], [("tri", 0, 128)])
     op("g", lambda: g.affine_select(T.upp[:, :], T.blk[:, :], [[-1, 128]], ALU.is_gt, 0.0, 0, 1), [("blk", 0, 128)], [("upp", 0, 128)])
-    iota(("kb", 0, G), [[1, G]], -256, 0)
+    scaled(0, -2)
+    scaled(1, -2)
     weights(1)
     weights(2)
-    arrive(G, 2048)
-    own(12, 18)
+    for i in range(16):
+        op("g", lambda i=i: g.affine_select(T.fan[:, 128 * i:128 * i + 128], T.zer[:, :], [[-16, 8], [0, 16]], ALU.not_equal, 1.0, -i, 1),
+           [("zer", 0, 128)], [("fan", 128 * i, 128 * i + 128)])
+    arrive(G, 2048, "v")
     first_lists(0, 128, "pw")
     first_lists(128, 224, "tw")
     for p in range(4):
@@ -294,16 +293,19 @@ def rank_program(g, core, T, topo):
         now[0] = (-1, "o%d" % p)
         sums("ab0", p, "lb", 256 + OLD[p])
         now[0] = None
-    now[0] = (-1, "n56-64")
-    copy("a", ("big", XA + V, XA + W), ("xin", V, W), -1.0)
+    for at, n in ((0, V), (V, G)):
+        dma("s", T.tab[:, TI + at:TI + at + n], T.tab[:, TA:TA + n], [("tab", TA, TA + n), ("row", TA, TA + 2), ("xin", V, W)], [("tab", TI + at, TI + at + n)])
+    rows(TI, W, 0, T.hib[:, :], ("hib", 0, 256))
+    rows(TI, W, 1, T.kb[:, 256:G], ("kb", 256, G))
+    dma("s", T.tab[:, TA + V:TA + W], T.tab[:, TI:TI + G], [("tab", TI, TI + G), ("row", TI, TI + 2)], [("tab", TA + V, TA + W)])
     now[0] = (-1, "old")
-    vcopy(("old", 0, 224), ("lb", 256, 480))
+    copy("a", ("old", 0, 224), ("lb", 256, 480))
 
     def one_round(r):
         last = r == 2
         X0 = (XA, XB, XC)[r]
-        came, made = (("xin", 0), ("nx", 0), ("big", XC))[r], (("big", XA), ("big", XB), ("nx", 0))[r]
-        new, nneg = (("nx", 0), ("big", XC), ("big", XA))[r], (("big", XB), ("nx", 0), None)[r]
+        came, mine = (("xin", 0), ("big", XB), ("big", XC))[r], (("big", XA), ("cp", 0), ("cp", 0))[r]
+        new = ("big", (XB, XC, XA)[r])
         tw0, tw1 = (TA, TI, TI)[r], (TB, TC, TC + W)[r]
         t0, t1 = (TA, TB, TC)[r], (TB, TC, TA)[r]
 
@@ -327,25 +329,29 @@ def rank_program(g, core, T, topo):
         def cols(*gp):
             return PS[gp[0]][0] // 16, PS[gp[-1]][1] // 16
 
+        def turning(p):
+            c0, c1 = cols(p)
+            c0 = KEPT[1] // 16 if KEPT[0] // 16 <= c0 < KEPT[1] // 16 else c0
+            return (c0, c1) if c0 < c1 else None
+
         def lens(gp, sg):
             (bank, c), (c0, c1) = LENS[r][gp[0], sg], cols(*gp)
             return (bank, c, c + c1 - c0)
 
         def region(what, c0, c1):
             n = [k for k, gp in enumerate(GROUPS[r]) if cols(*gp)[0] <= c0][-1]
-            if what == 1 and n:
-                return (("ob", "pw")[n - 1], c0, c1)
+            if what == 1 and n and not last:
+                return ("pw", c0, c1)
             at = 128 * what - cols(*GROUPS[r][n])[0]
             return (("xa", "xb")[n % 2], at + c0, at + c1)
 
         def form(gp, sg):
             at, (lo, hi) = place(r, gp[0], sg), reach(r, gp[0])
-            win, mine = (made, came) if sg else (came, made)
             for q, a, b in each("AB"[sg], lo, hi):
                 o, off = ("big", at + a, at + b), ("yl", a // 16, b // 16)
                 if a in shared:
                     k, name = shared.index(a), now[0]
-                    y, x = ("yy", G * k, G * k + G), (("tw", "xb", "ob")[k], 0, G)
+                    y, x = ("yy", G * k, G * k + G), (("tw", "xb", "ob", "tb")[k], 0, G)
                     if not sg:
                         step("H%d-%d" % (a // 64, b // 64))
                         pick("a", y, rg(came, 0, W), off)
@@ -353,11 +359,8 @@ def rank_program(g, core, T, topo):
                         mms([plainly(x, ("idn", 0, 128), ("big", X0 + a, X0 + b), True, True)])
                         now[0] = name
                     vtt(o, x, y, ALU.subtract if sg else ALU.add)
-                elif q == "v":
-                    vgt(o, rg(win, 0, W), off, rg(mine, a, b), ALU.subtract if (sg == 1) != last else ALU.add)
                 else:
-                    pick(q, o, rg(win, 0, W), off)
-                    dma("g", A(o), T.big[:, X0 + a:X0 + b], [("big", X0 + a, X0 + b), o], [o], accum_op=ALU.add)
+                    vgt(o, rg(came, 0, W), off, rg(mine, a, b), ALU.subtract if sg else ALU.add)
             for _, a, b in each("ab"[sg], lo, hi):
                 act(("ab%d" % sg, a, b), ("big", at + a, at + b), AF.Abs)
             for p in gp:
@@ -375,19 +378,21 @@ def rank_program(g, core, T, topo):
                 vtt((fz, c0, c1), lens(gp, sg), ("cc", 224 * sg + c0, 224 * sg + c1), ALU.min, out)
 
         def shorten():
-            for L, z in ((("la", 0, 160), ("zz", 0, 160)), (("lb", 0, 256), ("zz", 160, 416)), (("tw", 32, 64), ("zz", 416, 448))):
+            for L, z in ((("la", 0, 192), ("zz", 0, 192)), (("lb", 0, 256), ("zz", 192, 448))):
                 step("Z")
                 vts(z, L, 0.0, HUGE, ALU.is_equal, ALU.mult)
                 step("M")
                 vtt(L, L, z, ALU.max)
             step("m")
-            for p, sg, n in ((3, 0, 96), (1, 0, 128), (0, 1, 64), (1, 1, 128), (3, 1, 32)):
+            for p, sg, n in ((3, 0, 96), (1, 0, 128), (3, 1, 96), (1, 1, 128)):
                 (bank, c), o = LENS[r][p, sg], ("old", OLD[p], OLD[p] + n)
                 vtt(o, (bank, c, c + n), o, ALU.min)
 
         def begin(gp):
             step("b%d" % gp[0])
             mms([row(region(0, *cols(*gp)), ("c16b",) + cols(*gp), True), plainly(region(2, *cols(*gp)), ("idn", 0, 128), ("yf",) + cols(*gp), False, False)])
+            if last and turning(gp[0]):
+                mms([row(region(1, *cols(*gp)), ("one", 0, 8 * stride(gp[0])), False)])
 
         def flags(p, sg, out, tile, stop):
             H, fz = 16 // stride(p), ("fq%d" if p == 3 else "fz%d") % sg
@@ -395,7 +400,7 @@ def rank_program(g, core, T, topo):
             for h in range(H):
                 rs = (tile[0], tile[1] + 128 // H * h, tile[1] + 128 // H * h + out[2] - out[1])
                 lap = T[fz][:, 3 - h:35 - h, :] if H == 4 else T[fz][:, 1 - h + 16 * p:17 - h + 16 * p, :]
-                calls.append((out, A(out), (fz,) + cols(p), lap, rs, A(rs), (out[:2], sg, h) == (("ob", 64), 0, 0), stop and h == H - 1))
+                calls.append((out, A(out), (fz,) + cols(p), lap, rs, A(rs), False, stop and h == H - 1))
             mms(calls)
 
         def turn(name, gp, whats, sgs=(0, 1), stop=True):
@@ -412,7 +417,20 @@ def rank_program(g, core, T, topo):
             vts(("xl",) + cols(*gp), region(0, *cols(*gp)), float(X0 - win[1]), ("col", 0, 1), ALU.add, ALU.add)
             for q, a, b in each("s", lo, hi):
                 pick(q, rg(new, a, b), win, ("xl", a // 16, b // 16))
-                if last:
+                if last and KEPT[0] <= a and b <= KEPT[1]:
+                    dma("s", T.yx[:, a:b], A(rg(new, a, b)), [rg(new, a, b)], [])
+            if gp == (0,) and not last:
+                dma("s", A(("cp", lo, hi)), A(rg(new, lo, hi)), [rg(new, lo, hi)], [("cp", lo, hi)])
+            if last and turning(gp[0]):
+                c0, c1 = turning(gp[0])
+                step("S%d" % gp[0])
+                vtt(("turned", c0, c1), region(1, c0, c1), ("turned", c0, c1), ALU.mult)
+                for _, a, b in each("F", 16 * c0, 16 * c1):
+                    name, o, c = now[0], (("pw", "tb")[a // G % 2], 0, G), ("turned", a // 16, b // 16)
+                    step("W%d-%d" % (a // 64, b // 64))
+                    mms([(o, T[o[0]][:, i:G:16], ("fan", 128 * i, 128 * i + 128), T.fan[:, 128 * i:128 * i + 128], c, A(c), i == 0, i == 15) for i in range(16)])
+                    now[0] = name
+                    vtt(rg(new, a, b), rg(new, a, b), o, ALU.mult)
                     dma("s", T.yx[:, a:b], A(rg(new, a, b)), [rg(new, a, b)], [])
 
         def places(lo, hi):
@@ -421,7 +439,7 @@ def rank_program(g, core, T, topo):
 
         def follow():
             for q, a, b in each("g", 0, V):
-                pick(q, ("tab", t1 + a, t1 + b), ("tab", tw0, tw1), ("pl", a // 16, b // 16), [("row", 0, 2)] * (r == 0))
+                pick(q, ("tab", t1 + a, t1 + b), ("tab", tw0, tw1), ("pl", a // 16, b // 16), [("row", TA, TB)] * (r == 0))
 
         def scan(c0, c1):
             step("C%d" % (c0 // 64))
@@ -435,6 +453,9 @@ def rank_program(g, core, T, topo):
             form(gp, 1)
             begin(gp)
             decide(gp)
+            if last and turning(gp[0]):
+                step("T%d" % gp[0])
+                flags(gp[0], 1, region(1, *cols(*gp)), scaled(gp[0] // 3, -2), False)
             turn("T%d" % gp[0], gp, (0, 2) if last else (1, 0, 2))
             select(gp)
 
@@ -456,16 +477,12 @@ def rank_program(g, core, T, topo):
         mms([row(("pw", 224, 256), ("one", 0, 32), True)])
         for sg in range(2):
             flags(0, sg, ("pw", 224, 256), scaled(0, -1), False)
-        form((1, 2), 0)
-        form((1, 2), 1)
-        decide((1, 2))
-        turn("R1", (1, 2), (1,))
-        scan(64, 192)
-        for sg in range(2):
-            form((3,), sg)
-            decide((3,), (sg,))
-            turn("R3%d" % sg, (3,), (1,), (sg,), sg == 1)
-        scan(192, 256)
+        for gp in GROUPS[r][1:]:
+            form(gp, 0)
+            form(gp, 1)
+            decide(gp)
+            turn("R%d" % gp[0], gp, (1,), stop=gp == (3,))
+        scan(64, 256)
         for gp in GROUPS[r][1:]:
             begin(gp)
             turn("T%d" % gp[0], gp, (0, 2))
@@ -502,14 +519,21 @@ def rank_program(g, core, T, topo):
         for h in range(2):
             pick(who("gs%d" % h), (gs[0], 256 * h, 256 * h + 256), rg(new, 0, V), ("l3", 16 * h, 16 * h + 16))
         send(rg(new, V, W), gs, "x%d" % (r + 1))
+        dma("s", A(("cp", KEPT[1], V)), A(rg(new, KEPT[1], V)), [rg(new, KEPT[1], V)], [("cp", KEPT[1], V), gs])
         q = who("hs")
         mms([onto(("xa", 0, G), z, i, ("cm%d" % (n + 1), 0, G), n == 0, n == 2) for n, (z, i) in enumerate((("zf", 0), ("z16", 1), ("z1", 1)))])
         copy(q, hs, ("xa", 0, G))
         send(("tab", t1 + V, t1 + W), hs, "h%d" % (r + 1))
-        for q, a, b in each("n", 0, W):
-            copy(q, rg(nneg, a, b), rg(new, a, b), -1.0)
+        q = who("U")
+        mms([row(("xb", 0, 128), ("one", 0, 128), True), row(("xb", 128, 224), ("one", 0, 96), False)])
+        for p in (0, 2, 3):
+            flags(p, 1, ("xb",) + cols(p), scaled(p // 3, -2), p == 3)
+        if r == 0:
+            copy(q, ("turned", 0, 224), ("xb", 0, 224))
+        else:
+            vtt(("turned", 0, 224), ("xb", 0, 224), ("turned", 0, 224), ALU.mult)
         shorten()
-        for bank, lo, hi in (("pw", 0, 2048), ("ob", 2048, V)):
+        for bank, lo, hi in (("pw", 0, V),):
             for _, a, b in each("Y", lo, hi):
                 wrap((bank, a // 16, b // 16), "zw", ("tab", t1 + a, t1 + b))
                 step("y%d-%d" % (a // 64, b // 64))

@@ -3,57 +3,59 @@ from concourse.mybir import AluOpType as ALU, ActivationFunctionType as AF
 V, G, W = 3584, 512, 4096
 PS = [(0, 1024), (1024, 2048), (2048, 3072), (3072, 3584)]
 GROUPS = [[(0,), (1, 2), (3,)]] * 2 + [[(0,), (1,), (2,), (3,)]]
-LENS = [{(3, 0): ("la", 0), (0, 0): ("la", 32), (3, 1): ("la", 96), (0, 1): ("la", 128),
-         (1, 0): ("lb", 0), (2, 0): ("lb", 64), (1, 1): ("lb", 128), (2, 1): ("lb", 192)}] * 2 + [
-        {(p, sg): (("la", "lb")[p % 2], 128 * (p // 2) + 64 * sg) for p in range(4) for sg in range(2)}]
-OLD = [32, 96, 160, 0]
-XC, XB, SD, XA = 0, 4096, 8192, 15360
-BIGN = XA + W
-TA, TI, TB, TC = 0, W, 2 * W, 3 * W
+LENS = [{0: ("la", 0), 3: ("la", 64), 1: ("lb", 0), 2: ("lb", 64)}] * 2 + [
+        {p: (("la", "lb")[p % 2], 64 * (p // 2)) for p in range(4)}]
+OLD = [0, 96, 160, 64]
+XC, XB, XA, SD = 0, W, 2 * W, 2 * W + V
+TC, TB, TA, TI, TD = 0, W, 2 * W, 3 * W, 4 * W
 HUGE = float(2 ** 25)
 NT = 32
-
-SEARCH = {"v": "P0-16 D1 D3 C1 X1 cm1 t2 g0-3 l1 P16-48 cm2 X3 P48-56 Z l2 cm3 M l3 gs0 g16-35 y0-16 m y16-32 ",
-          "a": "s0-16 s16-48 t3 s48-56 g3-16 gs1 g35-56 hs ",
-          "t": "sB2 sA3 sB3 R1 T1 R3 E1 t2 l1 t3 b3 T3 l2a l2 l3a l3 Y0-16 hs U Y16-32 Y32-56"}
 KEPT = (1024, 2560)
-PHASE = {"v": "A0-16 y32-56' B0-16 A16-24 B16-24 A24-32 B24-32 A32-40 B32-40 D0 A40-48 X0 B40-44 B44-48 C0 A48-56 B48-53 B53-56 ",
-         "a": "H16-24 H24-32 a0-16 H32-40 f0-56' b0-16 old' a16-32 b16-32 a32-40 b32-40 a40-48 b40-44 b44-48 a48-56 b48-53 b53-56 ",
-         "t": "x16-24 x24-32 x32-40 sA0 sB0 b0 sA1 T0 oth sB1 b1 sA2 E0 "}
-PLAN = [
-    {"v": PHASE["v"] + SEARCH["v"], "a": PHASE["a"] + SEARCH["a"] + "U", "t": "o0' o1' o2' o3' " + PHASE["t"] + SEARCH["t"]},
-    {"v": PHASE["v"] + SEARCH["v"] + "U", "a": PHASE["a"] + SEARCH["a"], "t": PHASE["t"] + SEARCH["t"]},
-    {"v": "A0-16 y32-56' B0-16 A16-24 B16-24 A24-32 B24-32 A32-40 B32-40 D0 A40-48 X0 S0 P0-16 D1 B40-48 A48-56 X1 P16-32 B48-56 "
-          "F0-8 D2 F8-16 X2 S2 P32-48 D3 g0-7 X3 S3 P48-56 s48-56 F40-48 F48-56 g21-28 g42-52 yc",
-     "a": "H16-24 H24-32 a0-16 H32-40 b0-16 f0-56' a16-32 b16-32 a32-40 b32-40 a40-48 s0-16 b40-48 a48-56 b48-56 "
-          "s16-32 s40-48 s32-40 g7-21 g28-42 g52-56 yc",
-     "t": "x16-24 x24-32 x32-40 sA0 sB0 b0 sA1 T0 sB1 b1 T1 sA2 W0-8 b2 sB2 sA3 W8-16 T2 b3 sB3 T3 W40-48 W48-56 yc"}]
+EARLY = []
+
+ROUND = {
+    "v": "A0-16 y32-56' old' B0-16 A16-24 A24-32 B16-24 B24-32 A32-40 c0 B32-40 D0 A40-48 B40-48 A48-56 B48-56 X0 "
+         "c1 D1 s14-16 c3 D3 C0 X1 C3 g0-5 cm1 Z0 t2 l1 cm2 M0 X3 Z1 l2 cm3 U M1 l3 j0-4 g16-34 y0-16 m0 m1 y16-32",
+    "a": "H16-24 H24-32 a0-16 H32-40 b0-16 a16-32 f0-56' b16-32 a32-40 b32-40 a40-48 b40-48 a48-56 b48-56 "
+         "s0-14 s16-48 s48-56 g5-16 j4-8 U g34-56 hs",
+    "t": "x16-24 Y32-56' x24-32 sA0 x32-40 sB0 b0 sA1 b1 R0 T0 oth sB1 sA2 sB2 sA3 sB3 "
+         "R1 T1 R3 E0 E3 t2 l1 b3 l2a T3 l2 U l3a l3 hs Y0-16 Y16-32"}
+LAST = {
+    "v": "A0-16 y32-56' B0-16 A16-24 A40-48 A24-32 B16-24 B24-32 A32-40 c0 B32-40 D0 B40-48 X0 S0 c1 B48-56 D1 A48-56 "
+         "g12-16 X1 F0-8 c2 F8-16 D2 g25-32 S2 X2 c3 g22-25 D3 g0-12 S3 X3 F40-48 s48-56 g41-47 F48-56 yc",
+    "a": "H16-24 H24-32 a0-16 f0-56' H32-40 b0-16 a16-32 b16-32 a32-48 b32-48 s0-16 a48-56 b48-56 "
+         "s16-32 s40-48 g16-22 s32-40 g32-41 g47-56 out",
+    "t": "Y32-56' x16-24 x24-32 x32-40 sA0 sB0 b0 sA1 T0 sB1 sA2 W0-8 b1 T1 W8-16 sB2 b2 sA3 sB3 T2 b3 W40-48 T3 W48-56 u0-16",
+    "s": "0-8 8-16 16-32 32-40 40-48 48-56"}
+PLAN = [dict(ROUND, v=ROUND["v"].replace(" U", ""), t="o0' o1' o2' o3' " + ROUND["t"]),
+        dict(ROUND, a=ROUND["a"].replace(" U", "")), LAST]
 
 F32, BF, I32, U16 = "float32", "bfloat16", "int32", "uint16"
 SCRATCH = {
-    "xin": ("sbuf", [128, W], I32), "big": ("sbuf", [128, BIGN], F32), "cp": ("sbuf", [128, V], F32),
-    "ab0": ("sbuf", [128, V], F32), "ab1": ("sbuf", [128, V], F32), "tab": ("sbuf", [128, 4 * W], BF),
-    "yy": ("sbuf", [128, 4 * G], F32), "fan": ("sbuf", [128, 16 * 128], BF), "hib": ("sbuf", [128, 256], BF),
-    "turned": ("sbuf", [128, 224], BF), "ptb": ("sbuf", [128, 224], I32), "pti": ("sbuf", [128, 448], I32), "ptd": ("sbuf", [128, 448], BF),
-    "yl": ("sbuf", [128, 224], U16), "xl": ("sbuf", [128, 224], U16), "pl": ("sbuf", [128, 224], U16), "yf": ("sbuf", [128, 224], F32),
+    "xin": ("sbuf", [128, W], I32), "big": ("sbuf", [128, SD + 2 * V], F32), "cp": ("sbuf", [128, V], F32),
+    "ab0": ("sbuf", [128, V], F32), "ab1": ("sbuf", [128, V], F32), "tab": ("sbuf", [128, TD + V], BF),
+    "yy": ("sbuf", [128, 3 * G], F32), "fan": ("sbuf", [128, 16 * 128], BF), "hib": ("sbuf", [128, 256], BF),
+    "turned": ("sbuf", [128, 224], BF), "pin": ("sbuf", [128, 2, 112], I32), "pfl": ("sbuf", [128, 7, 32], F32),
+    "pti": ("sbuf", [128, 448], I32), "ptd": ("sbuf", [128, 448], BF),
+    "yl": ("sbuf", [128, 224], U16), "xp": ("sbuf", [128, 2, 256], U16), "yf": ("sbuf", [128, 224], F32),
     "l1": ("sbuf", [128, 32], U16), "l2": ("sbuf", [128, 32], U16), "l3": ("sbuf", [128, 32], U16),
-    "c16b": ("sbuf", [128, 224], BF), "ycs": ("sbuf", [128, 224], F32),
-    "old": ("sbuf", [128, 224], F32), "cc": ("sbuf", [128, 448], F32), "zz": ("sbuf", [128, 448], F32),
-    "fz0": ("sbuf", [128, 50, 8], BF), "fz1": ("sbuf", [128, 50, 8], BF), "fq0": ("sbuf", [128, 36, 4], BF), "fq1": ("sbuf", [128, 36, 4], BF),
-    "rr": ("sbuf", [128, 264], BF), "t2": ("sbuf", [128, 16], F32), "t3": ("sbuf", [128, 256], F32),
+    "c16b": ("sbuf", [128, 224], BF), "lane": ("sbuf", [128, 128], BF), "ycs": ("sbuf", [128, 224], F32),
+    "old": ("sbuf", [128, 2, 256], F32), "cc": ("sbuf", [128, 2, 256], F32), "zz": ("sbuf", [128, 2, 256], F32),
+    "fz": ("sbuf", [128, 2, 50, 8], BF), "fq": ("sbuf", [128, 2, 36, 4], BF),
+    "rr": ("sbuf", [128, 264], BF), "t23": ("sbuf", [128, 272], F32),
     "cm1": ("sbuf", [128, G], BF), "cm2": ("sbuf", [128, G], BF), "cm3": ("sbuf", [128, G], BF),
     "gs0": ("sbuf", [128, G], F32), "gs1": ("sbuf", [128, G], F32), "hs0": ("sbuf", [128, G], BF), "hs1": ("sbuf", [128, G], BF),
     "kk": ("sbuf", [128, G], F32), "kb": ("sbuf", [128, G], BF), "pc": ("sbuf", [128, 8], I32), "col": ("sbuf", [128, 8], F32),
-    "ur": ("sbuf", [128, 144], F32), "uu": ("sbuf", [128, 144], F32), "b1": ("sbuf", [128, 128], BF), "b2": ("sbuf", [128, 128], BF),
     "blk": ("sbuf", [128, 128], BF), "tri": ("sbuf", [128, 128], BF), "upp": ("sbuf", [128, 128], BF), "idn": ("sbuf", [128, 128], F32),
-    "z1": ("sbuf", [128, 144], BF), "z16": ("sbuf", [128, 144], BF), "zf": ("sbuf", [128, 144], BF), "zw": ("sbuf", [128, 144], BF),
-    "gind": ("sbuf", [128, 8], F32), "one": ("sbuf", [128, 192], BF), "zer": ("sbuf", [128, 128], BF),
+    "z0": ("sbuf", [128, 144], BF), "z1": ("sbuf", [128, 144], BF), "z16": ("sbuf", [128, 144], BF), "zf": ("sbuf", [128, 144], BF),
+    "zw": ("sbuf", [128, 144], BF), "gind": ("sbuf", [128, 8], F32), "one": ("sbuf", [128, 256], BF), "zer": ("sbuf", [128, 128], BF),
     "ssc": ("sbuf", [128, NT * 128], BF),
-    "la": ("psum", [128, 512], F32), "lb": ("psum", [128, 512], F32),
+    "la": ("psum", [128, 2, 256], F32), "lb": ("psum", [128, 2, 256], F32),
     "xa": ("psum", [128, 512], F32), "xb": ("psum", [128, 512], F32), "pw": ("psum", [128, 512], F32),
     "tb": ("psum", [128, 512], F32), "tw": ("psum", [128, 512], F32), "ob": ("psum", [128, 512], F32),
 }
 PSUM = [k for k, v in SCRATCH.items() if v[0] == "psum"]
+HALVES = [k for k, v in SCRATCH.items() if v[1][1:] == [2, 256]]
 WRITES = ["x0", "x1", "x2", "h1", "h2"]
 SEMAPHORES = ["cv", "ca", "ct", "cg"] + ["in" + w for w in WRITES] + ["out" + w for w in WRITES] + ["dm%d" % k for k in range(40)]
 
@@ -130,22 +132,29 @@ def rank_program(g, core, T, topo):
         job("t", [lambda c=c: g.tensor.matmul(c[1], c[3], c[5], c[6], c[7]) for c in calls],
             sorted({c[2] for c in calls} | {c[4] for c in calls}), sorted({c[0] for c in calls}))
 
-    def A(r):
-        return T[r[0]][:, r[1]:r[2]]
+    def A(r, step=1):
+        if len(r) == 4:
+            return T[r[0]][:, :, r[1]:r[2]]
+        if r[0] in HALVES:
+            return T[r[0]][:, r[1] // 256, r[1] % 256:r[2] - r[1] // 256 * 256:step]
+        return T[r[0]][:, r[1]:r[2]:step]
+
+    def parts(*rs):
+        return [(r[0], r[1] + 256 * h, r[2] + 256 * h) for r in rs for h in range(len(r) - 2)]
 
     def gat(win, off):
-        return T[win[0]][:, win[1]:win[2]].indirect(T[off[0]][:, off[1]:off[2]])
+        return A(win).indirect(A(off))
 
     def vcopy(o, i):
-        op("v", lambda: g.vector.tensor_copy(A(o), A(i)), [i], [o])
+        op("v", lambda: g.vector.tensor_copy(A(o), A(i)), parts(i), parts(o))
 
     def vts(o, i, s1, s2, *ops):
         cols = [s for s in (s1, s2) if isinstance(s, tuple)]
         args = [A(s) if isinstance(s, tuple) else s for s in (s1, s2)]
-        op("v", lambda: g.vector.tensor_scalar(A(o), A(i), args[0], args[1], *ops), [i] + cols, [o])
+        op("v", lambda: g.vector.tensor_scalar(A(o), A(i), args[0], args[1], *ops), parts(i) + cols, parts(o))
 
     def vtt(o, i0, i1, alu, oap=None):
-        op("v", lambda: g.vector.tensor_tensor(A(o) if oap is None else oap, A(i0), A(i1), alu), [i0, i1], [o])
+        op("v", lambda: g.vector.tensor_tensor(A(o) if oap is None else oap, A(i0), A(i1), alu), parts(i0, i1), parts(o))
 
     def vset(o, c, lo=None, hi=None):
         op("v", lambda: g.vector.memset(T[o][:] if lo is None else T[o][:, lo:hi], c), [], [(o, lo or 0, hi or 1 << 20)])
@@ -153,13 +162,13 @@ def rank_program(g, core, T, topo):
     def act(o, i, fn, **kw):
         cols = [s for s in kw.values() if isinstance(s, tuple)]
         args = {k: A(s) if isinstance(s, tuple) else s for k, s in kw.items()}
-        op("a", lambda: g.scalar.activation(A(o), A(i), fn, **args), [i] + cols, [o])
+        op("a", lambda: g.scalar.activation(A(o), A(i), fn, **args), parts(i) + cols, parts(o))
 
-    def copy(q, o, i, scale=1.0):
+    def copy(q, o, i):
         if q == "v":
-            vts(o, i, scale, None, ALU.mult)
+            vcopy(o, i)
         else:
-            act(o, i, AF.Copy, scale=scale)
+            act(o, i, AF.Copy)
 
     def pick(q, o, win, off, more=()):
         if q == "v":
@@ -173,11 +182,14 @@ def rank_program(g, core, T, topo):
     def plainly(o, l, r, st, sp):
         return (o, A(o), l, A(l), r, A(r), st, sp)
 
-    def row(o, r, st):
-        return (o, A(o), ("one", 0, 128), T.one[0:1, 0:128], r, T[r[0]][0:1, r[1]:r[2]], st, False)
+    def row(o, r, st, by="one"):
+        return (o, A(o), (by, 0, 128), T[by][0:1, 0:128], r, T[r[0]][0:1, r[1]:r[2]], st, False)
 
     def iota(o, pattern, base, mult):
         op("g", lambda: g.iota(A(o), pattern, base, mult, allow_small_or_imprecise_dtypes=True), [], [o])
+
+    def where(o, i, pattern, cmp, fill, base, mult):
+        op("g", lambda: g.affine_select(A(o), A(i), pattern, cmp, float(fill), base, mult), [i], [o])
 
     def onto(o, z, i, src, st, sp, step=1):
         return (o, A(o), (z, 0, 144), T[z][:, 15 - i:143 - i], src, T[src[0]][:, src[1] + (i if step > 1 else 0):src[2]:step], st, sp)
@@ -190,7 +202,7 @@ def rank_program(g, core, T, topo):
 
     def sums(ab, p, bank, c):
         (lo, hi), st = PS[p], stride(p)
-        mms([((bank, c, c + 8 * st), T[bank][:, c + m:c + 8 * st:st], (ab, lo, hi), T[ab][:, lo + m:hi:st], ("gind", 0, 8), T.gind[:, :], True, True)
+        mms([((bank, c, c + 8 * st), A((bank, c + m, c + 8 * st), st), (ab, lo, hi), T[ab][:, lo + m:hi:st], ("gind", 0, 8), T.gind[:, :], True, True)
              for m in range(st)])
 
     def reach(r, p):
@@ -199,19 +211,19 @@ def rank_program(g, core, T, topo):
 
     def place(r, p, sg):
         lo, hi = reach(r, p)
-        return (XA - 2 * hi if r == 0 else SD + 2 * lo) + sg * (hi - lo) - lo
+        return SD + lo + sg * (hi - lo)
 
     tiles = {}
     SHAPES = [[[-1, 2], [-2, 64]], [[-1, 4], [-4, 32]]]
 
     def scaled(kind, a):
         if (kind, a) not in tiles:
-            o = tiles[kind, a] = ("ssc", 128 * len(tiles), 128 * len(tiles) + 128)
-            op("g", lambda: g.affine_select(A(o), T.zer[:, :], SHAPES[kind], ALU.not_equal, float(a), 0, 1), [("zer", 0, 128)], [o])
+            tiles[kind, a] = ("ssc", 128 * len(tiles), 128 * len(tiles) + 128)
+            where(tiles[kind, a], ("zer", 0, 128), SHAPES[kind], ALU.not_equal, a, 0, 1)
         return tiles[kind, a]
 
     def weight(r, p, sg, what):
-        return scaled(p // 3, (place(r, p, sg) - (XA, XB, XC)[r], 1, (W, -W, -2 * W)[r])[what])
+        return scaled(p // 3, (place(r, p, sg) - (XA, XB, XC)[r], 1, TI - (TA, TB, TC)[r])[what])
 
     def weights(r):
         for p in range(4):
@@ -220,96 +232,96 @@ def rank_program(g, core, T, topo):
                     weight(r, p, sg, what)
 
     dma("a", T.xin[:, 0:G], T.x[:, 0:G], [], [("xin", 0, G)])
-    dma("s", T.ptb[:, :], T.pt[:, :], [], [("ptb", 0, 224)])
-    dma("s", T.xin[:, G:2048], T.x[:, G:2048], [], [("xin", G, 2048)])
-    op("g", lambda: g.iota(T.pc[:, 0:1], [[0, 1]], 0, 1), [], [("pc", 0, 1)])
-    iota(("ur", 0, 144), [[1, 144]], -15, -1)
-    iota(("c16b", 0, 224), [[16, 224]], 0, 0)
-    vset("tab", 0.0, TA, TA + V)
-    vts(("pc", 4, 5), ("pc", 0, 1), 15, None, ALU.bitwise_and)
-    vset("zer", 0.0)
-    vcopy(("col", 0, 1), ("pc", 4, 5))
-    vset("one", 1.0)
-    vts(("uu", 0, 144), ("ur", 0, 144), ("col", 0, 1), None, ALU.add)
-    vts(("col", 1, 2), ("col", 0, 1), 1.0, None, ALU.is_le)
-    vts(("pti", 0, 224), ("ptb", 0, 224), 0xF00, None, ALU.bitwise_and)
-    vts(("pti", 224, 448), ("ptb", 0, 224), 0xFF, None, ALU.bitwise_and)
-    vts(("zw", 0, 144), ("uu", 0, 144), 0.0, ("col", 1, 2), ALU.is_equal, ALU.mult)
-    vcopy(("ptd", 0, 448), ("pti", 0, 448))
-
-    def rows(at, n, k, src, rd):
-        dma("s", T.tab[k:128:16, at:at + n], src, [rd, ("tab", at, at + n)], [("row", at + k, at + k + 1)])
     for k in range(2):
-        rows(TA, V, k, T.ptd[:, 224 * k:224 * k + 224], ("ptd", 224 * k, 224 * k + 224))
+        dma("s", T.pin[:, k, :], T.pt[k:8:2, :], [], [("pin", 112 * k, 112 * k + 112)])
+    dma("s", T.xin[:, G:2048], T.x[:, G:2048], [], [("xin", G, 2048)])
+    vset("one", 1.0)
+    vset("zer", 0.0)
+    op("g", lambda: g.iota(T.pc[:, 0:1], [[0, 1]], 0, 256), [], [("pc", 0, 1)])
+    where(("z0", 0, 144), ("one", 0, 144), [[-16, 9], [1000, 16]], ALU.is_ge, 0, -15000, 1)
+    where(("z1", 0, 144), ("z0", 0, 144), [[16, 9], [0, 16]], ALU.is_ge, 0, 15, -1)
+    vset("tab", 0.0, TA, TA + V)
+    vts(("pc", 4, 5), ("pc", 0, 1), 0xF00, None, ALU.bitwise_and)
+    for k in range(2):
+        op("v", lambda k=k: g.vector.tensor_copy(T.pfl[:, :, 16 * k:16 * k + 16], T.pin[:, k, :]), [("pin", 112 * k, 112 * k + 112)], [("pfl", k, k + 1)])
+    for e in range(7):
+        op("v", lambda e=e: g.vector.transpose(T.yf[:, e:224:7], T.pfl[:, e, :]), [("pfl", 0, 2)], [("yf", e, e + 1)])
+    vcopy(("yl", 0, 224), ("yf", 0, 224))
+    for k, bits in enumerate((0xF00, 0xFF)):
+        op("v", lambda k=k, bits=bits: g.vector.tensor_scalar(T.pti[:, 224 * k:224 * k + 224], T.pin[:, :, :], bits, None, ALU.bitwise_and),
+           [("pin", 0, 224)], [("pti", 224 * k, 224 * k + 224)])
+
+    def rows(at, n, k, src, rd, step=16):
+        dma("s", T.tab[k:128:step, at:at + n], src, [rd, ("tab", at, at + n)], [("row", at + k, at + k + 1)])
     for lo, hi in PS[2:]:
-        dma("s", T.xin[:, lo:hi], T.x[:, lo:hi], [], [("xin", lo, hi)])
+        dma("s", T.xin[:, lo:hi], T.x[:, lo:hi], [("pfl", 0, 2)], [("xin", lo, hi)])
     send(("xin", V, W), ("xin", 0, G), "x0")
-    iota(("kb", 0, G), [[1, G]], -256, 0)
 
     def arrive(lo, hi, q):
         act(("ab0", lo, hi), ("xin", lo, hi), AF.Abs)
         copy(q, ("big", XA + lo, XA + hi), ("xin", lo, hi))
 
-    def first_lists(c0, c1, bank):
-        wrap((bank, c0, c1), "zw", ("tab", TA + 16 * c0, TA + 16 * c1))
-        jobs[-1]["rd"].append(("row", TA, TA + 2))
-        vcopy(("yl", c0, c1), (bank, c0, c1))
-        vcopy(("yf", c0, c1), (bank, c0, c1))
-
-    op("v", lambda: g.vector.tensor_scalar(T.gind[:, :], T.uu[:, 15:143:16], 0.0, None, ALU.is_equal), [("uu", 0, 144)], [("gind", 0, 8)])
     arrive(0, G, "a")
-    vts(("idn", 0, 128), ("ur", 15, 143), 0.0, None, ALU.is_equal)
-    vts(("b1", 0, 128), ("uu", 15, 143), 0.0, None, ALU.is_ge)
-    vts(("b2", 0, 128), ("uu", 15, 143), 15.0, None, ALU.is_le)
-    vts(("col", 2, 3), ("col", 0, 1), 13.0, -float(V), ALU.is_equal, ALU.mult)
-    vtt(("blk", 0, 128), ("b1", 0, 128), ("b2", 0, 128), ALU.mult)
-    vts(("col", 5, 6), ("col", 2, 3), 256.0, None, ALU.add)
-    vts(("z1", 0, 144), ("uu", 0, 144), 0.0, None, ALU.is_equal)
-    vts(("z16", 0, 144), ("uu", 0, 144), 0.0, 16.0, ALU.is_equal, ALU.mult)
-    vts(("zf", 0, 144), ("uu", 0, 144), 0.0, ("col", 5, 6), ALU.is_equal, ALU.mult)
-    vset("hib", 256.0)
+    op("a", lambda: g.scalar.activation(T.gind[:, :], T.z1[:, 15:143:16], AF.Copy), [("z1", 0, 144)], [("gind", 0, 8)])
+    act(("z16", 0, 144), ("z1", 0, 144), AF.Copy, scale=16.0)
+    act(("zf", 0, 144), ("z1", 0, 144), AF.Copy, scale=256.0)
+    act(("col", 0, 1), ("pc", 4, 5), AF.Copy)
+    act(("hib", 0, 256), ("one", 0, 256), AF.Copy, scale=("col", 0, 1))
     vset("rr", 0.0, 0, 8)
-    vts(("hib", 0, 256), ("hib", 0, 256), ("col", 0, 1), None, ALU.mult)
-    for f in ("fz0", "fz1", "fq0", "fq1"):
-        vset(f, 0.0)
-    weights(0)
+    vset("fz", 0.0)
+    vset("fq", 0.0)
+
+    def late(lo, hi):
+        where(("big", XA + lo, XA + hi), ("xin", lo, hi), [[0, hi - lo]], ALU.is_ge, 0, 0, 0)
+    where(("idn", 0, 128), ("zer", 0, 128), [[-1, 128]], ALU.not_equal, 1, 0, 1)
+    iota(("c16b", 0, 224), [[16, 224]], 0, 0)
+    iota(("lane", 0, 128), [[0, 8], [1, 16]], 0, 0)
+    late(2048, 2560)
+    for sg, what in ((0, 0), (1, 0), (0, 2)):
+        weight(0, 0, sg, what)
+    late(2560, 3072)
+    late(3072, V)
+    iota(("kb", 0, G), [[1, G]], -256, 0)
+    scaled(0, 1)
     scaled(0, -1)
+    weights(0)
+    where(("blk", 0, 128), ("one", 0, 128), [[-16, 8], [0, 16]], ALU.is_ge, 0, 0, 1)
     iota(("kk", 0, G), [[1, G]], 0, 0)
-    op("g", lambda: g.affine_select(T.tri[:, :], T.blk[:, :], [[1, 128]], ALU.is_ge, 0.0, 0, -1), [("blk", 0, 128)], [("tri", 0, 128)])
-    op("g", lambda: g.affine_select(T.upp[:, :], T.blk[:, :], [[-1, 128]], ALU.is_gt, 0.0, 0, 1), [("blk", 0, 128)], [("upp", 0, 128)])
+    where(("blk", 0, 128), ("blk", 0, 128), [[16, 8], [0, 16]], ALU.is_ge, 0, 15, -1)
+    where(("zf", 0, 144), ("zf", 0, 144), [[-16, 9], [1000, 16]], ALU.not_equal, 256 - V, -15013, 1)
+    where(("tri", 0, 128), ("blk", 0, 128), [[1, 128]], ALU.is_ge, 0, 0, -1)
+    where(("upp", 0, 128), ("blk", 0, 128), [[-1, 128]], ALU.is_gt, 0, 0, 1)
+    where(("zw", 0, 144), ("z0", 0, 144), [[16, 9], [0, 16]], ALU.is_ge, 0, 1, -1)
     scaled(0, -2)
     scaled(1, -2)
-    weights(1)
-    weights(2)
-    for i in range(16):
-        op("g", lambda i=i: g.affine_select(T.fan[:, 128 * i:128 * i + 128], T.zer[:, :], [[-16, 8], [0, 16]], ALU.not_equal, 1.0, -i, 1),
-           [("zer", 0, 128)], [("fan", 128 * i, 128 * i + 128)])
     arrive(G, 2048, "v")
-    first_lists(0, 128, "pw")
-    first_lists(128, 224, "tw")
+    act(("ptd", 0, 448), ("pti", 0, 448), AF.Copy)
+    for p in (2, 3):
+        act(("ab0",) + PS[p], ("xin",) + PS[p], AF.Abs)
     for p in range(4):
-        if p >= 2:
-            arrive(*PS[p], "va"[p - 2])
         now[0] = (-1, "o%d" % p)
         sums("ab0", p, "lb", 256 + OLD[p])
-        now[0] = None
+    now[0] = None
     for at, n in ((0, V), (V, G)):
-        dma("s", T.tab[:, TI + at:TI + at + n], T.tab[:, TA:TA + n], [("tab", TA, TA + n), ("row", TA, TA + 2), ("xin", V, W)], [("tab", TI + at, TI + at + n)])
+        dma("s", T.tab[:, TI + at:TI + at + n], T.tab[:, TA:TA + n], [("tab", TA, TA + n), ("row", TA, TA + 32), ("xin", V, W)], [("tab", TI + at, TI + at + n)])
+
+    def twice():
+        dma("s", A(("old", 256, 480)), A(("old", 0, 224)), [("old", 0, 224)], [("old", 256, 480)])
+    now[0] = (-1, "old")
+    copy("v" if now[0] in steps("v") else "a", ("old", 0, 224), ("lb", 256, 480))
+    twice()
+    for k in range(4):
+        rows(TA, V, k // 2 + 16 * (k % 2), T.ptd[:, 112 * k:112 * k + 112], ("ptd", 112 * k, 112 * k + 112), 32)
     rows(TI, W, 0, T.hib[:, :], ("hib", 0, 256))
     rows(TI, W, 1, T.kb[:, 256:G], ("kb", 256, G))
     dma("s", T.tab[:, TA + V:TA + W], T.tab[:, TI:TI + G], [("tab", TI, TI + G), ("row", TI, TI + 2)], [("tab", TA + V, TA + W)])
-    now[0] = (-1, "old")
-    copy("a", ("old", 0, 224), ("lb", 256, 480))
 
     def one_round(r):
         last = r == 2
         X0 = (XA, XB, XC)[r]
         came, mine = (("xin", 0), ("big", XB), ("big", XC))[r], (("big", XA), ("cp", 0), ("cp", 0))[r]
-        new = ("big", (XB, XC, XA)[r])
-        tw0, tw1 = (TA, TI, TI)[r], (TB, TC, TC + W)[r]
-        t0, t1 = (TA, TB, TC)[r], (TB, TC, TA)[r]
-
-        shared = [64 * int(s[1:].split("-")[0]) for r0, s in steps("a") if r0 == r and s[0] == "H"]
+        new = (("big", XB), ("big", XC), ("ab0", 0))[r]
+        t0, t1 = (TA, TB, TC)[r], (TB, TC, TD)[r]
 
         def step(name):
             now[0] = (r, name)
@@ -334,27 +346,26 @@ def rank_program(g, core, T, topo):
             c0 = KEPT[1] // 16 if KEPT[0] // 16 <= c0 < KEPT[1] // 16 else c0
             return (c0, c1) if c0 < c1 else None
 
-        def lens(gp, sg):
-            (bank, c), (c0, c1) = LENS[r][gp[0], sg], cols(*gp)
-            return (bank, c, c + c1 - c0)
+        def lens(gp):
+            (bank, c), n = LENS[r][gp[0]], cols(*gp)[1] - cols(*gp)[0]
+            return (bank, c, c + n, 2), (OLD[gp[0]], OLD[gp[0]] + n, 2)
 
         def region(what, c0, c1):
+            if what == 1 and not last:
+                return ("ob" if c0 >= 192 else "pw", c0, c1)
             n = [k for k, gp in enumerate(GROUPS[r]) if cols(*gp)[0] <= c0][-1]
-            if what == 1 and n and not last:
-                return ("pw", c0, c1)
-            at = 128 * what - cols(*GROUPS[r][n])[0]
+            g0, g1 = cols(*GROUPS[r][n])
+            at = (0, 2, 1)[what] * (g1 - g0) - g0
             return (("xa", "xb")[n % 2], at + c0, at + c1)
 
         def form(gp, sg):
             at, (lo, hi) = place(r, gp[0], sg), reach(r, gp[0])
             for q, a, b in each("AB"[sg], lo, hi):
                 o, off = ("big", at + a, at + b), ("yl", a // 16, b // 16)
-                if a in shared:
-                    k, name = shared.index(a), now[0]
-                    y, x = ("yy", G * k, G * k + G), (("tw", "xb", "ob", "tb")[k], 0, G)
+                if KEPT[0] <= a < KEPT[1]:
+                    y, x = ("yy", a - KEPT[0], b - KEPT[0]), (("tw", "ob", "xb")[(a - KEPT[0]) // G], 0, G)
                     if not sg:
-                        step("H%d-%d" % (a // 64, b // 64))
-                        pick("a", y, rg(came, 0, W), off)
+                        name = now[0]
                         step("x%d-%d" % (a // 64, b // 64))
                         mms([plainly(x, ("idn", 0, 128), ("big", X0 + a, X0 + b), True, True)])
                         now[0] = name
@@ -365,81 +376,90 @@ def rank_program(g, core, T, topo):
                 act(("ab%d" % sg, a, b), ("big", at + a, at + b), AF.Abs)
             for p in gp:
                 step("s%s%d" % ("AB"[sg], p))
-                sums("ab%d" % sg, p, *LENS[r][p, sg])
+                sums("ab%d" % sg, p, LENS[r][p][0], LENS[r][p][1] + 256 * sg)
 
-        def decide(gp, sgs=(0, 1)):
-            step("D%d" % gp[0] if len(sgs) == 2 else "D%d%d" % (gp[0], sgs[0]))
-            c0, c1 = cols(*gp)
-            for sg in sgs:
-                vtt(("cc", 224 * sg + c0, 224 * sg + c1), lens(gp, sg), ("old", OLD[gp[0]], OLD[gp[0]] + c1 - c0), ALU.is_lt)
-            for sg in sgs:
-                fz = ("fq%d" if gp == (3,) else "fz%d") % sg
-                out = T[fz][:, 3:35:4, :] if gp == (3,) else T[fz][:, 1 + 16 * gp[0]:17 + 16 * gp[-1]:2, :]
-                vtt((fz, c0, c1), lens(gp, sg), ("cc", 224 * sg + c0, 224 * sg + c1), ALU.min, out)
+        def lift(p, L, at):
+            step("Z%d" % p)
+            vts(("zz",) + at, L, 0.0, HUGE, ALU.is_equal, ALU.mult)
+            step("M%d" % p)
+            vtt(L, L, ("zz",) + at, ALU.max)
+
+        def decide(gp):
+            (L, at), name = lens(gp), "D%d" % gp[0]
+            fz = ("fq" if gp == (3,) else "fz",) + cols(*gp)
+            out = T.fq[:, :, 3:35:4, :] if gp == (3,) else T.fz[:, :, 1 + 16 * gp[0]:17 + 16 * gp[-1]:2, :]
+            if gp in EARLY and not last:
+                lift(gp[0], L, at)
+                step(name)
+                vtt(fz, L, ("old",) + at, ALU.is_lt, out)
+            else:
+                step("c%d" % gp[0])
+                vtt(("cc",) + at, L, ("old",) + at, ALU.is_lt)
+                step(name)
+                vtt(fz, L, ("cc",) + at, ALU.min, out)
 
         def shorten():
-            for L, z in ((("la", 0, 192), ("zz", 0, 192)), (("lb", 0, 256), ("zz", 192, 448))):
-                step("Z")
-                vts(z, L, 0.0, HUGE, ALU.is_equal, ALU.mult)
-                step("M")
-                vtt(L, L, z, ALU.max)
-            step("m")
-            for p, sg, n in ((3, 0, 96), (1, 0, 128), (3, 1, 96), (1, 1, 128)):
-                (bank, c), o = LENS[r][p, sg], ("old", OLD[p], OLD[p] + n)
-                vtt(o, (bank, c, c + n), o, ALU.min)
+            for p, n in ((1, 128), (0, 96)):
+                if not EARLY:
+                    lift(p, (LENS[r][p][0], 0, n, 2), (OLD[p], OLD[p] + n, 2))
+                elif p == 0:
+                    lift(3, *lens((3,)))
+            for sg in range(2):
+                step("m%d" % sg)
+                for p, n in ((1, 128), (0, 96)):
+                    (bank, c), o = LENS[r][p], ("old", OLD[p], OLD[p] + n)
+                    vtt(o, (bank, c + 256 * sg, c + 256 * sg + n), o, ALU.min)
+            twice()
 
         def begin(gp):
             step("b%d" % gp[0])
-            mms([row(region(0, *cols(*gp)), ("c16b",) + cols(*gp), True), plainly(region(2, *cols(*gp)), ("idn", 0, 128), ("yf",) + cols(*gp), False, False)])
+            c0, c1 = cols(*gp)
+            mms([row(region(0, c0, c1), ("c16b", c0, c1), True), row(region(0, c0, c1), ("one", 0, c1 - c0), False, "lane"),
+                 plainly(region(2, c0, c1), ("idn", 0, 128), ("yf", c0, c1), False, False)])
             if last and turning(gp[0]):
-                mms([row(region(1, *cols(*gp)), ("one", 0, 8 * stride(gp[0])), False)])
+                mms([row(region(1, c0, c1), ("one", 0, c1 - c0), False)])
 
         def flags(p, sg, out, tile, stop):
-            H, fz = 16 // stride(p), ("fq%d" if p == 3 else "fz%d") % sg
+            H, fz = 16 // stride(p), "fq" if p == 3 else "fz"
             calls = []
             for h in range(H):
                 rs = (tile[0], tile[1] + 128 // H * h, tile[1] + 128 // H * h + out[2] - out[1])
-                lap = T[fz][:, 3 - h:35 - h, :] if H == 4 else T[fz][:, 1 - h + 16 * p:17 - h + 16 * p, :]
+                lap = T.fq[:, sg, 3 - h:35 - h, :] if H == 4 else T.fz[:, sg, 1 - h + 16 * p:17 - h + 16 * p, :]
                 calls.append((out, A(out), (fz,) + cols(p), lap, rs, A(rs), False, stop and h == H - 1))
             mms(calls)
 
-        def turn(name, gp, whats, sgs=(0, 1), stop=True):
+        def turn(name, gp, whats, stop=True):
             step(name)
             for what in whats:
                 for p in gp:
-                    for sg in sgs:
-                        flags(p, sg, region(what, *cols(p)), weight(r, p, sg, what), stop and (what, p, sg) == (whats[-1], gp[-1], sgs[-1]))
+                    for sg in range(2):
+                        flags(p, sg, region(what, *cols(p)), weight(r, p, sg, what), stop and (what, p, sg) == (whats[-1], gp[-1], 1))
 
         def select(gp):
-            lo, hi = reach(r, gp[0])
-            win = ("big", place(r, gp[0], 0) + lo, XA + V) if r == 0 else ("big", X0, place(r, gp[0], 1) + hi)
+            (lo, hi), (c0, c1) = reach(r, gp[0]), cols(*gp)
             step("X%d" % gp[0])
-            vts(("xl",) + cols(*gp), region(0, *cols(*gp)), float(X0 - win[1]), ("col", 0, 1), ALU.add, ALU.add)
+            vcopy(("xp", c0, c1, 2), region(0, c0, 2 * c1 - c0))
             for q, a, b in each("s", lo, hi):
-                pick(q, rg(new, a, b), win, ("xl", a // 16, b // 16))
-                if last and KEPT[0] <= a and b <= KEPT[1]:
-                    dma("s", T.yx[:, a:b], A(rg(new, a, b)), [rg(new, a, b)], [])
+                pick(q, rg(new, a, b), ("big", X0, place(r, gp[0], 1) + hi), ("xp", a // 16, b // 16))
             if gp == (0,) and not last:
                 dma("s", A(("cp", lo, hi)), A(rg(new, lo, hi)), [rg(new, lo, hi)], [("cp", lo, hi)])
             if last and turning(gp[0]):
                 c0, c1 = turning(gp[0])
                 step("S%d" % gp[0])
                 vtt(("turned", c0, c1), region(1, c0, c1), ("turned", c0, c1), ALU.mult)
-                for _, a, b in each("F", 16 * c0, 16 * c1):
-                    name, o, c = now[0], (("pw", "tb")[a // G % 2], 0, G), ("turned", a // 16, b // 16)
-                    step("W%d-%d" % (a // 64, b // 64))
-                    mms([(o, T[o[0]][:, i:G:16], ("fan", 128 * i, 128 * i + 128), T.fan[:, 128 * i:128 * i + 128], c, A(c), i == 0, i == 15) for i in range(16)])
-                    now[0] = name
-                    vtt(rg(new, a, b), rg(new, a, b), o, ALU.mult)
-                    dma("s", T.yx[:, a:b], A(rg(new, a, b)), [rg(new, a, b)], [])
 
-        def places(lo, hi):
-            for _, a, b in each("P", lo, hi):
-                vts(("pl", a // 16, b // 16), region(2, a // 16, b // 16), float(t0 - tw0), None, ALU.add)
+        def signs(p):
+            c0, c1 = turning(p)
+            for _, a, b in each("F", 16 * c0, 16 * c1):
+                name, o, c = now[0], (("tb", "tw")[a // G % 2], 0, b - a), ("turned", a // 16, b // 16)
+                step("W%d-%d" % (a // 64, b // 64))
+                mms([(o, T[o[0]][:, i:b - a:16], ("fan", 128 * i, 128 * i + 128), T.fan[:, 128 * i:128 * i + 128], c, A(c), i == 0, i == 15) for i in range(16)])
+                now[0] = name
+                vtt(rg(new, a, b), rg(new, a, b), o, ALU.mult)
 
         def follow():
             for q, a, b in each("g", 0, V):
-                pick(q, ("tab", t1 + a, t1 + b), ("tab", tw0, tw1), ("pl", a // 16, b // 16), [("row", TA, TB)] * (r == 0))
+                pick(q, ("tab", t1 + a, t1 + b), ("tab", t0, TI + W), ("xp", 256 + a // 16, 256 + b // 16), [("row", TA, TD)] * (r == 0))
 
         def scan(c0, c1):
             step("C%d" % (c0 // 64))
@@ -449,59 +469,64 @@ def rank_program(g, core, T, topo):
             mms([onto(("tb", 0, 1), "z1", i, ("rr", 16 * i + 16, 16 * i + 17), i == 0, i == 15) for i in range(c0 // 16, c1 // 16)])
 
         def settle(gp):
-            form(gp, 0)
-            form(gp, 1)
             begin(gp)
             decide(gp)
             if last and turning(gp[0]):
                 step("T%d" % gp[0])
                 flags(gp[0], 1, region(1, *cols(*gp)), scaled(gp[0] // 3, -2), False)
-            turn("T%d" % gp[0], gp, (0, 2) if last else (1, 0, 2))
-            select(gp)
-
-        if last:
-            for gp in GROUPS[r]:
-                settle(gp)
-                places(*PS[gp[0]])
-            follow()
-            step("yc")
-            for i in range(16):
-                mms([onto(("ob", 0, 224), "zw", i, ("tab", t1 + 224 * i, t1 + 224 * i + 224), i == 0, i == 15)])
-            vcopy(("ycs", 0, 224), ("ob", 0, 224))
-            dma("a", T.yc[:, :], T.ycs[:, :], [("ycs", 0, 224)], [])
-            return
-        settle((0,))
-        scan(0, 64)
-        places(*PS[0])
-        step("oth")
-        mms([row(("pw", 224, 256), ("one", 0, 32), True)])
-        for sg in range(2):
-            flags(0, sg, ("pw", 224, 256), scaled(0, -1), False)
-        for gp in GROUPS[r][1:]:
-            form(gp, 0)
-            form(gp, 1)
-            decide(gp)
-            turn("R%d" % gp[0], gp, (1,), stop=gp == (3,))
-        scan(64, 256)
-        for gp in GROUPS[r][1:]:
-            begin(gp)
             turn("T%d" % gp[0], gp, (0, 2))
             select(gp)
-            places(*reach(r, gp[0]))
+
+        for _, a, b in each("H", *KEPT):
+            pick("a", ("yy", a - KEPT[0], b - KEPT[0]), rg(came, 0, W), ("yl", a // 16, b // 16))
+        if last:
+            for gp in GROUPS[r]:
+                for p in {0: (0,), 1: (1, 2), 2: (), 3: (3,)}[gp[0]]:
+                    form((p,), 0)
+                    form((p,), 1)
+                if gp[0] == 1:
+                    signs(0)
+                settle(gp)
+                if gp[0] > 1:
+                    signs(gp[0])
+            follow()
+            blocks = [(s, i) for _, s, a, b in sorted(spans(r, "u", 0, 1024), key=lambda e: steps("t").index((r, e[1]))) for i in range(a // 64, b // 64)]
+            for n, (name, i) in enumerate(blocks):
+                step(name)
+                mms([onto(("ob", 0, 224), "zw", i, ("tab", t1 + 224 * i, t1 + 224 * i + 224), n == 0, n == 15)])
+            copy(who("yc"), ("ycs", 0, 224), ("ob", 0, 224))
+            step("out")
+            dma("a", T.yc[:, :], T.ycs[:, :], [("ycs", 0, 224)], [])
+            for a, b in ([64 * int(k) for k in s.split("-")] for s in LAST["s"].split()):
+                dma("s", T.yx[:, a:b], A(rg(new, a, b)), [rg(new, a, b)], [])
+            return
+        for gp in GROUPS[r]:
+            form(gp, 0)
+            form(gp, 1)
+            settle(gp)
+            if gp == (0,):
+                step("R0")
+                mms([row(("pw", 0, 64), ("zer", 0, 64), True)])
+            if gp == (3,):
+                step("oth")
+                mms([row(("ob", 224, 256), ("one", 0, 32), True)])
+                for sg in range(2):
+                    flags(0, sg, ("ob", 224, 256), scaled(0, -1), False)
+            turn("R%d" % gp[0], gp, (1,), stop=gp != (0,))
+            if gp != (0,):
+                scan(*((192, 256) if gp == (3,) else (0, 192)))
         follow()
         step("cm1")
         vts(("cm1", 0, G), ("kb", 0, G), 256.0, ("tb", 0, 1), ALU.add, ALU.is_ge)
-        step("t2")
-        wrap(("tw", 0, 16), "z1", ("rr", 1, 257))
-        vcopy(("t2", 0, 16), ("tw", 0, 16))
+        q, o = who("t2"), ("tw", 16, 272)
+        wrap(("tw", 0, 16), "z1", ("rr", 1, 257), True, False)
+        mms([plainly(o, ("tri", 0, 128), ("rr", 1, 257), False, False), plainly(o, ("upp", 0, 128), ("rr", 0, 256), False, True)])
+        copy(q, ("t23", 0, 272), ("tw", 0, 272))
         step("l1")
         wrap(("tb", 32, 64), "z1", ("cm1", 0, G))
         vcopy(("l1", 0, 32), ("tb", 32, 64))
         step("cm2")
-        vgt(("cm2", 0, G), ("t2", 0, 16), ("l1", 0, 32), ("kk", 0, G), ALU.is_le)
-        q, o = who("t3"), ("tw", 256, 512)
-        mms([plainly(o, ("tri", 0, 128), ("rr", 1, 257), True, False), plainly(o, ("upp", 0, 128), ("rr", 0, 256), False, True)])
-        copy(q, ("t3", 0, 256), o)
+        vgt(("cm2", 0, G), ("t23", 0, 16), ("l1", 0, 32), ("kk", 0, G), ALU.is_le)
         step("l2a")
         wrap(("ob", 0, 32), "z16", ("cm1", 0, G), True, False)
         step("l2")
@@ -511,21 +536,22 @@ def rank_program(g, core, T, topo):
         wrap(("tb", 64, 96), "zf", ("cm1", 0, G), True, False)
         wrap(("tb", 64, 96), "z16", ("cm2", 0, G), False, False)
         step("cm3")
-        vgt(("cm3", 0, G), ("t3", 0, 256), ("l2", 0, 32), ("kk", 0, G), ALU.is_le)
+        vgt(("cm3", 0, G), ("t23", 16, 272), ("l2", 0, 32), ("kk", 0, G), ALU.is_le)
         step("l3")
         wrap(("tb", 64, 96), "z1", ("cm3", 0, G), False, True)
         vcopy(("l3", 0, 32), ("tb", 64, 96))
         gs, hs = ("gs%d" % r, 0, G), ("hs%d" % r, 0, G)
-        for h in range(2):
-            pick(who("gs%d" % h), (gs[0], 256 * h, 256 * h + 256), rg(new, 0, V), ("l3", 16 * h, 16 * h + 16))
+        for q, a, b in each("j", 0, G):
+            pick(q, (gs[0], a, b), rg(new, 0, V), ("l3", a // 16, b // 16))
         send(rg(new, V, W), gs, "x%d" % (r + 1))
-        dma("s", A(("cp", KEPT[1], V)), A(rg(new, KEPT[1], V)), [rg(new, KEPT[1], V)], [("cp", KEPT[1], V), gs])
+        weights(r + 1)
         q = who("hs")
         mms([onto(("xa", 0, G), z, i, ("cm%d" % (n + 1), 0, G), n == 0, n == 2) for n, (z, i) in enumerate((("zf", 0), ("z16", 1), ("z1", 1)))])
         copy(q, hs, ("xa", 0, G))
         send(("tab", t1 + V, t1 + W), hs, "h%d" % (r + 1))
+        dma("s", A(("cp", KEPT[1], V)), A(rg(new, KEPT[1], V)), [rg(new, KEPT[1], V)], [("cp", KEPT[1], V), gs])
         q = who("U")
-        mms([row(("xb", 0, 128), ("one", 0, 128), True), row(("xb", 128, 224), ("one", 0, 96), False)])
+        mms([row(("xb", 0, 224), ("one", 0, 224), True)])
         for p in (0, 2, 3):
             flags(p, 1, ("xb",) + cols(p), scaled(p // 3, -2), p == 3)
         if r == 0:
@@ -533,16 +559,19 @@ def rank_program(g, core, T, topo):
         else:
             vtt(("turned", 0, 224), ("xb", 0, 224), ("turned", 0, 224), ALU.mult)
         shorten()
-        for bank, lo, hi in (("pw", 0, V),):
-            for _, a, b in each("Y", lo, hi):
-                wrap((bank, a // 16, b // 16), "zw", ("tab", t1 + a, t1 + b))
-                step("y%d-%d" % (a // 64, b // 64))
-                vcopy(("yl", a // 16, b // 16), (bank, a // 16, b // 16))
-            for q, a, b in each("f", lo, hi):
-                copy(q, ("yf", a // 16, b // 16), (bank, a // 16, b // 16))
+        for _, name, a, b in sorted(spans(r, "Y", 0, V), key=lambda e: steps("t").index((r, e[1]))):
+            step(name)
+            wrap(("pw", a // 16, b // 16), "zw", ("tab", t1 + a, t1 + b))
+            step("y%d-%d" % (a // 64, b // 64))
+            vcopy(("yl", a // 16, b // 16), ("pw", a // 16, b // 16))
+        for q, a, b in each("f", 0, V):
+            copy(q, ("yf", a // 16, b // 16), ("pw", a // 16, b // 16))
 
-    for r in range(3):
-        one_round(r)
+    one_round(0)
+    for i in range(16):
+        where(("fan", 128 * i, 128 * i + 128), ("zer", 0, 128), [[-16, 8], [0, 16]], ALU.not_equal, 1, -i, 1)
+    one_round(1)
+    one_round(2)
 
     cnt = {"v": 0, "a": 0, "t": 0, "g": 0}
     known = {q: {} for q in Q}
@@ -564,6 +593,8 @@ def rank_program(g, core, T, topo):
     def note(q, rd, wr, tok, by):
         clocks[tok] = dict(known[q])
         top[tok[0]] = max(top.get(tok[0], 0), tok[1])
+        for bank in {acc[0] for acc in rd + wr if acc[0] in PSUM}:
+            hist[bank] = [e for e in hist.get(bank, []) if e[3] == by != "t"]
         for acc in wr:
             h = hist.setdefault(acc[0], [])
             if acc[0] not in PSUM:

from concourse.mybir import AluOpType as ALU, ActivationFunctionType as AF

V, G, W = 3584, 512, 4096
PS = [(0, 1024), (1024, 2048), (2048, 3072), (3072, 3584)]
GROUPS = [[(0,), (1, 2), (3,)]] * 2 + [[(0,), (1,), (2,), (3,)]]
LENS = [{0: ("la", 0), 3: ("la", 64), 1: ("lb", 0), 2: ("lb", 64)}] * 2 + [
        {p: (("la", "lb")[p % 2], 64 * (p // 2)) for p in range(4)}]
OLD = [0, 96, 160, 64]
XC, XB, XA, SD = 0, W, 2 * W, 2 * W + V
TC, TB, TA, TI, TD = 0, W, 2 * W, 3 * W, 4 * W
HUGE = float(2 ** 25)
NT = 32
KEPT = (1024, 2560)
EARLY = []

ROUND = {
    "v": "A0-16 y32-56' old' B0-16 A16-24 A24-32 B16-24 B24-32 A32-40 c0 B32-40 D0 A40-48 B40-48 A48-56 B48-56 X0 "
         "c1 D1 s14-16 c3 D3 C0 X1 C3 g0-5 cm1 Z0 t2 l1 cm2 M0 X3 Z1 l2 cm3 U M1 l3 j0-4 g16-34 y0-16 m0 m1 y16-32",
    "a": "H16-24 H24-32 a0-16 H32-40 b0-16 a16-32 f0-56' b16-32 a32-40 b32-40 a40-48 b40-48 a48-56 b48-56 "
         "s0-14 s16-48 s48-56 g5-16 j4-8 U g34-56 hs",
    "t": "x16-24 Y32-56' x24-32 sA0 x32-40 sB0 b0 sA1 b1 R0 T0 oth sB1 sA2 sB2 sA3 sB3 "
         "R1 T1 R3 E0 E3 t2 l1 b3 l2a T3 l2 U l3a l3 hs Y0-16 Y16-32"}
LAST = {
    "v": "A0-16 y32-56' B0-16 A16-24 A40-48 A24-32 B16-24 B24-32 A32-40 c0 B32-40 D0 B40-48 X0 S0 c1 B48-56 D1 A48-56 "
         "g12-16 X1 F0-8 c2 F8-16 D2 g25-32 S2 X2 c3 g22-25 D3 g0-12 S3 X3 F40-48 s48-56 g41-47 F48-56 yc",
    "a": "H16-24 H24-32 a0-16 f0-56' H32-40 b0-16 a16-32 b16-32 a32-48 b32-48 s0-16 a48-56 b48-56 "
         "s16-32 s40-48 g16-22 s32-40 g32-41 g47-56 out",
    "t": "Y32-56' x16-24 x24-32 x32-40 sA0 sB0 b0 sA1 T0 sB1 sA2 W0-8 b1 T1 W8-16 sB2 b2 sA3 sB3 T2 b3 W40-48 T3 W48-56 u0-16",
    "s": "0-8 8-16 16-32 32-40 40-48 48-56"}
PLAN = [dict(ROUND, v=ROUND["v"].replace(" U", ""), t="o0' o1' o2' o3' " + ROUND["t"]),
        dict(ROUND, a=ROUND["a"].replace(" U", "")), LAST]

F32, BF, I32, U16 = "float32", "bfloat16", "int32", "uint16"
SCRATCH = {
    "xin": ("sbuf", [128, W], I32), "big": ("sbuf", [128, SD + 2 * V], F32), "cp": ("sbuf", [128, V], F32),
    "ab0": ("sbuf", [128, V], F32), "ab1": ("sbuf", [128, V], F32), "tab": ("sbuf", [128, TD + V], BF),
    "yy": ("sbuf", [128, 3 * G], F32), "fan": ("sbuf", [128, 16 * 128], BF), "hib": ("sbuf", [128, 256], BF),
    "turned": ("sbuf", [128, 224], BF), "pin": ("sbuf", [128, 2, 112], I32), "pfl": ("sbuf", [128, 7, 32], F32),
    "pti": ("sbuf", [128, 448], I32), "ptd": ("sbuf", [128, 448], BF),
    "yl": ("sbuf", [128, 224], U16), "xp": ("sbuf", [128, 2, 256], U16), "yf": ("sbuf", [128, 224], F32),
    "l1": ("sbuf", [128, 32], U16), "l2": ("sbuf", [128, 32], U16), "l3": ("sbuf", [128, 32], U16),
    "c16b": ("sbuf", [128, 224], BF), "lane": ("sbuf", [128, 128], BF), "ycs": ("sbuf", [128, 224], F32),
    "old": ("sbuf", [128, 2, 256], F32), "cc": ("sbuf", [128, 2, 256], F32), "zz": ("sbuf", [128, 2, 256], F32),
    "fz": ("sbuf", [128, 2, 50, 8], BF), "fq": ("sbuf", [128, 2, 36, 4], BF),
    "rr": ("sbuf", [128, 264], BF), "t23": ("sbuf", [128, 272], F32),
    "cm1": ("sbuf", [128, G], BF), "cm2": ("sbuf", [128, G], BF), "cm3": ("sbuf", [128, G], BF),
    "gs0": ("sbuf", [128, G], F32), "gs1": ("sbuf", [128, G], F32), "hs0": ("sbuf", [128, G], BF), "hs1": ("sbuf", [128, G], BF),
    "kk": ("sbuf", [128, G], F32), "kb": ("sbuf", [128, G], BF), "pc": ("sbuf", [128, 8], I32), "col": ("sbuf", [128, 8], F32),
    "blk": ("sbuf", [128, 128], BF), "tri": ("sbuf", [128, 128], BF), "upp": ("sbuf", [128, 128], BF), "idn": ("sbuf", [128, 128], F32),
    "z0": ("sbuf", [128, 144], BF), "z1": ("sbuf", [128, 144], BF), "z16": ("sbuf", [128, 144], BF), "zf": ("sbuf", [128, 144], BF),
    "zw": ("sbuf", [128, 144], BF), "gind": ("sbuf", [128, 8], F32), "one": ("sbuf", [128, 256], BF), "zer": ("sbuf", [128, 128], BF),
    "ssc": ("sbuf", [128, NT * 128], BF),
    "la": ("psum", [128, 2, 256], F32), "lb": ("psum", [128, 2, 256], F32),
    "xa": ("psum", [128, 512], F32), "xb": ("psum", [128, 512], F32), "pw": ("psum", [128, 512], F32),
    "tb": ("psum", [128, 512], F32), "tw": ("psum", [128, 512], F32), "ob": ("psum", [128, 512], F32),
}
PSUM = [k for k, v in SCRATCH.items() if v[0] == "psum"]
HALVES = [k for k, v in SCRATCH.items() if v[1][1:] == [2, 256]]
WRITES = ["x0", "x1", "x2", "h1", "h2"]
SEMAPHORES = ["cv", "ca", "ct", "cg"] + ["in" + w for w in WRITES] + ["out" + w for w in WRITES] + ["dm%d" % k for k in range(40)]


def steps(q):
    return [(r - s.endswith("'"), s.rstrip("'")) for r in range(3) for s in PLAN[r][q].split()]


def spans(r, letter, lo, hi):
    found = []
    for q in "vat":
        for r0, s in steps(q):
            if r0 == r and s[0] == letter and "-" in s:
                a, b = (64 * int(k) for k in s[1:].split("-"))
                if lo <= a and b <= hi:
                    found.append((q, s, a, b))
    found.sort(key=lambda e: e[2])
    assert [lo] + [e[3] for e in found] == [e[2] for e in found] + [hi], (r, letter, lo, hi, found)
    return found


def clash(acc, isw, seen):
    return (seen[2] or isw) and seen[0] < acc[2] and acc[1] < seen[1]


def arrange(jobs):
    seen, pre = {}, []
    for n, j in enumerate(jobs):
        both = [(r, False) for r in j["rd"]] + [(w, True) for w in j["wr"]]
        pre.append({e[3] for acc, isw in both for e in seen.get(acc[0], [])
                    if clash(acc, isw, e) or (acc[0] in PSUM and (jobs[e[3]]["q"] != j["q"] or (j["q"] == "t" and acc[0] not in ("la", "lb"))))})
        for acc in j["wr"]:
            seen[acc[0]] = [e for e in seen.get(acc[0], []) if acc[0] in PSUM or not (acc[1] <= e[0] and e[1] <= acc[2])]
        for acc, isw in both:
            seen.setdefault(acc[0], []).append((acc[1], acc[2], isw, n))
    lines = []
    for q in "vatgs":
        at = {s: k for k, s in enumerate(steps(q))} if q in "vat" else {}
        lines.append(sorted((n for n, j in enumerate(jobs) if j["q"] == q), key=lambda n: (at[jobs[n]["step"]] if at and jobs[n]["step"] else -1, n)))
    done, out = set(), []
    while len(out) < len(jobs):
        ready = [line for line in lines if line and pre[line[0]] <= done]
        assert ready, [(jobs[line[0]]["step"], [jobs[m]["step"] for m in pre[line[0]] - done]) for line in lines if line]
        out.append(min(ready).pop(0))
        done.add(out[-1])
    return out


def rank_program(g, core, T, topo):
    rank = T.rank_of(core)
    if rank is None:
        return
    nxt = T.cores[(rank + 1) % len(T.cores)]
    rid, pid, _ = topo.addr(nxt)
    mask = topo.mask(core, nxt)
    neng = len(topo.engines(core, nxt))
    Q = {"v": g.vector, "a": g.scalar, "t": g.tensor, "g": g, "s": g.sync}

    jobs, now = [], [None]

    def job(q, calls, rd, wr, kind="op"):
        jobs.append({"q": q, "calls": calls, "rd": rd, "wr": wr, "kind": kind, "step": now[0]})

    def op(q, call, rd, wr):
        job(q, [call], rd, wr)

    def dma(q, out, in_, rd, wr, **kw):
        job(q, [lambda: Q[q].dma_start(out, in_, **kw)], rd, wr, "dma")

    def send(dst, src, name):
        job("g", name, [src], [dst], "send")

    def mms(calls):
        job("t", [lambda c=c: g.tensor.matmul(c[1], c[3], c[5], c[6], c[7]) for c in calls],
            sorted({c[2] for c in calls} | {c[4] for c in calls}), sorted({c[0] for c in calls}))

    def A(r, step=1):
        if len(r) == 4:
            return T[r[0]][:, :, r[1]:r[2]]
        if r[0] in HALVES:
            return T[r[0]][:, r[1] // 256, r[1] % 256:r[2] - r[1] // 256 * 256:step]
        return T[r[0]][:, r[1]:r[2]:step]

    def parts(*rs):
        return [(r[0], r[1] + 256 * h, r[2] + 256 * h) for r in rs for h in range(len(r) - 2)]

    def gat(win, off):
        return A(win).indirect(A(off))

    def vcopy(o, i):
        op("v", lambda: g.vector.tensor_copy(A(o), A(i)), parts(i), parts(o))

    def vts(o, i, s1, s2, *ops):
        cols = [s for s in (s1, s2) if isinstance(s, tuple)]
        args = [A(s) if isinstance(s, tuple) else s for s in (s1, s2)]
        op("v", lambda: g.vector.tensor_scalar(A(o), A(i), args[0], args[1], *ops), parts(i) + cols, parts(o))

    def vtt(o, i0, i1, alu, oap=None):
        op("v", lambda: g.vector.tensor_tensor(A(o) if oap is None else oap, A(i0), A(i1), alu), parts(i0, i1), parts(o))

    def vset(o, c, lo=None, hi=None):
        op("v", lambda: g.vector.memset(T[o][:] if lo is None else T[o][:, lo:hi], c), [], [(o, lo or 0, hi or 1 << 20)])

    def act(o, i, fn, **kw):
        cols = [s for s in kw.values() if isinstance(s, tuple)]
        args = {k: A(s) if isinstance(s, tuple) else s for k, s in kw.items()}
        op("a", lambda: g.scalar.activation(A(o), A(i), fn, **args), parts(i) + cols, parts(o))

    def copy(q, o, i):
        if q == "v":
            vcopy(o, i)
        else:
            act(o, i, AF.Copy)

    def pick(q, o, win, off, more=()):
        if q == "v":
            op("v", lambda: g.vector.tensor_copy(A(o), gat(win, off)), [win, off, *more], [o])
        else:
            op("a", lambda: g.scalar.activation(A(o), gat(win, off), AF.Copy), [win, off, *more], [o])

    def vgt(o, win, off, i1, alu):
        op("v", lambda: g.vector.tensor_tensor(A(o), gat(win, off), A(i1), alu), [win, off, i1], [o])

    def plainly(o, l, r, st, sp):
        return (o, A(o), l, A(l), r, A(r), st, sp)

    def row(o, r, st, by="one"):
        return (o, A(o), (by, 0, 128), T[by][0:1, 0:128], r, T[r[0]][0:1, r[1]:r[2]], st, False)

    def iota(o, pattern, base, mult):
        op("g", lambda: g.iota(A(o), pattern, base, mult, allow_small_or_imprecise_dtypes=True), [], [o])

    def where(o, i, pattern, cmp, fill, base, mult):
        op("g", lambda: g.affine_select(A(o), A(i), pattern, cmp, float(fill), base, mult), [i], [o])

    def onto(o, z, i, src, st, sp, step=1):
        return (o, A(o), (z, 0, 144), T[z][:, 15 - i:143 - i], src, T[src[0]][:, src[1] + (i if step > 1 else 0):src[2]:step], st, sp)

    def wrap(o, z, src, st=True, sp=True):
        mms([onto(o, z, i, src, st and i == 0, sp and i == 15, 16) for i in range(16)])

    def stride(p):
        return (PS[p][1] - PS[p][0]) // 128

    def sums(ab, p, bank, c):
        (lo, hi), st = PS[p], stride(p)
        mms([((bank, c, c + 8 * st), A((bank, c + m, c + 8 * st), st), (ab, lo, hi), T[ab][:, lo + m:hi:st], ("gind", 0, 8), T.gind[:, :], True, True)
             for m in range(st)])

    def reach(r, p):
        gp = [k for k in GROUPS[r] if p in k][0]
        return PS[gp[0]][0], PS[gp[-1]][1]

    def place(r, p, sg):
        lo, hi = reach(r, p)
        return SD + lo + sg * (hi - lo)

    tiles = {}
    SHAPES = [[[-1, 2], [-2, 64]], [[-1, 4], [-4, 32]]]

    def scaled(kind, a):
        if (kind, a) not in tiles:
            tiles[kind, a] = ("ssc", 128 * len(tiles), 128 * len(tiles) + 128)
            where(tiles[kind, a], ("zer", 0, 128), SHAPES[kind], ALU.not_equal, a, 0, 1)
        return tiles[kind, a]

    def weight(r, p, sg, what):
        return scaled(p // 3, (place(r, p, sg) - (XA, XB, XC)[r], 1, TI - (TA, TB, TC)[r])[what])

    def weights(r):
        for p in range(4):
            for what in range(3):
                for sg in range(2):
                    weight(r, p, sg, what)

    dma("a", T.xin[:, 0:G], T.x[:, 0:G], [], [("xin", 0, G)])
    for k in range(2):
        dma("s", T.pin[:, k, :], T.pt[k:8:2, :], [], [("pin", 112 * k, 112 * k + 112)])
    dma("s", T.xin[:, G:2048], T.x[:, G:2048], [], [("xin", G, 2048)])
    vset("one", 1.0)
    vset("zer", 0.0)
    op("g", lambda: g.iota(T.pc[:, 0:1], [[0, 1]], 0, 256), [], [("pc", 0, 1)])
    where(("z0", 0, 144), ("one", 0, 144), [[-16, 9], [1000, 16]], ALU.is_ge, 0, -15000, 1)
    where(("z1", 0, 144), ("z0", 0, 144), [[16, 9], [0, 16]], ALU.is_ge, 0, 15, -1)
    vset("tab", 0.0, TA, TA + V)
    vts(("pc", 4, 5), ("pc", 0, 1), 0xF00, None, ALU.bitwise_and)
    for k in range(2):
        op("v", lambda k=k: g.vector.tensor_copy(T.pfl[:, :, 16 * k:16 * k + 16], T.pin[:, k, :]), [("pin", 112 * k, 112 * k + 112)], [("pfl", k, k + 1)])
    for e in range(7):
        op("v", lambda e=e: g.vector.transpose(T.yf[:, e:224:7], T.pfl[:, e, :]), [("pfl", 0, 2)], [("yf", e, e + 1)])
    vcopy(("yl", 0, 224), ("yf", 0, 224))
    for k, bits in enumerate((0xF00, 0xFF)):
        op("v", lambda k=k, bits=bits: g.vector.tensor_scalar(T.pti[:, 224 * k:224 * k + 224], T.pin[:, :, :], bits, None, ALU.bitwise_and),
           [("pin", 0, 224)], [("pti", 224 * k, 224 * k + 224)])

    def rows(at, n, k, src, rd, step=16):
        dma("s", T.tab[k:128:step, at:at + n], src, [rd, ("tab", at, at + n)], [("row", at + k, at + k + 1)])
    for lo, hi in PS[2:]:
        dma("s", T.xin[:, lo:hi], T.x[:, lo:hi], [("pfl", 0, 2)], [("xin", lo, hi)])
    send(("xin", V, W), ("xin", 0, G), "x0")

    def arrive(lo, hi, q):
        act(("ab0", lo, hi), ("xin", lo, hi), AF.Abs)
        copy(q, ("big", XA + lo, XA + hi), ("xin", lo, hi))

    arrive(0, G, "a")
    op("a", lambda: g.scalar.activation(T.gind[:, :], T.z1[:, 15:143:16], AF.Copy), [("z1", 0, 144)], [("gind", 0, 8)])
    act(("z16", 0, 144), ("z1", 0, 144), AF.Copy, scale=16.0)
    act(("zf", 0, 144), ("z1", 0, 144), AF.Copy, scale=256.0)
    act(("col", 0, 1), ("pc", 4, 5), AF.Copy)
    act(("hib", 0, 256), ("one", 0, 256), AF.Copy, scale=("col", 0, 1))
    vset("rr", 0.0, 0, 8)
    vset("fz", 0.0)
    vset("fq", 0.0)

    def late(lo, hi):
        where(("big", XA + lo, XA + hi), ("xin", lo, hi), [[0, hi - lo]], ALU.is_ge, 0, 0, 0)
    where(("idn", 0, 128), ("zer", 0, 128), [[-1, 128]], ALU.not_equal, 1, 0, 1)
    iota(("c16b", 0, 224), [[16, 224]], 0, 0)
    iota(("lane", 0, 128), [[0, 8], [1, 16]], 0, 0)
    late(2048, 2560)
    for sg, what in ((0, 0), (1, 0), (0, 2)):
        weight(0, 0, sg, what)
    late(2560, 3072)
    late(3072, V)
    iota(("kb", 0, G), [[1, G]], -256, 0)
    scaled(0, 1)
    scaled(0, -1)
    weights(0)
    where(("blk", 0, 128), ("one", 0, 128), [[-16, 8], [0, 16]], ALU.is_ge, 0, 0, 1)
    iota(("kk", 0, G), [[1, G]], 0, 0)
    where(("blk", 0, 128), ("blk", 0, 128), [[16, 8], [0, 16]], ALU.is_ge, 0, 15, -1)
    where(("zf", 0, 144), ("zf", 0, 144), [[-16, 9], [1000, 16]], ALU.not_equal, 256 - V, -15013, 1)
    where(("tri", 0, 128), ("blk", 0, 128), [[1, 128]], ALU.is_ge, 0, 0, -1)
    where(("upp", 0, 128), ("blk", 0, 128), [[-1, 128]], ALU.is_gt, 0, 0, 1)
    where(("zw", 0, 144), ("z0", 0, 144), [[16, 9], [0, 16]], ALU.is_ge, 0, 1, -1)
    scaled(0, -2)
    scaled(1, -2)
    arrive(G, 2048, "v")
    act(("ptd", 0, 448), ("pti", 0, 448), AF.Copy)
    for p in (2, 3):
        act(("ab0",) + PS[p], ("xin",) + PS[p], AF.Abs)
    for p in range(4):
        now[0] = (-1, "o%d" % p)
        sums("ab0", p, "lb", 256 + OLD[p])
    now[0] = None
    for at, n in ((0, V), (V, G)):
        dma("s", T.tab[:, TI + at:TI + at + n], T.tab[:, TA:TA + n], [("tab", TA, TA + n), ("row", TA, TA + 32), ("xin", V, W)], [("tab", TI + at, TI + at + n)])

    def twice():
        dma("s", A(("old", 256, 480)), A(("old", 0, 224)), [("old", 0, 224)], [("old", 256, 480)])
    now[0] = (-1, "old")
    copy("v" if now[0] in steps("v") else "a", ("old", 0, 224), ("lb", 256, 480))
    twice()
    for k in range(4):
        rows(TA, V, k // 2 + 16 * (k % 2), T.ptd[:, 112 * k:112 * k + 112], ("ptd", 112 * k, 112 * k + 112), 32)
    rows(TI, W, 0, T.hib[:, :], ("hib", 0, 256))
    rows(TI, W, 1, T.kb[:, 256:G], ("kb", 256, G))
    dma("s", T.tab[:, TA + V:TA + W], T.tab[:, TI:TI + G], [("tab", TI, TI + G), ("row", TI, TI + 2)], [("tab", TA + V, TA + W)])

    def one_round(r):
        last = r == 2
        X0 = (XA, XB, XC)[r]
        came, mine = (("xin", 0), ("big", XB), ("big", XC))[r], (("big", XA), ("cp", 0), ("cp", 0))[r]
        new = (("big", XB), ("big", XC), ("ab0", 0))[r]
        t0, t1 = (TA, TB, TC)[r], (TB, TC, TD)[r]

        def step(name):
            now[0] = (r, name)

        def who(name):
            step(name)
            return "v" if (r, name) in steps("v") else "a"

        def each(letter, lo, hi):
            for q, s, a, b in spans(r, letter, lo, hi):
                step(s)
                yield q, a, b

        def rg(buf, a, b):
            return (buf[0], buf[1] + a, buf[1] + b)

        def cols(*gp):
            return PS[gp[0]][0] // 16, PS[gp[-1]][1] // 16

        def turning(p):
            c0, c1 = cols(p)
            c0 = KEPT[1] // 16 if KEPT[0] // 16 <= c0 < KEPT[1] // 16 else c0
            return (c0, c1) if c0 < c1 else None

        def lens(gp):
            (bank, c), n = LENS[r][gp[0]], cols(*gp)[1] - cols(*gp)[0]
            return (bank, c, c + n, 2), (OLD[gp[0]], OLD[gp[0]] + n, 2)

        def region(what, c0, c1):
            if what == 1 and not last:
                return ("ob" if c0 >= 192 else "pw", c0, c1)
            n = [k for k, gp in enumerate(GROUPS[r]) if cols(*gp)[0] <= c0][-1]
            g0, g1 = cols(*GROUPS[r][n])
            at = (0, 2, 1)[what] * (g1 - g0) - g0
            return (("xa", "xb")[n % 2], at + c0, at + c1)

        def form(gp, sg):
            at, (lo, hi) = place(r, gp[0], sg), reach(r, gp[0])
            for q, a, b in each("AB"[sg], lo, hi):
                o, off = ("big", at + a, at + b), ("yl", a // 16, b // 16)
                if KEPT[0] <= a < KEPT[1]:
                    y, x = ("yy", a - KEPT[0], b - KEPT[0]), (("tw", "ob", "xb")[(a - KEPT[0]) // G], 0, G)
                    if not sg:
                        name = now[0]
                        step("x%d-%d" % (a // 64, b // 64))
                        mms([plainly(x, ("idn", 0, 128), ("big", X0 + a, X0 + b), True, True)])
                        now[0] = name
                    vtt(o, x, y, ALU.subtract if sg else ALU.add)
                else:
                    vgt(o, rg(came, 0, W), off, rg(mine, a, b), ALU.subtract if sg else ALU.add)
            for _, a, b in each("ab"[sg], lo, hi):
                act(("ab%d" % sg, a, b), ("big", at + a, at + b), AF.Abs)
            for p in gp:
                step("s%s%d" % ("AB"[sg], p))
                sums("ab%d" % sg, p, LENS[r][p][0], LENS[r][p][1] + 256 * sg)

        def lift(p, L, at):
            step("Z%d" % p)
            vts(("zz",) + at, L, 0.0, HUGE, ALU.is_equal, ALU.mult)
            step("M%d" % p)
            vtt(L, L, ("zz",) + at, ALU.max)

        def decide(gp):
            (L, at), name = lens(gp), "D%d" % gp[0]
            fz = ("fq" if gp == (3,) else "fz",) + cols(*gp)
            out = T.fq[:, :, 3:35:4, :] if gp == (3,) else T.fz[:, :, 1 + 16 * gp[0]:17 + 16 * gp[-1]:2, :]
            if gp in EARLY and not last:
                lift(gp[0], L, at)
                step(name)
                vtt(fz, L, ("old",) + at, ALU.is_lt, out)
            else:
                step("c%d" % gp[0])
                vtt(("cc",) + at, L, ("old",) + at, ALU.is_lt)
                step(name)
                vtt(fz, L, ("cc",) + at, ALU.min, out)

        def shorten():
            for p, n in ((1, 128), (0, 96)):
                if not EARLY:
                    lift(p, (LENS[r][p][0], 0, n, 2), (OLD[p], OLD[p] + n, 2))
                elif p == 0:
                    lift(3, *lens((3,)))
            for sg in range(2):
                step("m%d" % sg)
                for p, n in ((1, 128), (0, 96)):
                    (bank, c), o = LENS[r][p], ("old", OLD[p], OLD[p] + n)
                    vtt(o, (bank, c + 256 * sg, c + 256 * sg + n), o, ALU.min)
            twice()

        def begin(gp):
            step("b%d" % gp[0])
            c0, c1 = cols(*gp)
            mms([row(region(0, c0, c1), ("c16b", c0, c1), True), row(region(0, c0, c1), ("one", 0, c1 - c0), False, "lane"),
                 plainly(region(2, c0, c1), ("idn", 0, 128), ("yf", c0, c1), False, False)])
            if last and turning(gp[0]):
                mms([row(region(1, c0, c1), ("one", 0, c1 - c0), False)])

        def flags(p, sg, out, tile, stop):
            H, fz = 16 // stride(p), "fq" if p == 3 else "fz"
            calls = []
            for h in range(H):
                rs = (tile[0], tile[1] + 128 // H * h, tile[1] + 128 // H * h + out[2] - out[1])
                lap = T.fq[:, sg, 3 - h:35 - h, :] if H == 4 else T.fz[:, sg, 1 - h + 16 * p:17 - h + 16 * p, :]
                calls.append((out, A(out), (fz,) + cols(p), lap, rs, A(rs), False, stop and h == H - 1))
            mms(calls)

        def turn(name, gp, whats, stop=True):
            step(name)
            for what in whats:
                for p in gp:
                    for sg in range(2):
                        flags(p, sg, region(what, *cols(p)), weight(r, p, sg, what), stop and (what, p, sg) == (whats[-1], gp[-1], 1))

        def select(gp):
            (lo, hi), (c0, c1) = reach(r, gp[0]), cols(*gp)
            step("X%d" % gp[0])
            vcopy(("xp", c0, c1, 2), region(0, c0, 2 * c1 - c0))
            for q, a, b in each("s", lo, hi):
                pick(q, rg(new, a, b), ("big", X0, place(r, gp[0], 1) + hi), ("xp", a // 16, b // 16))
            if gp == (0,) and not last:
                dma("s", A(("cp", lo, hi)), A(rg(new, lo, hi)), [rg(new, lo, hi)], [("cp", lo, hi)])
            if last and turning(gp[0]):
                c0, c1 = turning(gp[0])
                step("S%d" % gp[0])
                vtt(("turned", c0, c1), region(1, c0, c1), ("turned", c0, c1), ALU.mult)

        def signs(p):
            c0, c1 = turning(p)
            for _, a, b in each("F", 16 * c0, 16 * c1):
                name, o, c = now[0], (("tb", "tw")[a // G % 2], 0, b - a), ("turned", a // 16, b // 16)
                step("W%d-%d" % (a // 64, b // 64))
                mms([(o, T[o[0]][:, i:b - a:16], ("fan", 128 * i, 128 * i + 128), T.fan[:, 128 * i:128 * i + 128], c, A(c), i == 0, i == 15) for i in range(16)])
                now[0] = name
                vtt(rg(new, a, b), rg(new, a, b), o, ALU.mult)

        def follow():
            for q, a, b in each("g", 0, V):
                pick(q, ("tab", t1 + a, t1 + b), ("tab", t0, TI + W), ("xp", 256 + a // 16, 256 + b // 16), [("row", TA, TD)] * (r == 0))

        def scan(c0, c1):
            step("C%d" % (c0 // 64))
            rd = [region(1, c0, c1), ("one", 0, c1 - c0), ("rr", c0, c0 + 1)]
            op("v", lambda: g.vector.tensor_tensor_scan(A(("rr", c0 + 1, c1 + 1)), A(rd[1]), A(rd[0]), A(rd[2]), ALU.mult, ALU.add), rd, [("rr", c0 + 1, c1 + 1)])
            step("E%d" % (c0 // 64))
            mms([onto(("tb", 0, 1), "z1", i, ("rr", 16 * i + 16, 16 * i + 17), i == 0, i == 15) for i in range(c0 // 16, c1 // 16)])

        def settle(gp):
            begin(gp)
            decide(gp)
            if last and turning(gp[0]):
                step("T%d" % gp[0])
                flags(gp[0], 1, region(1, *cols(*gp)), scaled(gp[0] // 3, -2), False)
            turn("T%d" % gp[0], gp, (0, 2))
            select(gp)

        for _, a, b in each("H", *KEPT):
            pick("a", ("yy", a - KEPT[0], b - KEPT[0]), rg(came, 0, W), ("yl", a // 16, b // 16))
        if last:
            for gp in GROUPS[r]:
                for p in {0: (0,), 1: (1, 2), 2: (), 3: (3,)}[gp[0]]:
                    form((p,), 0)
                    form((p,), 1)
                if gp[0] == 1:
                    signs(0)
                settle(gp)
                if gp[0] > 1:
                    signs(gp[0])
            follow()
            blocks = [(s, i) for _, s, a, b in sorted(spans(r, "u", 0, 1024), key=lambda e: steps("t").index((r, e[1]))) for i in range(a // 64, b // 64)]
            for n, (name, i) in enumerate(blocks):
                step(name)
                mms([onto(("ob", 0, 224), "zw", i, ("tab", t1 + 224 * i, t1 + 224 * i + 224), n == 0, n == 15)])
            copy(who("yc"), ("ycs", 0, 224), ("ob", 0, 224))
            step("out")
            dma("a", T.yc[:, :], T.ycs[:, :], [("ycs", 0, 224)], [])
            for a, b in ([64 * int(k) for k in s.split("-")] for s in LAST["s"].split()):
                dma("s", T.yx[:, a:b], A(rg(new, a, b)), [rg(new, a, b)], [])
            return
        for gp in GROUPS[r]:
            form(gp, 0)
            form(gp, 1)
            settle(gp)
            if gp == (0,):
                step("R0")
                mms([row(("pw", 0, 64), ("zer", 0, 64), True)])
            if gp == (3,):
                step("oth")
                mms([row(("ob", 224, 256), ("one", 0, 32), True)])
                for sg in range(2):
                    flags(0, sg, ("ob", 224, 256), scaled(0, -1), False)
            turn("R%d" % gp[0], gp, (1,), stop=gp != (0,))
            if gp != (0,):
                scan(*((192, 256) if gp == (3,) else (0, 192)))
        follow()
        step("cm1")
        vts(("cm1", 0, G), ("kb", 0, G), 256.0, ("tb", 0, 1), ALU.add, ALU.is_ge)
        q, o = who("t2"), ("tw", 16, 272)
        wrap(("tw", 0, 16), "z1", ("rr", 1, 257), True, False)
        mms([plainly(o, ("tri", 0, 128), ("rr", 1, 257), False, False), plainly(o, ("upp", 0, 128), ("rr", 0, 256), False, True)])
        copy(q, ("t23", 0, 272), ("tw", 0, 272))
        step("l1")
        wrap(("tb", 32, 64), "z1", ("cm1", 0, G))
        vcopy(("l1", 0, 32), ("tb", 32, 64))
        step("cm2")
        vgt(("cm2", 0, G), ("t23", 0, 16), ("l1", 0, 32), ("kk", 0, G), ALU.is_le)
        step("l2a")
        wrap(("ob", 0, 32), "z16", ("cm1", 0, G), True, False)
        step("l2")
        wrap(("ob", 0, 32), "z1", ("cm2", 0, G), False, True)
        vcopy(("l2", 0, 32), ("ob", 0, 32))
        step("l3a")
        wrap(("tb", 64, 96), "zf", ("cm1", 0, G), True, False)
        wrap(("tb", 64, 96), "z16", ("cm2", 0, G), False, False)
        step("cm3")
        vgt(("cm3", 0, G), ("t23", 16, 272), ("l2", 0, 32), ("kk", 0, G), ALU.is_le)
        step("l3")
        wrap(("tb", 64, 96), "z1", ("cm3", 0, G), False, True)
        vcopy(("l3", 0, 32), ("tb", 64, 96))
        gs, hs = ("gs%d" % r, 0, G), ("hs%d" % r, 0, G)
        for q, a, b in each("j", 0, G):
            pick(q, (gs[0], a, b), rg(new, 0, V), ("l3", a // 16, b // 16))
        send(rg(new, V, W), gs, "x%d" % (r + 1))
        weights(r + 1)
        q = who("hs")
        mms([onto(("xa", 0, G), z, i, ("cm%d" % (n + 1), 0, G), n == 0, n == 2) for n, (z, i) in enumerate((("zf", 0), ("z16", 1), ("z1", 1)))])
        copy(q, hs, ("xa", 0, G))
        send(("tab", t1 + V, t1 + W), hs, "h%d" % (r + 1))
        dma("s", A(("cp", KEPT[1], V)), A(rg(new, KEPT[1], V)), [rg(new, KEPT[1], V)], [("cp", KEPT[1], V), gs])
        q = who("U")
        mms([row(("xb", 0, 224), ("one", 0, 224), True)])
        for p in (0, 2, 3):
            flags(p, 1, ("xb",) + cols(p), scaled(p // 3, -2), p == 3)
        if r == 0:
            copy(q, ("turned", 0, 224), ("xb", 0, 224))
        else:
            vtt(("turned", 0, 224), ("xb", 0, 224), ("turned", 0, 224), ALU.mult)
        shorten()
        for _, name, a, b in sorted(spans(r, "Y", 0, V), key=lambda e: steps("t").index((r, e[1]))):
            step(name)
            wrap(("pw", a // 16, b // 16), "zw", ("tab", t1 + a, t1 + b))
            step("y%d-%d" % (a // 64, b // 64))
            vcopy(("yl", a // 16, b // 16), ("pw", a // 16, b // 16))
        for q, a, b in each("f", 0, V):
            copy(q, ("yf", a // 16, b // 16), ("pw", a // 16, b // 16))

    one_round(0)
    for i in range(16):
        where(("fan", 128 * i, 128 * i + 128), ("zer", 0, 128), [[-16, 8], [0, 16]], ALU.not_equal, 1, -i, 1)
    one_round(1)
    one_round(2)

    cnt = {"v": 0, "a": 0, "t": 0, "g": 0}
    known = {q: {} for q in Q}
    clocks, hist, top, ndma = {}, {}, {}, 0

    def order(q, rd, wr):
        need = {}
        for acc, isw in [(r, False) for r in rd] + [(w, True) for w in wr]:
            for (lo, hi, w0, q0, tok) in hist.get(acc[0], []):
                if (q0, q) != ("t", "t") and ((acc[0] in PSUM and q0 != q) or clash(acc, isw, (lo, hi, w0))):
                    need[tok[0]] = max(need.get(tok[0], 0), tok[1])
        for s, val in sorted(need.items(), key=lambda t: -len(clocks.get(t, {}))):
            if known[q].get(s, 0) < val:
                Q[q].wait_ge(T.sem[s], val)
                known[q][s] = val
                for s2, v2 in clocks.get((s, val), {}).items():
                    known[q][s2] = max(known[q].get(s2, 0), v2)

    def note(q, rd, wr, tok, by):
        clocks[tok] = dict(known[q])
        top[tok[0]] = max(top.get(tok[0], 0), tok[1])
        for bank in {acc[0] for acc in rd + wr if acc[0] in PSUM}:
            hist[bank] = [e for e in hist.get(bank, []) if e[3] == by != "t"]
        for acc in wr:
            h = hist.setdefault(acc[0], [])
            if acc[0] not in PSUM:
                h[:] = [e for e in h if not (acc[1] <= e[0] and e[1] <= acc[2])]
            h.append((acc[1], acc[2], True, by, tok))
        for acc in rd:
            hist.setdefault(acc[0], []).append((acc[1], acc[2], False, by, tok))

    for n in arrange(jobs):
        j = jobs[n]
        q, rd, wr = j["q"], j["rd"], j["wr"]
        if j["kind"] == "send":
            name = j["calls"]
            order(q, rd, [])
            g.remote_dma(A(wr[0]), A(rd[0]), T.sem["in" + name], T.sem["out" + name], pid, rid, mask)
            note(q, rd, [], ("out" + name, neng), "dma")
            note(q, [], wr, ("in" + name, neng), "dma")
            clocks[("in" + name, neng)] = {}
            continue
        order(q, rd, wr)
        if j["kind"] == "dma":
            j["calls"][0]().then_inc(T.sem["dm%d" % ndma], 16)
            note(q, rd, wr, ("dm%d" % ndma, 16), "dma")
            ndma += 1
        else:
            for call in j["calls"]:
                call().then_inc(T.sem["c" + q], 1)
                cnt[q] += 1
            note(q, rd, wr, ("c" + q, cnt[q]), q)

    for s, val in top.items():
        g.sync.wait_ge(T.sem[s], val)
